import numpy as np
import ml_dtypes


def mxq(x, axis, fmt="e4m3"):
    dtype, down = {"e4m3": (ml_dtypes.float8_e4m3fn, 7), "e5m2": (ml_dtypes.float8_e5m2, 14)}[fmt]
    v = np.moveaxis(np.asarray(x, np.float32).astype(ml_dtypes.bfloat16).astype(np.float64), axis, -1)
    blocks = v.reshape(v.shape[:-1] + (-1, 32))
    amax = np.abs(blocks).max(-1, keepdims=True)
    byte = np.maximum(np.where(amax > 0, np.frexp(amax)[1] - 1 + 127, 0) - down, 1)
    scale = np.exp2(byte - 127.0)
    codes = (blocks / scale).astype(np.float32).astype(dtype).astype(np.float64)
    return np.moveaxis((codes * scale).reshape(v.shape), -1, axis)


WIDE = False


def mx_kscale(k):
    if not WIDE:
        return np.ones(k)
    levels = np.array([10, -10, 5, -5, 0])
    if k % 512:
        return np.exp2(np.random.permutation(np.resize(levels, k // 32))).repeat(32)
    a = np.empty((k // 512, 16))
    for p in range(k // 512):
        a[p, :8] = np.random.permutation(np.resize(levels, 8))
        for g in range(8):
            far = levels[np.abs(levels - a[p, g]) >= 10]
            a[p, g + 8] = far[np.random.randint(len(far))]
    return np.exp2(a.ravel()).repeat(32)


def f64(x):
    return np.asarray(x).astype(np.float64)


def striped(idx):
    return np.tile(idx.reshape(-1, 16).T, (8, 1)).astype(np.uint16)


def unstriped(offs):
    return offs[:16].T.reshape(-1).astype(np.int64)


E2M1 = np.array([0.0, 0.5, 1.0, 1.5, 2.0, 3.0, 4.0, 6.0, -0.0, -0.5, -1.0, -1.5, -2.0, -3.0, -4.0, -6.0])


def pack_weight(w, fmt):
    k, n = w.shape
    w = f64(np.asarray(w, np.float32).astype(ml_dtypes.bfloat16)).reshape(k // 32, 32, n)
    amax = np.abs(w).max(1)
    if fmt == "e4m3":
        byte = np.frexp(amax)[1] - 1 + 127 - 7
    else:
        mant, ex = np.frexp(amax / 6.0)
        byte = np.where(mant > 0.5, ex, ex - 1) + 127
    byte = np.clip(np.where(amax > 0, byte, 1), 1, 254)
    scaled = (w * np.exp2(127.0 - byte)[:, None, :]).reshape(k, n).astype(np.float32)
    by_word = np.ascontiguousarray(scaled.reshape(k // 512, 128, 4, n).transpose(0, 1, 3, 2))
    if fmt == "e4m3":
        words = by_word.astype(ml_dtypes.float8_e4m3fn).view(np.uint8)
    else:
        c = by_word.astype(ml_dtypes.float4_e2m1fn).view(np.uint8) & 0xF
        words = (c[..., 0::2] | (c[..., 1::2] << 4)).reshape(k // 512, 128, 2 * n)
    return np.ascontiguousarray(words), np.ascontiguousarray(byte.astype(np.uint8).reshape(k // 512, 16, n))


def unpack_weight(words, scales, fmt):
    g, _, n = scales.shape
    words = np.ascontiguousarray(words).reshape(g, 128, n, -1)
    if fmt == "e4m3":
        vals = words.view(ml_dtypes.float8_e4m3fn).astype(np.float64)
    else:
        nib = np.empty((g, 128, n, 4), np.uint8)
        nib[..., 0::2] = words & 0xF
        nib[..., 1::2] = words >> 4
        vals = E2M1[nib]
    vals = vals * np.repeat(np.exp2(scales.astype(np.float64) - 127.0), 8, axis=1)[..., None]
    return vals.transpose(0, 1, 3, 2).reshape(g * 512, n)


def gelu(v):
    return 0.5 * v * (1.0 + np.tanh(np.sqrt(2.0 / np.pi) * (v + 0.044715 * v**3)))


K, H, N, T, S = 1024, 1024, 512, 2048, 1024

def setup_inputs():
    n = np.random.standard_normal
    s = mx_kscale(K)[:, None]
    u = mx_kscale(H)[:, None]
    tab_words, tab_scales = pack_weight(n((K, T)) * s, "e4m3")
    wl_words, wl_scales = pack_weight(n((K, N)) / np.sqrt(K) / s, "e2m1")
    return {
        "tab_words": tab_words, "tab_scales": tab_scales,
        "offs": striped(np.random.permutation(T)[:S]),
        "wf": (n((K, H)) / np.sqrt(K) / s).astype(np.float32),
        "wl_words": wl_words, "wl_scales": wl_scales,
        "gain": (np.exp(0.3 * n(H)) * u[:, 0]).astype(np.float32),
        "wm": (0.7 * n((H, N)) / np.sqrt(H) / u).astype(np.float32),
        "b0": (0.5 * n(N)).astype(np.float32),
    }

def reference(tab_words, tab_scales, offs, wf, wl_words, wl_scales, gain, wm, b0):
    v = unpack_weight(tab_words, tab_scales, "e4m3")[:, unstriped(offs)]
    wl = unpack_weight(wl_words, wl_scales, "e2m1")
    h = mxq(f64(wf), 0, "e4m3").T @ v
    lin = wl.T @ v
    z = np.square(h) * f64(gain)[:, None]
    y = mxq(f64(wm), 0, "e4m3").T @ mxq(z, 0, "e4m3")
    return np.square(lin) - y + f64(b0)[:, None]

@@ -1,0 +1,254 @@
+from contextlib import ExitStack
+
+import concourse.mybir as mybir
+
+K, H, N, T, S = 1024, 1024, 512, 2048, 1024
+FLOPS = 2 * S * (K * H + K * N + H * N)
+
+F32 = mybir.dt.float32
+BF16 = mybir.dt.bfloat16
+I32 = mybir.dt.int32
+U32 = mybir.dt.uint32
+U16 = mybir.dt.uint16
+U8 = mybir.dt.uint8
+FP8X4 = mybir.dt.float8_e4m3fn_x4
+FP4X4 = mybir.dt.float4_e2m1fn_x4
+ALU = mybir.AluOpType
+ACT = mybir.ActivationFunctionType
+
+P = 128
+PACK = 4
+PASS = P * PACK
+COLS = 512
+HALVES = S // COLS
+K_PASSES = K // PASS
+H_PASSES = H // PASS
+N_TILES = N // P
+LIST_COLS = COLS // 16
+
+
+def tile_list_factored_quadratic_scores_kernel(
+    tc, tab_words, tab_scales, offs, wf, wl_words, wl_scales, gain, wm, b0, out
+):
+    nc = tc.nc
+    with ExitStack() as ctx:
+        keep = ctx.enter_context(tc.tile_pool(name="keep", bufs=1))
+        psum = ctx.enter_context(tc.psum_pool(name="psum", bufs=8))
+
+        def held(name, shape, dtype):
+            return keep.tile(shape, dtype, name=name, align_bytes=64)
+
+        offsets = keep.tile([P, S // 16], U16, name="offsets")
+        nc.sync.dma_start(offsets[:], offs)
+
+        tab_sc = keep.tile([P, T // 4], I32, name="tab_sc", tag="stage0", align_bytes=64)
+        nc.vector.memset(tab_sc[:], 0)
+        wl_sc = held("wl_sc", [P, K_PASSES, N // 4], I32)
+        nc.gpsimd.memset(wl_sc[:], 0)
+        v_sc_low = held("v_sc_low", [P, S // 4], I32)
+        nc.gpsimd.memset(v_sc_low[:], 0)
+
+        gain_sb = held("gain_sb", [P, H_PASSES, PACK], F32)
+        nc.sync.dma_start(gain_sb[:], gain.rearrange("(b p t) -> p b t", p=P, t=PACK))
+        tab_scales_i = tab_scales.bitcast(I32)
+        for q in range(4):
+            nc.sync.dma_start(tab_sc[32 * q : 32 * q + 8, :], tab_scales_i[:, 4 * q : 4 * q + 4, :])
+        tab_w = []
+        for a in range(K_PASSES):
+            words = keep.tile([P, T], I32, name="tab_w%d" % a, tag="stage%d" % (a + 1), align_bytes=64)
+            nc.sync.dma_start(words[:], tab_words[a].rearrange("p t i -> p (t i)").bitcast(I32))
+            tab_w.append(words)
+        wl_w = held("wl_w", [P, K_PASSES, N // 2], I32)
+        nc.sync.dma_start(wl_w[:], wl_words.bitcast(I32).rearrange("a p c -> p a c"))
+        wl_scales_i = wl_scales.bitcast(I32)
+        for q in range(4):
+            nc.sync.dma_start(
+                wl_sc[32 * q : 32 * q + 4, :, :],
+                wl_scales_i[:, 4 * q : 4 * q + 4, :].rearrange("a r c -> r a c"),
+            )
+
+        sign = held("sign", [P, H_PASSES, PACK], F32)
+        magnitude = held("magnitude", [P, H_PASSES, PACK], F32)
+        one_half = held("one_half", [P, H_PASSES, PACK], F32)
+        root = held("root", [P, H_PASSES, PACK], F32)
+        nc.gpsimd.memset(one_half[:], 0.5)
+        nc.scalar.activation(magnitude[:], gain_sb[:], ACT.Abs)
+        nc.scalar.activation(sign[:], gain_sb[:], ACT.Sign)
+        nc.gpsimd.tensor_tensor(root[:], magnitude[:], one_half[:], ALU.pow)
+
+        v_sc = held("v_sc", [P, S], U8)
+        nc.vector.tensor_copy(v_sc[:], tab_sc[:].bitcast(U8).indirect(offsets[:]))
+        nc.sync.dma_start(v_sc_low[0 : P - 4, :], v_sc[4:P, :].bitcast(I32))
+        v_w = {}
+        for a in range(K_PASSES):
+            for jh in range(HALVES):
+                picked = held("v_w%d%d" % (a, jh), [P, COLS], U32)
+                nc.vector.tensor_copy(
+                    picked[:], tab_w[a][:].bitcast(U32).indirect(offsets[:, jh * LIST_COLS : (jh + 1) * LIST_COLS])
+                )
+                v_w[(a, jh)] = picked
+
+        UNIT = PACK * PASS
+        staged = [keep.tile([P, 2 * UNIT + 8], F32, name="staged%d" % i, tag="stage%d" % i, align_bytes=64) for i in range(3)]
+        wf_raw = {}
+        wm_raw = {}
+
+        def load_wf(b, a, parts, room):
+            width = PASS // parts
+            for part in range(parts):
+                raw = room[:, part * PACK * width : (part + 1) * PACK * width].rearrange("p (j c) -> p j c", j=PACK)
+                c0 = b * PASS + part * width
+                nc.sync.dma_start(
+                    raw,
+                    wf[a * PASS : (a + 1) * PASS, c0 : c0 + width].rearrange("(p j) c -> p j c", j=PACK),
+                )
+                wf_raw[(b, a, part)] = raw
+
+        def load_wm(b, room):
+            raw = room.rearrange("p (j c) -> p j c", j=PACK)
+            nc.sync.dma_start(raw, wm[b * PASS : (b + 1) * PASS, :].rearrange("(p j) c -> p j c", j=PACK))
+            wm_raw[b] = raw
+
+        first_room = held("first_room", [P, UNIT], F32)
+        load_wf(0, 0, 1, first_room[:])
+        load_wf(0, 1, 2, staged[0][:, 0:UNIT])
+        load_wm(0, staged[0][:, UNIT : 2 * UNIT])
+        load_wf(1, 0, 1, staged[1][:, 0:UNIT])
+        load_wf(1, 1, 2, staged[1][:, UNIT : 2 * UNIT])
+        load_wm(1, staged[2][:, UNIT : 2 * UNIT])
+        bias = staged[2][:, 2 * UNIT : 2 * UNIT + N_TILES]
+        with nc.allow_non_contiguous_dma(reason="one bias value a partition"):
+            nc.sync.dma_start(bias, b0.rearrange("(u p) -> p u", p=P))
+
+        lin_sq = {}
+        for jh in range(HALVES):
+            cols = slice(jh * COLS, (jh + 1) * COLS)
+            for u in range(N_TILES):
+                acc = psum.tile([P, COLS], F32, name="acc")
+                for a in reversed(range(K_PASSES)):
+                    plane = v_sc[:, cols] if a == 0 else v_sc_low[:].bitcast(U8)[:, cols]
+                    nc.tensor.matmul_mx(
+                        out=acc[:],
+                        lhsT=wl_w[:, a, :].bitcast(U8)[:, 2 * u * P : 2 * (u + 1) * P].bitcast(FP4X4),
+                        lhsT_scale=wl_sc[:, a, :].bitcast(U8)[:, u * P : (u + 1) * P],
+                        rhs=v_w[(a, jh)][:].bitcast(FP8X4),
+                        rhs_scale=plane,
+                        start=(a == K_PASSES - 1),
+                        stop=(a == 0),
+                    )
+                squared = held("lin_sq%d%d" % (jh, u), [P, COLS], F32)
+                nc.scalar.activation(squared[:], acc[:], ACT.Square)
+                lin_sq[(jh, u)] = squared
+
+        quantised = {}
+
+        def quantise(key, grouped):
+            codes = held("codes_" + key, [P, COLS], U32)
+            scales = held("scales_" + key, [P, COLS], U8)
+            nc.vector.quantize_mx(out=codes[:].bitcast(FP8X4), scales=scales[:], in_=grouped[:])
+            quantised[key] = (codes, scales)
+
+        grouped_tiles = {}
+
+        def cast_wf(b, a, parts, on_scalar):
+            grouped = held("wf_grouped%d%d" % (b, a), [P, PASS * PACK], BF16)
+            width = P // parts
+            for part in range(parts):
+                dst = grouped[:].rearrange("p (t m j) -> p m j t", t=PACK, j=PACK)[:, part * width : (part + 1) * width, :, :]
+                src = wf_raw[(b, a, part)].rearrange("p j (m t) -> p m j t", t=PACK)
+                if on_scalar:
+                    nc.scalar.activation(dst, src, ACT.Copy)
+                else:
+                    nc.vector.tensor_copy(dst, src)
+            grouped_tiles["wf%d%d" % (b, a)] = grouped
+
+        def cast_wm(b):
+            grouped = held("wm_grouped%d" % b, [P, N * PACK], BF16)
+            nc.vector.tensor_tensor(
+                grouped[:].rearrange("p (c i j) -> p c j i", i=4, j=PACK),
+                wm_raw[b].rearrange("p j (c i) -> p c j i", i=4),
+                sign[:, b, :].unsqueeze(1).unsqueeze(3).broadcast_to([P, N // 4, PACK, 4]),
+                ALU.mult,
+            )
+            grouped_tiles["wm%d" % b] = grouped
+
+        z_planes = {}
+
+        def square_h(b, jh):
+            cols = slice(jh * COLS, (jh + 1) * COLS)
+            planes = held("z_planes%d%d" % (b, jh), [P, PACK, COLS], BF16)
+            for t in range(PACK):
+                acc = psum.tile([P, COLS], F32, name="acc")
+                for a in range(K_PASSES):
+                    codes, scales = quantised["wf%d%d" % (b, a)]
+                    nc.tensor.matmul_mx(
+                        out=acc[:],
+                        lhsT=codes[:, t * P : (t + 1) * P].bitcast(FP8X4),
+                        lhsT_scale=scales[:, t * P : (t + 1) * P],
+                        rhs=v_w[(a, jh)][:].bitcast(FP8X4),
+                        rhs_scale=v_sc[4 * a : P, cols],
+                        start=(a == 0),
+                        stop=(a == K_PASSES - 1),
+                    )
+                nc.scalar.activation(planes[:, t, :], acc[:], ACT.Square, scale=root[:, b, t : t + 1])
+            z_planes[(b, jh)] = planes
+
+        def interleave_z(b, jh):
+            grouped = held("z_grouped%d%d" % (b, jh), [P, COLS * PACK], BF16)
+            nc.vector.tensor_copy(
+                grouped[:].rearrange("p (c i t) -> p c t i", i=4, t=PACK),
+                z_planes[(b, jh)][:].rearrange("p t (c i) -> p c t i", i=4),
+            )
+            grouped_tiles["z%d%d" % (b, jh)] = grouped
+
+        def finish(jh):
+            cols = slice(jh * COLS, (jh + 1) * COLS)
+            for u in range(N_TILES):
+                acc = psum.tile([P, COLS], F32, name="acc")
+                for b in reversed(range(H_PASSES)):
+                    w_codes, w_scales = quantised["wm%d" % b]
+                    z_codes, z_scales = quantised["z%d%d" % (b, jh)]
+                    nc.tensor.matmul_mx(
+                        out=acc[:],
+                        lhsT=w_codes[:, u * P : (u + 1) * P].bitcast(FP8X4),
+                        lhsT_scale=w_scales[:, u * P : (u + 1) * P],
+                        rhs=z_codes[:].bitcast(FP8X4),
+                        rhs_scale=z_scales[:],
+                        start=(b == H_PASSES - 1),
+                        stop=(b == 0),
+                    )
+                result = held("result%d%d" % (jh, u), [P, COLS], F32)
+                nc.vector.scalar_tensor_tensor(
+                    result[:], lin_sq[(jh, u)][:], bias[:, u : u + 1], acc[:], ALU.add, ALU.subtract
+                )
+                nc.sync.dma_start(out[u * P : (u + 1) * P, cols], result[:])
+
+        def quantise_key(key):
+            quantise(key, grouped_tiles[key])
+
+        cast_wf(0, 0, 1, False)
+        quantise_key("wf00")
+        cast_wf(0, 1, 2, False)
+        quantise_key("wf01")
+        square_h(0, 0)
+        cast_wm(0)
+        cast_wf(1, 0, 1, True)
+        quantise_key("wm0")
+        interleave_z(0, 0)
+        cast_wf(1, 1, 2, False)
+        quantise_key("wf10")
+        quantise_key("wf11")
+        quantise_key("z00")
+        square_h(0, 1)
+        square_h(1, 0)
+        cast_wm(1)
+        interleave_z(0, 1)
+        quantise_key("wm1")
+        interleave_z(1, 0)
+        quantise_key("z01")
+        quantise_key("z10")
+        square_h(1, 1)
+        finish(0)
+        interleave_z(1, 1)
+        quantise_key("z11")
+        finish(1)

@@ -33,15 +33,25 @@ def tile_list_factored_quadratic_scores_kernel(
     nc = tc.nc
     with ExitStack() as ctx:
         keep = ctx.enter_context(tc.tile_pool(name="keep", bufs=1))
-        psum = ctx.enter_context(tc.psum_pool(name="psum", bufs=8))
+        psum = ctx.enter_context(tc.psum_pool(name="psum", bufs=1))
 
         def held(name, shape, dtype):
             return keep.tile(shape, dtype, name=name, align_bytes=64)
 
+        banks_opened = []
+
+        def next_bank():
+            bank = len(banks_opened) % 8
+            banks_opened.append(bank)
+            return psum.tile([P, COLS], F32, name="acc", tag="bank%d" % bank)
+
+        def work_room(name, shape, dtype):
+            return keep.tile(shape, dtype, name=name, tag="work_room", align_bytes=64)
+
         offsets = keep.tile([P, S // 16], U16, name="offsets")
         nc.sync.dma_start(offsets[:], offs)
 
-        tab_sc = keep.tile([P, T // 4], I32, name="tab_sc", tag="stage0", align_bytes=64)
+        tab_sc = held("tab_sc", [P, T // 4], I32)
         nc.vector.memset(tab_sc[:], 0)
         wl_sc = held("wl_sc", [P, K_PASSES, N // 4], I32)
         nc.gpsimd.memset(wl_sc[:], 0)
@@ -53,28 +63,28 @@ def tile_list_factored_quadratic_scores_kernel(
         tab_scales_i = tab_scales.bitcast(I32)
         for q in range(4):
             nc.sync.dma_start(tab_sc[32 * q : 32 * q + 8, :], tab_scales_i[:, 4 * q : 4 * q + 4, :])
-        tab_w = []
+        tab_w = [held("tab_w0", [P, T], I32), work_room("tab_w1", [P, T], I32)]
         for a in range(K_PASSES):
-            words = keep.tile([P, T], I32, name="tab_w%d" % a, tag="stage%d" % (a + 1), align_bytes=64)
-            nc.sync.dma_start(words[:], tab_words[a].rearrange("p t i -> p (t i)").bitcast(I32))
-            tab_w.append(words)
-        wl_w = held("wl_w", [P, K_PASSES, N // 2], I32)
-        nc.sync.dma_start(wl_w[:], wl_words.bitcast(I32).rearrange("a p c -> p a c"))
-        wl_scales_i = wl_scales.bitcast(I32)
-        for q in range(4):
-            nc.sync.dma_start(
-                wl_sc[32 * q : 32 * q + 4, :, :],
-                wl_scales_i[:, 4 * q : 4 * q + 4, :].rearrange("a r c -> r a c"),
-            )
+            nc.sync.dma_start(tab_w[a][:], tab_words[a].rearrange("p t i -> p (t i)").bitcast(I32))
 
         sign = held("sign", [P, H_PASSES, PACK], F32)
         magnitude = held("magnitude", [P, H_PASSES, PACK], F32)
-        one_half = held("one_half", [P, H_PASSES, PACK], F32)
         root = held("root", [P, H_PASSES, PACK], F32)
-        nc.gpsimd.memset(one_half[:], 0.5)
         nc.scalar.activation(magnitude[:], gain_sb[:], ACT.Abs)
+        nc.scalar.activation(root[:], magnitude[:], ACT.Sqrt)
         nc.scalar.activation(sign[:], gain_sb[:], ACT.Sign)
-        nc.gpsimd.tensor_tensor(root[:], magnitude[:], one_half[:], ALU.pow)
+
+        wf_raw = {}
+        for b in range(H_PASSES):
+            for a in range(K_PASSES):
+                for part in range(2):
+                    raw = held("wf_raw%d%d%d" % (b, a, part), [P, PACK, PASS // 2], F32)
+                    c0 = b * PASS + part * PASS // 2
+                    nc.sync.dma_start(
+                        raw[:],
+                        wf[a * PASS : (a + 1) * PASS, c0 : c0 + PASS // 2].rearrange("(p j) c -> p j c", j=PACK),
+                    )
+                    wf_raw[(b, a, part)] = raw[:]
 
         v_sc = held("v_sc", [P, S], U8)
         nc.vector.tensor_copy(v_sc[:], tab_sc[:].bitcast(U8).indirect(offsets[:]))
@@ -88,44 +98,34 @@ def tile_list_factored_quadratic_scores_kernel(
                 )
                 v_w[(a, jh)] = picked
 
-        UNIT = PACK * PASS
-        staged = [keep.tile([P, 2 * UNIT + 8], F32, name="staged%d" % i, tag="stage%d" % i, align_bytes=64) for i in range(3)]
-        wf_raw = {}
         wm_raw = {}
 
-        def load_wf(b, a, parts, room):
-            width = PASS // parts
-            for part in range(parts):
-                raw = room[:, part * PACK * width : (part + 1) * PACK * width].rearrange("p (j c) -> p j c", j=PACK)
-                c0 = b * PASS + part * width
-                nc.sync.dma_start(
-                    raw,
-                    wf[a * PASS : (a + 1) * PASS, c0 : c0 + width].rearrange("(p j) c -> p j c", j=PACK),
-                )
-                wf_raw[(b, a, part)] = raw
+        def load_wm(b):
+            raw = held("wm_raw%d" % b, [P, PACK, N], F32)
+            nc.sync.dma_start(raw[:], wm[b * PASS : (b + 1) * PASS, :].rearrange("(p j) c -> p j c", j=PACK))
+            wm_raw[b] = raw[:]
 
-        def load_wm(b, room):
-            raw = room.rearrange("p (j c) -> p j c", j=PACK)
-            nc.sync.dma_start(raw, wm[b * PASS : (b + 1) * PASS, :].rearrange("(p j) c -> p j c", j=PACK))
-            wm_raw[b] = raw
-
-        first_room = held("first_room", [P, UNIT], F32)
-        load_wf(0, 0, 1, first_room[:])
-        load_wf(0, 1, 2, staged[0][:, 0:UNIT])
-        load_wm(0, staged[0][:, UNIT : 2 * UNIT])
-        load_wf(1, 0, 1, staged[1][:, 0:UNIT])
-        load_wf(1, 1, 2, staged[1][:, UNIT : 2 * UNIT])
-        load_wm(1, staged[2][:, UNIT : 2 * UNIT])
-        bias = staged[2][:, 2 * UNIT : 2 * UNIT + N_TILES]
+        load_wm(0)
+        wl_w = held("wl_w", [P, K_PASSES, N // 2], I32)
+        nc.sync.dma_start(wl_w[:], wl_words.bitcast(I32).rearrange("a p c -> p a c"))
+        wl_scales_i = wl_scales.bitcast(I32)
+        for q in range(4):
+            nc.sync.dma_start(
+                wl_sc[32 * q : 32 * q + 4, :, :],
+                wl_scales_i[:, 4 * q : 4 * q + 4, :].rearrange("a r c -> r a c"),
+            )
+        load_wm(1)
+        bias = held("bias", [P, N_TILES], F32)
         with nc.allow_non_contiguous_dma(reason="one bias value a partition"):
-            nc.sync.dma_start(bias, b0.rearrange("(u p) -> p u", p=P))
+            nc.sync.dma_start(bias[:], b0.rearrange("(u p) -> p u", p=P))
 
         lin_sq = {}
-        for jh in range(HALVES):
+
+        def square_lin(jh):
             cols = slice(jh * COLS, (jh + 1) * COLS)
             for u in range(N_TILES):
-                acc = psum.tile([P, COLS], F32, name="acc")
-                for a in reversed(range(K_PASSES)):
+                acc = next_bank()
+                for a in range(K_PASSES):
                     plane = v_sc[:, cols] if a == 0 else v_sc_low[:].bitcast(U8)[:, cols]
                     nc.tensor.matmul_mx(
                         out=acc[:],
@@ -133,8 +133,8 @@ def tile_list_factored_quadratic_scores_kernel(
                         lhsT_scale=wl_sc[:, a, :].bitcast(U8)[:, u * P : (u + 1) * P],
                         rhs=v_w[(a, jh)][:].bitcast(FP8X4),
                         rhs_scale=plane,
-                        start=(a == K_PASSES - 1),
-                        stop=(a == 0),
+                        start=(a == 0),
+                        stop=(a == K_PASSES - 1),
                     )
                 squared = held("lin_sq%d%d" % (jh, u), [P, COLS], F32)
                 nc.scalar.activation(squared[:], acc[:], ACT.Square)
@@ -151,7 +151,7 @@ def tile_list_factored_quadratic_scores_kernel(
         grouped_tiles = {}
 
         def cast_wf(b, a, parts, on_scalar):
-            grouped = held("wf_grouped%d%d" % (b, a), [P, PASS * PACK], BF16)
+            grouped = (held if on_scalar else work_room)("wf_grouped%d%d" % (b, a), [P, PASS * PACK], BF16)
             width = P // parts
             for part in range(parts):
                 dst = grouped[:].rearrange("p (t m j) -> p m j t", t=PACK, j=PACK)[:, part * width : (part + 1) * width, :, :]
@@ -163,7 +163,7 @@ def tile_list_factored_quadratic_scores_kernel(
             grouped_tiles["wf%d%d" % (b, a)] = grouped
 
         def cast_wm(b):
-            grouped = held("wm_grouped%d" % b, [P, N * PACK], BF16)
+            grouped = work_room("wm_grouped%d" % b, [P, N * PACK], BF16)
             nc.vector.tensor_tensor(
                 grouped[:].rearrange("p (c i j) -> p c j i", i=4, j=PACK),
                 wm_raw[b].rearrange("p j (c i) -> p c j i", i=4),
@@ -178,7 +178,7 @@ def tile_list_factored_quadratic_scores_kernel(
             cols = slice(jh * COLS, (jh + 1) * COLS)
             planes = held("z_planes%d%d" % (b, jh), [P, PACK, COLS], BF16)
             for t in range(PACK):
-                acc = psum.tile([P, COLS], F32, name="acc")
+                acc = next_bank()
                 for a in range(K_PASSES):
                     codes, scales = quantised["wf%d%d" % (b, a)]
                     nc.tensor.matmul_mx(
@@ -193,19 +193,21 @@ def tile_list_factored_quadratic_scores_kernel(
                 nc.scalar.activation(planes[:, t, :], acc[:], ACT.Square, scale=root[:, b, t : t + 1])
             z_planes[(b, jh)] = planes
 
-        def interleave_z(b, jh):
+        def interleave_z(b, jh, on_scalar):
             grouped = held("z_grouped%d%d" % (b, jh), [P, COLS * PACK], BF16)
-            nc.vector.tensor_copy(
-                grouped[:].rearrange("p (c i t) -> p c t i", i=4, t=PACK),
-                z_planes[(b, jh)][:].rearrange("p t (c i) -> p c t i", i=4),
-            )
+            dst = grouped[:].rearrange("p (c i t) -> p c t i", i=4, t=PACK)
+            src = z_planes[(b, jh)][:].rearrange("p t (c i) -> p c t i", i=4)
+            if on_scalar:
+                nc.scalar.activation(dst, src, ACT.Copy)
+            else:
+                nc.vector.tensor_copy(dst, src)
             grouped_tiles["z%d%d" % (b, jh)] = grouped
 
         def finish(jh):
             cols = slice(jh * COLS, (jh + 1) * COLS)
             for u in range(N_TILES):
-                acc = psum.tile([P, COLS], F32, name="acc")
-                for b in reversed(range(H_PASSES)):
+                acc = next_bank()
+                for b in range(H_PASSES):
                     w_codes, w_scales = quantised["wm%d" % b]
                     z_codes, z_scales = quantised["z%d%d" % (b, jh)]
                     nc.tensor.matmul_mx(
@@ -214,8 +216,8 @@ def tile_list_factored_quadratic_scores_kernel(
                         lhsT_scale=w_scales[:, u * P : (u + 1) * P],
                         rhs=z_codes[:].bitcast(FP8X4),
                         rhs_scale=z_scales[:],
-                        start=(b == H_PASSES - 1),
-                        stop=(b == 0),
+                        start=(b == 0),
+                        stop=(b == H_PASSES - 1),
                     )
                 result = held("result%d%d" % (jh, u), [P, COLS], F32)
                 nc.vector.scalar_tensor_tensor(
@@ -226,29 +228,31 @@ def tile_list_factored_quadratic_scores_kernel(
         def quantise_key(key):
             quantise(key, grouped_tiles[key])
 
-        cast_wf(0, 0, 1, False)
-        quantise_key("wf00")
+        cast_wf(0, 0, 2, True)
         cast_wf(0, 1, 2, False)
+        quantise_key("wf00")
         quantise_key("wf01")
         square_h(0, 0)
-        cast_wm(0)
-        cast_wf(1, 0, 1, True)
-        quantise_key("wm0")
-        interleave_z(0, 0)
-        cast_wf(1, 1, 2, False)
+        cast_wf(1, 0, 2, False)
         quantise_key("wf10")
-        quantise_key("wf11")
-        quantise_key("z00")
+        cast_wf(1, 1, 2, False)
         square_h(0, 1)
+        quantise_key("wf11")
+        interleave_z(0, 0, False)
         square_h(1, 0)
-        cast_wm(1)
-        interleave_z(0, 1)
-        quantise_key("wm1")
-        interleave_z(1, 0)
-        quantise_key("z01")
-        quantise_key("z10")
+        cast_wm(0)
+        quantise_key("z00")
+        interleave_z(0, 1, False)
+        quantise_key("wm0")
         square_h(1, 1)
-        finish(0)
-        interleave_z(1, 1)
+        cast_wm(1)
+        quantise_key("z01")
+        interleave_z(1, 0, True)
+        interleave_z(1, 1, False)
+        quantise_key("wm1")
+        square_lin(0)
+        quantise_key("z10")
         quantise_key("z11")
+        square_lin(1)
+        finish(0)
         finish(1)

@@ -1,6 +1,7 @@
 from contextlib import ExitStack
 
 import concourse.mybir as mybir
+from concourse.masks import make_identity
 
 K, H, N, T, S = 1024, 1024, 512, 2048, 1024
 FLOPS = 2 * S * (K * H + K * N + H * N)
@@ -51,15 +52,23 @@ def tile_list_factored_quadratic_scores_kernel(
         offsets = keep.tile([P, S // 16], U16, name="offsets")
         nc.sync.dma_start(offsets[:], offs)
 
+        GAINS = H_PASSES * PACK
+        gain_rows = held("gain_rows", [P, P], F32)
+        nc.gpsimd.memset(gain_rows[:], 0.0)
         tab_sc = held("tab_sc", [P, T // 4], I32)
         nc.vector.memset(tab_sc[:], 0)
+        identity = held("identity", [P, P], F32)
+        make_identity(nc, identity[:])
         wl_sc = held("wl_sc", [P, K_PASSES, N // 4], I32)
         nc.gpsimd.memset(wl_sc[:], 0)
         v_sc_low = held("v_sc_low", [P, S // 4], I32)
         nc.gpsimd.memset(v_sc_low[:], 0)
 
-        gain_sb = held("gain_sb", [P, H_PASSES, PACK], F32)
-        nc.sync.dma_start(gain_sb[:], gain.rearrange("(b p t) -> p b t", p=P, t=PACK))
+        for b in range(H_PASSES):
+            nc.sync.dma_start(
+                gain_rows[PACK * b : PACK * (b + 1), :].rearrange("t (u i) -> t u i", i=4),
+                gain[b * PASS : (b + 1) * PASS].rearrange("(u t i) -> t u i", t=PACK, i=4),
+            )
         tab_scales_i = tab_scales.bitcast(I32)
         for q in range(4):
             nc.sync.dma_start(tab_sc[32 * q : 32 * q + 8, :], tab_scales_i[:, 4 * q : 4 * q + 4, :])
@@ -67,24 +76,31 @@ def tile_list_factored_quadratic_scores_kernel(
         for a in range(K_PASSES):
             nc.sync.dma_start(tab_w[a][:], tab_words[a].rearrange("p t i -> p (t i)").bitcast(I32))
 
-        sign = held("sign", [P, H_PASSES, PACK], F32)
-        magnitude = held("magnitude", [P, H_PASSES, PACK], F32)
-        root = held("root", [P, H_PASSES, PACK], F32)
-        nc.scalar.activation(magnitude[:], gain_sb[:], ACT.Abs)
+        gain_columns = psum.tile([P, COLS], F32, name="gain_columns", tag="bank7")
+        nc.tensor.transpose(gain_columns[:, 0:P], gain_rows[:], identity[:])
+        magnitude = held("magnitude", [P, GAINS], F32)
+        root = held("root", [P, GAINS], F32)
+        sign = held("sign", [P, GAINS], F32)
+        nc.scalar.activation(magnitude[:], gain_columns[:, 0:GAINS], ACT.Abs)
         nc.scalar.activation(root[:], magnitude[:], ACT.Sqrt)
-        nc.scalar.activation(sign[:], gain_sb[:], ACT.Sign)
+        nc.scalar.activation(sign[:], gain_columns[:, 0:GAINS], ACT.Sign)
 
         wf_raw = {}
-        for b in range(H_PASSES):
-            for a in range(K_PASSES):
-                for part in range(2):
-                    raw = held("wf_raw%d%d%d" % (b, a, part), [P, PACK, PASS // 2], F32)
-                    c0 = b * PASS + part * PASS // 2
-                    nc.sync.dma_start(
-                        raw[:],
-                        wf[a * PASS : (a + 1) * PASS, c0 : c0 + PASS // 2].rearrange("(p j) c -> p j c", j=PACK),
-                    )
-                    wf_raw[(b, a, part)] = raw[:]
+
+        def load_wf(b, a):
+            for part in range(2):
+                raw = held("wf_raw%d%d%d" % (b, a, part), [P, PACK, PASS // 2], F32)
+                c0 = b * PASS + part * PASS // 2
+                nc.sync.dma_start(
+                    raw[:],
+                    wf[a * PASS : (a + 1) * PASS, c0 : c0 + PASS // 2].rearrange("(p j) c -> p j c", j=PACK),
+                )
+                wf_raw[(b, a, part)] = raw[:]
+
+        load_wf(0, 0)
+        load_wf(0, 1)
+        load_wf(1, 0)
+        load_wf(1, 1)
 
         v_sc = held("v_sc", [P, S], U8)
         nc.vector.tensor_copy(v_sc[:], tab_sc[:].bitcast(U8).indirect(offsets[:]))
@@ -102,7 +118,9 @@ def tile_list_factored_quadratic_scores_kernel(
 
         def load_wm(b):
             raw = held("wm_raw%d" % b, [P, PACK, N], F32)
-            nc.sync.dma_start(raw[:], wm[b * PASS : (b + 1) * PASS, :].rearrange("(p j) c -> p j c", j=PACK))
+            rows = wm[b * PASS : (b + 1) * PASS, :].rearrange("(u t i) c -> t u i c", t=PACK, i=4)
+            for t in range(PACK):
+                nc.sync.dma_start(raw[:, t, :], rows[t])
             wm_raw[b] = raw[:]
 
         load_wm(0)
@@ -115,6 +133,7 @@ def tile_list_factored_quadratic_scores_kernel(
                 wl_scales_i[:, 4 * q : 4 * q + 4, :].rearrange("a r c -> r a c"),
             )
         load_wm(1)
+
         bias = held("bias", [P, N_TILES], F32)
         with nc.allow_non_contiguous_dma(reason="one bias value a partition"):
             nc.sync.dma_start(bias[:], b0.rearrange("(u p) -> p u", p=P))
@@ -143,7 +162,7 @@ def tile_list_factored_quadratic_scores_kernel(
         quantised = {}
 
         def quantise(key, grouped):
-            codes = held("codes_" + key, [P, COLS], U32)
+            codes = keep.tile([P, COLS], U32, name="codes_" + key, tag="codes_" + key, align_bytes=64)
             scales = held("scales_" + key, [P, COLS], U8)
             nc.vector.quantize_mx(out=codes[:].bitcast(FP8X4), scales=scales[:], in_=grouped[:])
             quantised[key] = (codes, scales)
@@ -152,12 +171,15 @@ def tile_list_factored_quadratic_scores_kernel(
 
         def cast_wf(b, a, parts, on_scalar):
             grouped = (held if on_scalar else work_room)("wf_grouped%d%d" % (b, a), [P, PASS * PACK], BF16)
-            width = P // parts
+            width = P // 4 // parts
             for part in range(parts):
-                dst = grouped[:].rearrange("p (t m j) -> p m j t", t=PACK, j=PACK)[:, part * width : (part + 1) * width, :, :]
-                src = wf_raw[(b, a, part)].rearrange("p j (m t) -> p m j t", t=PACK)
+                dst = grouped[:].rearrange("p (t u i j) -> p t u j i", t=PACK, i=4, j=PACK)[
+                    :, :, part * width : (part + 1) * width, :, :
+                ]
+                src = wf_raw[(b, a, part)].rearrange("p j (u t i) -> p t u j i", t=PACK, i=4)
                 if on_scalar:
-                    nc.scalar.activation(dst, src, ACT.Copy)
+                    for t in range(PACK):
+                        nc.scalar.activation(dst[:, t], src[:, t], ACT.Copy)
                 else:
                     nc.vector.tensor_copy(dst, src)
             grouped_tiles["wf%d%d" % (b, a)] = grouped
@@ -167,7 +189,7 @@ def tile_list_factored_quadratic_scores_kernel(
             nc.vector.tensor_tensor(
                 grouped[:].rearrange("p (c i j) -> p c j i", i=4, j=PACK),
                 wm_raw[b].rearrange("p j (c i) -> p c j i", i=4),
-                sign[:, b, :].unsqueeze(1).unsqueeze(3).broadcast_to([P, N // 4, PACK, 4]),
+                sign[:, PACK * b : PACK * (b + 1)].unsqueeze(1).unsqueeze(3).broadcast_to([P, N // 4, PACK, 4]),
                 ALU.mult,
             )
             grouped_tiles["wm%d" % b] = grouped
@@ -179,7 +201,8 @@ def tile_list_factored_quadratic_scores_kernel(
             planes = held("z_planes%d%d" % (b, jh), [P, PACK, COLS], BF16)
             for t in range(PACK):
                 acc = next_bank()
-                for a in range(K_PASSES):
+                order = (0, 1) if (b, jh) == (0, 0) else (1, 0)
+                for a in order:
                     codes, scales = quantised["wf%d%d" % (b, a)]
                     nc.tensor.matmul_mx(
                         out=acc[:],
@@ -187,14 +210,16 @@ def tile_list_factored_quadratic_scores_kernel(
                         lhsT_scale=scales[:, t * P : (t + 1) * P],
                         rhs=v_w[(a, jh)][:].bitcast(FP8X4),
                         rhs_scale=v_sc[4 * a : P, cols],
-                        start=(a == 0),
-                        stop=(a == K_PASSES - 1),
+                        start=(a == order[0]),
+                        stop=(a == order[1]),
                     )
-                nc.scalar.activation(planes[:, t, :], acc[:], ACT.Square, scale=root[:, b, t : t + 1])
+                nc.scalar.activation(planes[:, t, :], acc[:], ACT.Square, scale=root[:, PACK * b + t : PACK * b + t + 1])
             z_planes[(b, jh)] = planes
 
         def interleave_z(b, jh, on_scalar):
-            grouped = held("z_grouped%d%d" % (b, jh), [P, COLS * PACK], BF16)
+            name = "z_grouped%d%d" % (b, jh)
+            tag = {(0, 0): "work_room", (1, 0): "codes_wf11"}.get((b, jh), name)
+            grouped = keep.tile([P, COLS * PACK], BF16, name=name, tag=tag, align_bytes=64)
             dst = grouped[:].rearrange("p (c i t) -> p c t i", i=4, t=PACK)
             src = z_planes[(b, jh)][:].rearrange("p t (c i) -> p c t i", i=4)
             if on_scalar:
@@ -240,8 +265,8 @@ def tile_list_factored_quadratic_scores_kernel(
         quantise_key("wf11")
         interleave_z(0, 0, False)
         square_h(1, 0)
-        cast_wm(0)
         quantise_key("z00")
+        cast_wm(0)
         interleave_z(0, 1, False)
         quantise_key("wm0")
         square_h(1, 1)

@@ -80,31 +80,31 @@ def tile_list_factored_quadratic_scores_kernel(
         nc.tensor.transpose(gain_columns[:, 0:P], gain_rows[:], identity[:])
         magnitude = held("magnitude", [P, GAINS], F32)
         root = held("root", [P, GAINS], F32)
-        sign = held("sign", [P, GAINS], F32)
+        sign = held("sign", [P, GAINS], BF16)
         nc.scalar.activation(magnitude[:], gain_columns[:, 0:GAINS], ACT.Abs)
         nc.scalar.activation(root[:], magnitude[:], ACT.Sqrt)
         nc.scalar.activation(sign[:], gain_columns[:, 0:GAINS], ACT.Sign)
 
         wf_raw = {}
 
-        def load_wf(b, a):
-            for part in range(2):
-                raw = held("wf_raw%d%d%d" % (b, a, part), [P, PACK, PASS // 2], F32)
-                c0 = b * PASS + part * PASS // 2
+        def load_wf(b, a, parts):
+            width = PASS // parts
+            for part in range(parts):
+                raw = held("wf_raw%d%d%d" % (b, a, part), [P, PACK, width], F32)
+                c0 = b * PASS + part * width
                 nc.sync.dma_start(
                     raw[:],
-                    wf[a * PASS : (a + 1) * PASS, c0 : c0 + PASS // 2].rearrange("(p j) c -> p j c", j=PACK),
+                    wf[a * PASS : (a + 1) * PASS, c0 : c0 + width].rearrange("(p j) c -> p j c", j=PACK),
                 )
                 wf_raw[(b, a, part)] = raw[:]
 
-        load_wf(0, 0)
-        load_wf(0, 1)
-        load_wf(1, 0)
-        load_wf(1, 1)
+        load_wf(0, 0, 1)
+        load_wf(0, 1, 1)
+        load_wf(1, 0, 1)
+        load_wf(1, 1, 2)
 
         v_sc = held("v_sc", [P, S], U8)
         nc.vector.tensor_copy(v_sc[:], tab_sc[:].bitcast(U8).indirect(offsets[:]))
-        nc.sync.dma_start(v_sc_low[0 : P - 4, :], v_sc[4:P, :].bitcast(I32))
         v_w = {}
         for a in range(K_PASSES):
             for jh in range(HALVES):
@@ -124,6 +124,9 @@ def tile_list_factored_quadratic_scores_kernel(
             wm_raw[b] = raw[:]
 
         load_wm(0)
+        load_wm(1)
+        for q in range(4):
+            nc.sync.dma_start(v_sc_low[32 * q : 32 * q + 4, :], v_sc[32 * q + 4 : 32 * q + 8, :].bitcast(I32))
         wl_w = held("wl_w", [P, K_PASSES, N // 2], I32)
         nc.sync.dma_start(wl_w[:], wl_words.bitcast(I32).rearrange("a p c -> p a c"))
         wl_scales_i = wl_scales.bitcast(I32)
@@ -132,7 +135,6 @@ def tile_list_factored_quadratic_scores_kernel(
                 wl_sc[32 * q : 32 * q + 4, :, :],
                 wl_scales_i[:, 4 * q : 4 * q + 4, :].rearrange("a r c -> r a c"),
             )
-        load_wm(1)
 
         bias = held("bias", [P, N_TILES], F32)
         with nc.allow_non_contiguous_dma(reason="one bias value a partition"):
@@ -169,36 +171,35 @@ def tile_list_factored_quadratic_scores_kernel(
 
         grouped_tiles = {}
 
-        def cast_wf(b, a, parts, on_scalar):
-            grouped = (held if on_scalar else work_room)("wf_grouped%d%d" % (b, a), [P, PASS * PACK], BF16)
+        def cast_wf(b, a, parts):
+            grouped = work_room("wf_grouped%d%d" % (b, a), [P, PASS * PACK], BF16)
+            dst = grouped[:].rearrange("p (t u i j) -> p t u j i", t=PACK, i=4, j=PACK)
             width = P // 4 // parts
             for part in range(parts):
-                dst = grouped[:].rearrange("p (t u i j) -> p t u j i", t=PACK, i=4, j=PACK)[
-                    :, :, part * width : (part + 1) * width, :, :
-                ]
                 src = wf_raw[(b, a, part)].rearrange("p j (u t i) -> p t u j i", t=PACK, i=4)
-                if on_scalar:
-                    for t in range(PACK):
-                        nc.scalar.activation(dst[:, t], src[:, t], ACT.Copy)
-                else:
-                    nc.vector.tensor_copy(dst, src)
+                nc.vector.tensor_copy(dst[:, :, part * width : (part + 1) * width, :, :], src)
             grouped_tiles["wf%d%d" % (b, a)] = grouped
 
         def cast_wm(b):
-            grouped = work_room("wm_grouped%d" % b, [P, N * PACK], BF16)
-            nc.vector.tensor_tensor(
+            tag = "z_planes01" if b == 0 else "z_grouped01"
+            grouped = keep.tile([P, N * PACK], BF16, name="wm_grouped%d" % b, tag=tag, align_bytes=64)
+            nc.vector.tensor_copy(
                 grouped[:].rearrange("p (c i j) -> p c j i", i=4, j=PACK),
                 wm_raw[b].rearrange("p j (c i) -> p c j i", i=4),
-                sign[:, PACK * b : PACK * (b + 1)].unsqueeze(1).unsqueeze(3).broadcast_to([P, N // 4, PACK, 4]),
-                ALU.mult,
             )
             grouped_tiles["wm%d" % b] = grouped
+
+        def sign_wm(b):
+            grouped = grouped_tiles["wm%d" % b][:].rearrange("p (c j) -> p c j", j=PACK)
+            signs = sign[:, PACK * b : PACK * (b + 1)].unsqueeze(1).broadcast_to([P, N, PACK])
+            nc.vector.tensor_tensor(grouped, grouped, signs, ALU.mult)
 
         z_planes = {}
 
         def square_h(b, jh):
             cols = slice(jh * COLS, (jh + 1) * COLS)
-            planes = held("z_planes%d%d" % (b, jh), [P, PACK, COLS], BF16)
+            name = "z_planes%d%d" % (b, jh)
+            planes = keep.tile([P, PACK, COLS], BF16, name=name, tag=name, align_bytes=64)
             for t in range(PACK):
                 acc = next_bank()
                 order = (0, 1) if (b, jh) == (0, 0) else (1, 0)
@@ -223,7 +224,11 @@ def tile_list_factored_quadratic_scores_kernel(
             dst = grouped[:].rearrange("p (c i t) -> p c t i", i=4, t=PACK)
             src = z_planes[(b, jh)][:].rearrange("p t (c i) -> p c t i", i=4)
             if on_scalar:
-                nc.scalar.activation(dst, src, ACT.Copy)
+                nc.scalar.activation(
+                    grouped[:].rearrange("p (c t) -> p c t", t=PACK),
+                    z_planes[(b, jh)][:].rearrange("p t c -> p c t"),
+                    ACT.Copy,
+                )
             else:
                 nc.vector.tensor_copy(dst, src)
             grouped_tiles["z%d%d" % (b, jh)] = grouped
@@ -253,31 +258,33 @@ def tile_list_factored_quadratic_scores_kernel(
         def quantise_key(key):
             quantise(key, grouped_tiles[key])
 
-        cast_wf(0, 0, 2, True)
-        cast_wf(0, 1, 2, False)
+        cast_wf(0, 0, 1)
         quantise_key("wf00")
+        cast_wf(0, 1, 1)
         quantise_key("wf01")
         square_h(0, 0)
-        cast_wf(1, 0, 2, False)
+        cast_wf(1, 0, 1)
         quantise_key("wf10")
-        cast_wf(1, 1, 2, False)
+        cast_wf(1, 1, 2)
         square_h(0, 1)
         quantise_key("wf11")
         interleave_z(0, 0, False)
         square_h(1, 0)
         quantise_key("z00")
-        cast_wm(0)
         interleave_z(0, 1, False)
-        quantise_key("wm0")
+        cast_wm(0)
+        quantise_key("z01")
+        sign_wm(0)
         square_h(1, 1)
         cast_wm(1)
-        quantise_key("z01")
+        quantise_key("wm0")
         interleave_z(1, 0, True)
+        sign_wm(1)
         interleave_z(1, 1, False)
         quantise_key("wm1")
-        square_lin(0)
         quantise_key("z10")
         quantise_key("z11")
-        square_lin(1)
-        finish(0)
-        finish(1)
+        for jh in range(HALVES):
+            square_lin(jh)
+        for jh in range(HALVES):
+            finish(jh)

@@ -46,67 +46,79 @@ def tile_list_factored_quadratic_scores_kernel(
             banks_opened.append(bank)
             return psum.tile([P, COLS], F32, name="acc", tag="bank%d" % bank)
 
-        def work_room(name, shape, dtype):
-            return keep.tile(shape, dtype, name=name, tag="work_room", align_bytes=64)
+        def shared(name, tag, shape, dtype):
+            return keep.tile(shape, dtype, name=name, tag=tag, align_bytes=64)
 
         offsets = keep.tile([P, S // 16], U16, name="offsets")
         nc.sync.dma_start(offsets[:], offs)
 
-        GAINS = H_PASSES * PACK
-        gain_rows = held("gain_rows", [P, P], F32)
-        nc.gpsimd.memset(gain_rows[:], 0.0)
-        tab_sc = held("tab_sc", [P, T // 4], I32)
-        nc.vector.memset(tab_sc[:], 0)
-        identity = held("identity", [P, P], F32)
-        make_identity(nc, identity[:])
-        wl_sc = held("wl_sc", [P, K_PASSES, N // 4], I32)
-        nc.gpsimd.memset(wl_sc[:], 0)
-        v_sc_low = held("v_sc_low", [P, S // 4], I32)
-        nc.gpsimd.memset(v_sc_low[:], 0)
-
-        for b in range(H_PASSES):
-            nc.sync.dma_start(
-                gain_rows[PACK * b : PACK * (b + 1), :].rearrange("t (u i) -> t u i", i=4),
-                gain[b * PASS : (b + 1) * PASS].rearrange("(u t i) -> t u i", t=PACK, i=4),
-            )
+        tab_sc = shared("tab_sc", "room2", [P, T // 4], I32)
+        nc.gpsimd.memset(tab_sc[:], 0)
+        gain_rows = held("gain_rows", [H_PASSES, PASS], F32)
+        nc.sync.dma_start(gain_rows[:], gain.rearrange("(b r) -> b r", b=H_PASSES))
+        bias_rows = held("bias_rows", [N_TILES, P], F32)
+        nc.sync.dma_start(bias_rows[:], b0.rearrange("(u p) -> u p", p=P))
         tab_scales_i = tab_scales.bitcast(I32)
         for q in range(4):
             nc.sync.dma_start(tab_sc[32 * q : 32 * q + 8, :], tab_scales_i[:, 4 * q : 4 * q + 4, :])
-        tab_w = [held("tab_w0", [P, T], I32), work_room("tab_w1", [P, T], I32)]
-        for a in range(K_PASSES):
+        tab_w = [shared("tab_w%d" % a, "room%d" % a, [P, T], I32) for a in range(K_PASSES)]
+
+        def load_table_words(a):
             nc.sync.dma_start(tab_w[a][:], tab_words[a].rearrange("p t i -> p (t i)").bitcast(I32))
 
-        gain_columns = psum.tile([P, COLS], F32, name="gain_columns", tag="bank7")
-        nc.tensor.transpose(gain_columns[:, 0:P], gain_rows[:], identity[:])
-        magnitude = held("magnitude", [P, GAINS], F32)
-        root = held("root", [P, GAINS], F32)
-        sign = held("sign", [P, GAINS], BF16)
-        nc.scalar.activation(magnitude[:], gain_columns[:, 0:GAINS], ACT.Abs)
-        nc.scalar.activation(root[:], magnitude[:], ACT.Sqrt)
-        nc.scalar.activation(sign[:], gain_columns[:, 0:GAINS], ACT.Sign)
+        load_table_words(0)
+
+        wl_sc = held("wl_sc", [P, K_PASSES, N // 4], I32)
+        nc.gpsimd.memset(wl_sc[:], 0)
+        vec_rows = held("vec_rows", [P, PACK + 1, P], F32)
+        nc.gpsimd.memset(vec_rows[:], 0.0)
+        v_sc_low = held("v_sc_low", [P, S // 4], I32)
+        nc.gpsimd.memset(v_sc_low[:], 0)
+        identity = held("identity", [P, P], F32)
+        make_identity(nc, identity[:])
+
+        wl_scales_i = wl_scales.bitcast(I32)
+        for q in range(4):
+            nc.sync.dma_start(
+                wl_sc[32 * q : 32 * q + 4, :, :],
+                wl_scales_i[:, 4 * q : 4 * q + 4, :].rearrange("a r c -> r a c"),
+            )
+        load_table_words(1)
+        wl_w = held("wl_w", [P, K_PASSES, N // 2], I32)
+        nc.sync.dma_start(wl_w[:], wl_words.bitcast(I32).rearrange("a p c -> p a c"))
 
         wf_raw = {}
 
-        def load_wf(b, a, parts):
-            width = PASS // parts
-            for part in range(parts):
-                raw = held("wf_raw%d%d%d" % (b, a, part), [P, PACK, width], F32)
-                c0 = b * PASS + part * width
-                nc.sync.dma_start(
-                    raw[:],
-                    wf[a * PASS : (a + 1) * PASS, c0 : c0 + width].rearrange("(p j) c -> p j c", j=PACK),
-                )
-                wf_raw[(b, a, part)] = raw[:]
+        def load_wf(b, a, tag):
+            raw = shared("wf_raw%d%d" % (b, a), tag, [P, PACK, PASS], F32)
+            nc.sync.dma_start(
+                raw[:],
+                wf[a * PASS : (a + 1) * PASS, b * PASS : (b + 1) * PASS].rearrange("(p j) c -> p j c", j=PACK),
+            )
+            wf_raw[(b, a)] = raw[:]
 
-        load_wf(0, 0, 1)
-        load_wf(0, 1, 1)
-        load_wf(1, 0, 1)
-        load_wf(1, 1, 2)
+        nc.scalar.copy(
+            vec_rows[0:H_PASSES, 0:PACK, :].rearrange("b t (u i) -> b t u i", i=4),
+            gain_rows[:].rearrange("b (u t i) -> b t u i", t=PACK, i=4),
+        )
+        nc.scalar.copy(vec_rows[0:N_TILES, PACK, :], bias_rows[:])
+        gain_columns = psum.tile([P, PACK, P], F32, name="gain_columns", tag="bank7")
+        for t in range(PACK):
+            nc.tensor.transpose(gain_columns[:, t, :], vec_rows[:, t, :], identity[:])
+        bias_columns = psum.tile([P, P], F32, name="bias_columns", tag="bank6")
+        nc.tensor.transpose(bias_columns[:], vec_rows[:, PACK, :], identity[:])
+        magnitude = held("magnitude", [P, PACK, H_PASSES], F32)
+        root = held("root", [P, PACK, H_PASSES], F32)
+        sign = held("sign", [P, H_PASSES, PACK], BF16)
+        bias = held("bias", [P, N_TILES], F32)
+        nc.scalar.activation(magnitude[:], gain_columns[:, :, 0:H_PASSES], ACT.Abs)
+        nc.scalar.activation(root[:], magnitude[:], ACT.Sqrt)
+        nc.scalar.activation(sign[:].rearrange("p b t -> p t b"), gain_columns[:, :, 0:H_PASSES], ACT.Sign)
+        nc.scalar.activation(bias[:], bias_columns[:, 0:N_TILES], ACT.Copy)
 
-        v_sc = held("v_sc", [P, S], U8)
-        nc.vector.tensor_copy(v_sc[:], tab_sc[:].bitcast(U8).indirect(offsets[:]))
         v_w = {}
-        for a in range(K_PASSES):
+
+        def gather_words(a):
             for jh in range(HALVES):
                 picked = held("v_w%d%d" % (a, jh), [P, COLS], U32)
                 nc.vector.tensor_copy(
@@ -114,31 +126,24 @@ def tile_list_factored_quadratic_scores_kernel(
                 )
                 v_w[(a, jh)] = picked
 
+        v_sc = held("v_sc", [P, S], U8)
+        nc.vector.tensor_copy(v_sc[:], tab_sc[:].bitcast(U8).indirect(offsets[:]))
+        for q in range(4):
+            nc.sync.dma_start(v_sc_low[32 * q : 32 * q + 4, :], v_sc[32 * q + 4 : 32 * q + 8, :].bitcast(I32))
+        load_wf(0, 0, "room2")
+        gather_words(0)
+        load_wf(0, 1, "room0")
+        gather_words(1)
+        load_wf(1, 0, "room1")
+
         wm_raw = {}
 
-        def load_wm(b):
-            raw = held("wm_raw%d" % b, [P, PACK, N], F32)
+        def load_wm(b, tag):
+            raw = shared("wm_raw%d" % b, tag, [P, PACK, N], F32)
             rows = wm[b * PASS : (b + 1) * PASS, :].rearrange("(u t i) c -> t u i c", t=PACK, i=4)
             for t in range(PACK):
                 nc.sync.dma_start(raw[:, t, :], rows[t])
             wm_raw[b] = raw[:]
-
-        load_wm(0)
-        load_wm(1)
-        for q in range(4):
-            nc.sync.dma_start(v_sc_low[32 * q : 32 * q + 4, :], v_sc[32 * q + 4 : 32 * q + 8, :].bitcast(I32))
-        wl_w = held("wl_w", [P, K_PASSES, N // 2], I32)
-        nc.sync.dma_start(wl_w[:], wl_words.bitcast(I32).rearrange("a p c -> p a c"))
-        wl_scales_i = wl_scales.bitcast(I32)
-        for q in range(4):
-            nc.sync.dma_start(
-                wl_sc[32 * q : 32 * q + 4, :, :],
-                wl_scales_i[:, 4 * q : 4 * q + 4, :].rearrange("a r c -> r a c"),
-            )
-
-        bias = held("bias", [P, N_TILES], F32)
-        with nc.allow_non_contiguous_dma(reason="one bias value a partition"):
-            nc.sync.dma_start(bias[:], b0.rearrange("(u p) -> p u", p=P))
 
         lin_sq = {}
 
@@ -146,7 +151,8 @@ def tile_list_factored_quadratic_scores_kernel(
             cols = slice(jh * COLS, (jh + 1) * COLS)
             for u in range(N_TILES):
                 acc = next_bank()
-                for a in range(K_PASSES):
+                order = (0, 1) if jh == 0 else (1, 0)
+                for a in order:
                     plane = v_sc[:, cols] if a == 0 else v_sc_low[:].bitcast(U8)[:, cols]
                     nc.tensor.matmul_mx(
                         out=acc[:],
@@ -154,35 +160,30 @@ def tile_list_factored_quadratic_scores_kernel(
                         lhsT_scale=wl_sc[:, a, :].bitcast(U8)[:, u * P : (u + 1) * P],
                         rhs=v_w[(a, jh)][:].bitcast(FP8X4),
                         rhs_scale=plane,
-                        start=(a == 0),
-                        stop=(a == K_PASSES - 1),
+                        start=(a == order[0]),
+                        stop=(a == order[1]),
                     )
-                squared = held("lin_sq%d%d" % (jh, u), [P, COLS], F32)
+                squared = shared("lin_sq%d%d" % (jh, u), "lin_sq%d%d" % (jh, u), [P, COLS], F32)
                 nc.scalar.activation(squared[:], acc[:], ACT.Square)
                 lin_sq[(jh, u)] = squared
 
         quantised = {}
-
-        def quantise(key, grouped):
-            codes = keep.tile([P, COLS], U32, name="codes_" + key, tag="codes_" + key, align_bytes=64)
-            scales = held("scales_" + key, [P, COLS], U8)
-            nc.vector.quantize_mx(out=codes[:].bitcast(FP8X4), scales=scales[:], in_=grouped[:])
-            quantised[key] = (codes, scales)
-
         grouped_tiles = {}
 
-        def cast_wf(b, a, parts):
-            grouped = work_room("wf_grouped%d%d" % (b, a), [P, PASS * PACK], BF16)
+        def quantise(key, tag=None):
+            codes = shared("codes_" + key, tag or "codes_" + key, [P, COLS], U32)
+            scales = held("scales_" + key, [P, COLS], U8)
+            nc.vector.quantize_mx(out=codes[:].bitcast(FP8X4), scales=scales[:], in_=grouped_tiles[key][:])
+            quantised[key] = (codes, scales)
+
+        def cast_wf(b, a, tag, copy):
+            grouped = shared("wf_grouped%d%d" % (b, a), tag, [P, PASS * PACK], BF16)
             dst = grouped[:].rearrange("p (t u i j) -> p t u j i", t=PACK, i=4, j=PACK)
-            width = P // 4 // parts
-            for part in range(parts):
-                src = wf_raw[(b, a, part)].rearrange("p j (u t i) -> p t u j i", t=PACK, i=4)
-                nc.vector.tensor_copy(dst[:, :, part * width : (part + 1) * width, :, :], src)
+            copy(dst, wf_raw[(b, a)].rearrange("p j (u t i) -> p t u j i", t=PACK, i=4))
             grouped_tiles["wf%d%d" % (b, a)] = grouped
 
-        def cast_wm(b):
-            tag = "z_planes01" if b == 0 else "z_grouped01"
-            grouped = keep.tile([P, N * PACK], BF16, name="wm_grouped%d" % b, tag=tag, align_bytes=64)
+        def cast_wm(b, tag):
+            grouped = shared("wm_grouped%d" % b, tag, [P, N * PACK], BF16)
             nc.vector.tensor_copy(
                 grouped[:].rearrange("p (c i j) -> p c j i", i=4, j=PACK),
                 wm_raw[b].rearrange("p j (c i) -> p c j i", i=4),
@@ -191,7 +192,7 @@ def tile_list_factored_quadratic_scores_kernel(
 
         def sign_wm(b):
             grouped = grouped_tiles["wm%d" % b][:].rearrange("p (c j) -> p c j", j=PACK)
-            signs = sign[:, PACK * b : PACK * (b + 1)].unsqueeze(1).broadcast_to([P, N, PACK])
+            signs = sign[:, b, :].unsqueeze(1).broadcast_to([P, N, PACK])
             nc.vector.tensor_tensor(grouped, grouped, signs, ALU.mult)
 
         z_planes = {}
@@ -199,11 +200,10 @@ def tile_list_factored_quadratic_scores_kernel(
         def square_h(b, jh):
             cols = slice(jh * COLS, (jh + 1) * COLS)
             name = "z_planes%d%d" % (b, jh)
-            planes = keep.tile([P, PACK, COLS], BF16, name=name, tag=name, align_bytes=64)
+            planes = shared(name, name, [P, PACK, COLS], BF16)
             for t in range(PACK):
                 acc = next_bank()
-                order = (0, 1) if (b, jh) == (0, 0) else (1, 0)
-                for a in order:
+                for a in range(K_PASSES):
                     codes, scales = quantised["wf%d%d" % (b, a)]
                     nc.tensor.matmul_mx(
                         out=acc[:],
@@ -211,31 +211,21 @@ def tile_list_factored_quadratic_scores_kernel(
                         lhsT_scale=scales[:, t * P : (t + 1) * P],
                         rhs=v_w[(a, jh)][:].bitcast(FP8X4),
                         rhs_scale=v_sc[4 * a : P, cols],
-                        start=(a == order[0]),
-                        stop=(a == order[1]),
+                        start=(a == 0),
+                        stop=(a == K_PASSES - 1),
                     )
-                nc.scalar.activation(planes[:, t, :], acc[:], ACT.Square, scale=root[:, PACK * b + t : PACK * b + t + 1])
+                nc.scalar.activation(planes[:, t, :], acc[:], ACT.Square, scale=root[:, t, b : b + 1])
             z_planes[(b, jh)] = planes
 
-        def interleave_z(b, jh, on_scalar):
-            name = "z_grouped%d%d" % (b, jh)
-            tag = {(0, 0): "work_room", (1, 0): "codes_wf11"}.get((b, jh), name)
-            grouped = keep.tile([P, COLS * PACK], BF16, name=name, tag=tag, align_bytes=64)
+        def interleave_z(b, jh, tag, copy):
+            grouped = shared("z_grouped%d%d" % (b, jh), tag, [P, COLS * PACK], BF16)
             dst = grouped[:].rearrange("p (c i t) -> p c t i", i=4, t=PACK)
-            src = z_planes[(b, jh)][:].rearrange("p t (c i) -> p c t i", i=4)
-            if on_scalar:
-                nc.scalar.activation(
-                    grouped[:].rearrange("p (c t) -> p c t", t=PACK),
-                    z_planes[(b, jh)][:].rearrange("p t c -> p c t"),
-                    ACT.Copy,
-                )
-            else:
-                nc.vector.tensor_copy(dst, src)
+            copy(dst, z_planes[(b, jh)][:].rearrange("p t (c i) -> p c t i", i=4))
             grouped_tiles["z%d%d" % (b, jh)] = grouped
 
-        def finish(jh):
+        def finish(jh, tiles):
             cols = slice(jh * COLS, (jh + 1) * COLS)
-            for u in range(N_TILES):
+            for u in tiles:
                 acc = next_bank()
                 for b in range(H_PASSES):
                     w_codes, w_scales = quantised["wm%d" % b]
@@ -255,36 +245,40 @@ def tile_list_factored_quadratic_scores_kernel(
                 )
                 nc.sync.dma_start(out[u * P : (u + 1) * P, cols], result[:])
 
-        def quantise_key(key):
-            quantise(key, grouped_tiles[key])
+        on_vector, on_scalar = nc.vector.tensor_copy, nc.scalar.copy
 
-        cast_wf(0, 0, 1)
-        quantise_key("wf00")
-        cast_wf(0, 1, 1)
-        quantise_key("wf01")
+        square_lin(0)
+        square_lin(1)
+        cast_wf(0, 0, "work", on_vector)
+        load_wf(1, 1, "room2")
+        quantise("wf00")
+        cast_wf(0, 1, "work", on_vector)
+        load_wm(0, "room0")
+        quantise("wf01")
         square_h(0, 0)
-        cast_wf(1, 0, 1)
-        quantise_key("wf10")
-        cast_wf(1, 1, 2)
+        cast_wf(1, 0, "work", on_vector)
+        load_wm(1, "room1")
+        quantise("wf10")
         square_h(0, 1)
-        quantise_key("wf11")
-        interleave_z(0, 0, False)
+        cast_wf(1, 1, "work", on_vector)
+        quantise("wf11")
         square_h(1, 0)
-        quantise_key("z00")
-        interleave_z(0, 1, False)
-        cast_wm(0)
-        quantise_key("z01")
-        sign_wm(0)
         square_h(1, 1)
-        cast_wm(1)
-        quantise_key("wm0")
-        interleave_z(1, 0, True)
+        interleave_z(0, 0, "work", on_vector)
+        cast_wm(0, "z_planes00")
+        quantise("z00")
+        sign_wm(0)
+        cast_wm(1, "work")
+        quantise("wm0")
         sign_wm(1)
-        interleave_z(1, 1, False)
-        quantise_key("wm1")
-        quantise_key("z10")
-        quantise_key("z11")
-        for jh in range(HALVES):
-            square_lin(jh)
-        for jh in range(HALVES):
-            finish(jh)
+        interleave_z(1, 0, "z_planes00", on_vector)
+        quantise("wm1")
+        interleave_z(0, 1, "codes_wf11", on_scalar)
+        interleave_z(1, 1, "z_grouped11", on_scalar)
+        quantise("z10")
+        finish(0, [0])
+        quantise("z01", "lin_sq00")
+        finish(0, [1, 2])
+        quantise("z11", "lin_sq02")
+        finish(0, [3])
+        finish(1, range(N_TILES))

@@ -116,6 +116,15 @@ def tile_list_factored_quadratic_scores_kernel(
         nc.scalar.activation(sign[:].rearrange("p b t -> p t b"), gain_columns[:, :, 0:H_PASSES], ACT.Sign)
         nc.scalar.activation(bias[:], bias_columns[:, 0:N_TILES], ACT.Copy)
 
+        wm_raw = {}
+
+        def load_wm(b, tag):
+            raw = shared("wm_raw%d" % b, tag, [P, PACK, N], F32)
+            rows = wm[b * PASS : (b + 1) * PASS, :].rearrange("(u t i) c -> t u i c", t=PACK, i=4)
+            for t in range(PACK):
+                nc.sync.dma_start(raw[:, t, :], rows[t])
+            wm_raw[b] = raw[:]
+
         v_w = {}
 
         def gather_words(a):
@@ -134,22 +143,13 @@ def tile_list_factored_quadratic_scores_kernel(
         gather_words(0)
         load_wf(0, 1, "room0")
         gather_words(1)
-        load_wf(1, 0, "room1")
-
-        wm_raw = {}
-
-        def load_wm(b, tag):
-            raw = shared("wm_raw%d" % b, tag, [P, PACK, N], F32)
-            rows = wm[b * PASS : (b + 1) * PASS, :].rearrange("(u t i) c -> t u i c", t=PACK, i=4)
-            for t in range(PACK):
-                nc.sync.dma_start(raw[:, t, :], rows[t])
-            wm_raw[b] = raw[:]
+        load_wm(0, "room1")
 
         lin_sq = {}
 
-        def square_lin(jh):
+        def square_lin(jh, tiles, room=None):
             cols = slice(jh * COLS, (jh + 1) * COLS)
-            for u in range(N_TILES):
+            for u in tiles:
                 acc = next_bank()
                 order = (0, 1) if jh == 0 else (1, 0)
                 for a in order:
@@ -163,8 +163,11 @@ def tile_list_factored_quadratic_scores_kernel(
                         start=(a == order[0]),
                         stop=(a == order[1]),
                     )
-                squared = shared("lin_sq%d%d" % (jh, u), "lin_sq%d%d" % (jh, u), [P, COLS], F32)
-                nc.scalar.activation(squared[:], acc[:], ACT.Square)
+                if room is None:
+                    squared = shared("lin_sq%d%d" % (jh, u), "lin_sq%d%d" % (jh, u), [P, COLS], F32)[:]
+                else:
+                    squared = room[:, u - 1, :]
+                nc.scalar.activation(squared, acc[:], ACT.Square)
                 lin_sq[(jh, u)] = squared
 
         quantised = {}
@@ -200,7 +203,7 @@ def tile_list_factored_quadratic_scores_kernel(
         def square_h(b, jh):
             cols = slice(jh * COLS, (jh + 1) * COLS)
             name = "z_planes%d%d" % (b, jh)
-            planes = shared(name, name, [P, PACK, COLS], BF16)
+            planes = shared(name, "z_planes01" if (b, jh) == (1, 0) else name, [P, PACK, COLS], BF16)
             for t in range(PACK):
                 acc = next_bank()
                 for a in range(K_PASSES):
@@ -223,10 +226,16 @@ def tile_list_factored_quadratic_scores_kernel(
             copy(dst, z_planes[(b, jh)][:].rearrange("p t (c i) -> p c t i", i=4))
             grouped_tiles["z%d%d" % (b, jh)] = grouped
 
+        y_banks = []
+
         def finish(jh, tiles):
             cols = slice(jh * COLS, (jh + 1) * COLS)
             for u in tiles:
-                acc = next_bank()
+                if jh == 0:
+                    acc = next_bank()
+                    y_banks.append(banks_opened[-1])
+                else:
+                    acc = psum.tile([P, COLS], F32, name="acc", tag="bank%d" % y_banks.pop(0))
                 for b in range(H_PASSES):
                     w_codes, w_scales = quantised["wm%d" % b]
                     z_codes, z_scales = quantised["z%d%d" % (b, jh)]
@@ -240,45 +249,52 @@ def tile_list_factored_quadratic_scores_kernel(
                         stop=(b == H_PASSES - 1),
                     )
                 result = held("result%d%d" % (jh, u), [P, COLS], F32)
-                nc.vector.scalar_tensor_tensor(
-                    result[:], lin_sq[(jh, u)][:], bias[:, u : u + 1], acc[:], ALU.add, ALU.subtract
-                )
-                nc.sync.dma_start(out[u * P : (u + 1) * P, cols], result[:])
+                if u == N_TILES - 1:
+                    rest = late[:, 2 + jh, :]
+                    nc.scalar.activation(rest, acc[:], ACT.Identity, bias=bias[:, u : u + 1], scale=-1.0)
+                    nc.gpsimd.tensor_tensor(result[:], lin_sq[(jh, u)], rest, ALU.add)
+                else:
+                    nc.vector.scalar_tensor_tensor(
+                        result[:], lin_sq[(jh, u)], bias[:, u : u + 1], acc[:], ALU.add, ALU.subtract
+                    )
+                queue = nc.scalar if u == N_TILES - 1 else nc.sync
+                queue.dma_start(out[u * P : (u + 1) * P, cols], result[:])
 
         on_vector, on_scalar = nc.vector.tensor_copy, nc.scalar.copy
 
-        square_lin(0)
-        square_lin(1)
+        square_lin(0, range(N_TILES))
+        square_lin(1, [3, 0])
         cast_wf(0, 0, "work", on_vector)
-        load_wf(1, 1, "room2")
+        load_wf(1, 0, "room2")
         quantise("wf00")
         cast_wf(0, 1, "work", on_vector)
-        load_wm(0, "room0")
+        load_wf(1, 1, "room0")
         quantise("wf01")
         square_h(0, 0)
-        cast_wf(1, 0, "work", on_vector)
-        load_wm(1, "room1")
-        quantise("wf10")
         square_h(0, 1)
-        cast_wf(1, 1, "work", on_vector)
+        cast_wm(0, "work")
+        sign_wm(0)
+        cast_wf(1, 0, "room1", on_vector)
+        load_wm(1, "room2")
+        quantise("wm0")
+        quantise("wf10")
+        cast_wf(1, 1, "room1", on_vector)
         quantise("wf11")
+        interleave_z(0, 1, "z_grouped01", on_scalar)
         square_h(1, 0)
         square_h(1, 1)
-        interleave_z(0, 0, "work", on_vector)
-        cast_wm(0, "z_planes00")
+        interleave_z(0, 0, "room1", on_vector)
+        cast_wm(1, "z_planes00")
         quantise("z00")
-        sign_wm(0)
-        cast_wm(1, "work")
-        quantise("wm0")
         sign_wm(1)
-        interleave_z(1, 0, "z_planes00", on_vector)
+        interleave_z(1, 0, "room2", on_vector)
         quantise("wm1")
-        interleave_z(0, 1, "codes_wf11", on_scalar)
         interleave_z(1, 1, "z_grouped11", on_scalar)
         quantise("z10")
+        quantise("z01", "z_planes00")
+        late = shared("late", "z_planes11", [P, 4, COLS], F32)
         finish(0, [0])
-        quantise("z01", "lin_sq00")
-        finish(0, [1, 2])
-        quantise("z11", "lin_sq02")
-        finish(0, [3])
-        finish(1, range(N_TILES))
+        quantise("z11", "lin_sq00")
+        finish(0, [3, 1, 2])
+        square_lin(1, [1, 2], late)
+        finish(1, [3, 0, 1, 2])

@@ -166,37 +166,50 @@ def tile_list_factored_quadratic_scores_kernel(
                 if room is None:
                     squared = shared("lin_sq%d%d" % (jh, u), "lin_sq%d%d" % (jh, u), [P, COLS], F32)[:]
                 else:
-                    squared = room[:, u - 1, :]
+                    squared = room[:, u - 2, :]
                 nc.scalar.activation(squared, acc[:], ACT.Square)
                 lin_sq[(jh, u)] = squared
 
         quantised = {}
         grouped_tiles = {}
 
-        def quantise(key, tag=None):
+        def quantise(key, tag=None, parts=1):
             codes = shared("codes_" + key, tag or "codes_" + key, [P, COLS], U32)
             scales = held("scales_" + key, [P, COLS], U8)
-            nc.vector.quantize_mx(out=codes[:].bitcast(FP8X4), scales=scales[:], in_=grouped_tiles[key][:])
+            width = COLS // parts
+            for part in range(parts):
+                words = slice(part * width, (part + 1) * width)
+                nc.vector.quantize_mx(
+                    out=codes[:, words].bitcast(FP8X4),
+                    scales=scales[:, words],
+                    in_=grouped_tiles[key][:, PACK * part * width : PACK * (part + 1) * width],
+                )
             quantised[key] = (codes, scales)
 
         def cast_wf(b, a, tag, copy):
             grouped = shared("wf_grouped%d%d" % (b, a), tag, [P, PASS * PACK], BF16)
             dst = grouped[:].rearrange("p (t u i j) -> p t u j i", t=PACK, i=4, j=PACK)
-            copy(dst, wf_raw[(b, a)].rearrange("p j (u t i) -> p t u j i", t=PACK, i=4))
+            src = wf_raw[(b, a)].rearrange("p j (u t i) -> p t u j i", t=PACK, i=4)
+            for t in (0, 2):
+                copy(dst[:, t : t + 2], src[:, t : t + 2])
             grouped_tiles["wf%d%d" % (b, a)] = grouped
 
-        def cast_wm(b, tag):
+        def cast_wm(b, tag, parts=1):
             grouped = shared("wm_grouped%d" % b, tag, [P, N * PACK], BF16)
-            nc.vector.tensor_copy(
-                grouped[:].rearrange("p (c i j) -> p c j i", i=4, j=PACK),
-                wm_raw[b].rearrange("p j (c i) -> p c j i", i=4),
-            )
+            dst = grouped[:].rearrange("p (c i j) -> p c j i", i=4, j=PACK)
+            src = wm_raw[b].rearrange("p j (c i) -> p c j i", i=4)
+            width = N // 4 // parts
+            for part in range(parts):
+                nc.vector.tensor_copy(dst[:, part * width : (part + 1) * width], src[:, part * width : (part + 1) * width])
             grouped_tiles["wm%d" % b] = grouped
 
-        def sign_wm(b):
+        def sign_wm(b, parts=1):
             grouped = grouped_tiles["wm%d" % b][:].rearrange("p (c j) -> p c j", j=PACK)
-            signs = sign[:, b, :].unsqueeze(1).broadcast_to([P, N, PACK])
-            nc.vector.tensor_tensor(grouped, grouped, signs, ALU.mult)
+            width = N // parts
+            signs = sign[:, b, :].unsqueeze(1).broadcast_to([P, width, PACK])
+            for part in range(parts):
+                columns = grouped[:, part * width : (part + 1) * width, :]
+                nc.vector.tensor_tensor(columns, columns, signs, ALU.mult)
 
         z_planes = {}
 
@@ -226,16 +239,14 @@ def tile_list_factored_quadratic_scores_kernel(
             copy(dst, z_planes[(b, jh)][:].rearrange("p t (c i) -> p c t i", i=4))
             grouped_tiles["z%d%d" % (b, jh)] = grouped
 
-        y_banks = []
+        y_bank = {(0, 0): 2, (0, 1): 3, (0, 2): 4, (0, 3): 5, (1, 0): 0, (1, 1): 1, (1, 2): 2, (1, 3): 3}
+
+        late_stores = []
 
         def finish(jh, tiles):
             cols = slice(jh * COLS, (jh + 1) * COLS)
             for u in tiles:
-                if jh == 0:
-                    acc = next_bank()
-                    y_banks.append(banks_opened[-1])
-                else:
-                    acc = psum.tile([P, COLS], F32, name="acc", tag="bank%d" % y_banks.pop(0))
+                acc = psum.tile([P, COLS], F32, name="acc", tag="bank%d" % y_bank[(jh, u)])
                 for b in range(H_PASSES):
                     w_codes, w_scales = quantised["wm%d" % b]
                     z_codes, z_scales = quantised["z%d%d" % (b, jh)]
@@ -249,52 +260,55 @@ def tile_list_factored_quadratic_scores_kernel(
                         stop=(b == H_PASSES - 1),
                     )
                 result = held("result%d%d" % (jh, u), [P, COLS], F32)
-                if u == N_TILES - 1:
-                    rest = late[:, 2 + jh, :]
+                if jh == 0 and u >= 2:
+                    rest = late[:, u, :]
                     nc.scalar.activation(rest, acc[:], ACT.Identity, bias=bias[:, u : u + 1], scale=-1.0)
                     nc.gpsimd.tensor_tensor(result[:], lin_sq[(jh, u)], rest, ALU.add)
                 else:
                     nc.vector.scalar_tensor_tensor(
                         result[:], lin_sq[(jh, u)], bias[:, u : u + 1], acc[:], ALU.add, ALU.subtract
                     )
-                queue = nc.scalar if u == N_TILES - 1 else nc.sync
-                queue.dma_start(out[u * P : (u + 1) * P, cols], result[:])
+                if jh == 0 and u >= 2:
+                    late_stores.append((out[u * P : (u + 1) * P, cols], result[:]))
+                else:
+                    nc.sync.dma_start(out[u * P : (u + 1) * P, cols], result[:])
 
         on_vector, on_scalar = nc.vector.tensor_copy, nc.scalar.copy
 
         square_lin(0, range(N_TILES))
-        square_lin(1, [3, 0])
+        square_lin(1, [0, 1])
         cast_wf(0, 0, "work", on_vector)
         load_wf(1, 0, "room2")
-        quantise("wf00")
+        quantise("wf00", parts=2)
         cast_wf(0, 1, "work", on_vector)
         load_wf(1, 1, "room0")
-        quantise("wf01")
+        quantise("wf01", parts=2)
         square_h(0, 0)
         square_h(0, 1)
-        cast_wm(0, "work")
-        sign_wm(0)
-        cast_wf(1, 0, "room1", on_vector)
-        load_wm(1, "room2")
-        quantise("wm0")
-        quantise("wf10")
-        cast_wf(1, 1, "room1", on_vector)
-        quantise("wf11")
+        cast_wm(0, "work", parts=2)
+        load_wm(1, "room1")
+        sign_wm(0, parts=2)
+        quantise("wm0", parts=2)
+        cast_wf(1, 0, "other_work", on_vector)
+        quantise("wf10", parts=2)
+        cast_wf(1, 1, "work", on_vector)
+        quantise("wf11", parts=2)
         interleave_z(0, 1, "z_grouped01", on_scalar)
         square_h(1, 0)
         square_h(1, 1)
-        interleave_z(0, 0, "room1", on_vector)
-        cast_wm(1, "z_planes00")
+        interleave_z(0, 0, "room0", on_vector)
+        cast_wm(1, "other_work")
         quantise("z00")
         sign_wm(1)
-        interleave_z(1, 0, "room2", on_vector)
+        interleave_z(1, 0, "room1", on_vector)
         quantise("wm1")
         interleave_z(1, 1, "z_grouped11", on_scalar)
         quantise("z10")
-        quantise("z01", "z_planes00")
+        quantise("z01", "z_planes01")
         late = shared("late", "z_planes11", [P, 4, COLS], F32)
-        finish(0, [0])
-        quantise("z11", "lin_sq00")
-        finish(0, [3, 1, 2])
-        square_lin(1, [1, 2], late)
-        finish(1, [3, 0, 1, 2])
+        finish(0, range(N_TILES))
+        quantise("z11", "lin_sq01")
+        square_lin(1, [2, 3], late)
+        for rows, result in late_stores:
+            nc.scalar.dma_start(rows, result)
+        finish(1, range(N_TILES))

@@ -98,8 +98,8 @@ def tile_list_factored_quadratic_scores_kernel(
             wf_raw[(b, a)] = raw[:]
 
         nc.scalar.copy(
-            vec_rows[0:H_PASSES, 0:PACK, :].rearrange("b t (u i) -> b t u i", i=4),
-            gain_rows[:].rearrange("b (u t i) -> b t u i", t=PACK, i=4),
+            vec_rows[0:H_PASSES, 0:PACK, :].rearrange("b (e f) (u i) -> b e f u i", f=2, i=4),
+            gain_rows[:].rearrange("b (u e i f) -> b e f u i", e=2, i=4, f=2),
         )
         nc.scalar.copy(vec_rows[0:N_TILES, PACK, :], bias_rows[:])
         gain_columns = psum.tile([P, PACK, P], F32, name="gain_columns", tag="bank7")
@@ -120,9 +120,9 @@ def tile_list_factored_quadratic_scores_kernel(
 
         def load_wm(b, tag):
             raw = shared("wm_raw%d" % b, tag, [P, PACK, N], F32)
-            rows = wm[b * PASS : (b + 1) * PASS, :].rearrange("(u t i) c -> t u i c", t=PACK, i=4)
-            for t in range(PACK):
-                nc.sync.dma_start(raw[:, t, :], rows[t])
+            rows = wm[b * PASS : (b + 1) * PASS, :].rearrange("(u e i f) c -> e u i (f c)", e=2, i=4, f=2)
+            for e in range(2):
+                nc.sync.dma_start(raw[:, 2 * e : 2 * e + 2, :].rearrange("p f c -> p (f c)"), rows[e])
             wm_raw[b] = raw[:]
 
         v_w = {}
@@ -188,10 +188,10 @@ def tile_list_factored_quadratic_scores_kernel(
 
         def cast_wf(b, a, tag, copy):
             grouped = shared("wf_grouped%d%d" % (b, a), tag, [P, PASS * PACK], BF16)
-            dst = grouped[:].rearrange("p (t u i j) -> p t u j i", t=PACK, i=4, j=PACK)
-            src = wf_raw[(b, a)].rearrange("p j (u t i) -> p t u j i", t=PACK, i=4)
-            for t in (0, 2):
-                copy(dst[:, t : t + 2], src[:, t : t + 2])
+            dst = grouped[:].rearrange("p (e f u i j) -> p e u j i f", e=2, f=2, i=4, j=PACK)
+            src = wf_raw[(b, a)].rearrange("p j (u e i f) -> p e u j i f", e=2, i=4, f=2)
+            for e in range(2):
+                copy(dst[:, e], src[:, e])
             grouped_tiles["wf%d%d" % (b, a)] = grouped
 
         def cast_wm(b, tag, parts=1):

@@ -56,11 +56,9 @@ def tile_list_factored_quadratic_scores_kernel(
         nc.gpsimd.memset(tab_sc[:], 0)
         gain_rows = held("gain_rows", [H_PASSES, PASS], F32)
         nc.sync.dma_start(gain_rows[:], gain.rearrange("(b r) -> b r", b=H_PASSES))
-        bias_rows = held("bias_rows", [N_TILES, P], F32)
-        nc.sync.dma_start(bias_rows[:], b0.rearrange("(u p) -> u p", p=P))
-        tab_scales_i = tab_scales.bitcast(I32)
-        for q in range(4):
-            nc.sync.dma_start(tab_sc[32 * q : 32 * q + 8, :], tab_scales_i[:, 4 * q : 4 * q + 4, :])
+        scale_rows = tab_scales.bitcast(I32).rearrange("a (q r) c -> r q a c", r=4)
+        for r in range(4):
+            nc.sync.dma_start(tab_sc[r:P:16, :], scale_rows[r])
         tab_w = [shared("tab_w%d" % a, "room%d" % a, [P, T], I32) for a in range(K_PASSES)]
 
         def load_table_words(a):
@@ -70,7 +68,7 @@ def tile_list_factored_quadratic_scores_kernel(
 
         wl_sc = held("wl_sc", [P, K_PASSES, N // 4], I32)
         nc.gpsimd.memset(wl_sc[:], 0)
-        vec_rows = held("vec_rows", [P, PACK + 1, P], F32)
+        vec_rows = held("vec_rows", [P, PACK, P], F32)
         nc.gpsimd.memset(vec_rows[:], 0.0)
         v_sc_low = held("v_sc_low", [P, S // 4], I32)
         nc.gpsimd.memset(v_sc_low[:], 0)
@@ -89,32 +87,29 @@ def tile_list_factored_quadratic_scores_kernel(
 
         wf_raw = {}
 
-        def load_wf(b, a, tag):
-            raw = shared("wf_raw%d%d" % (b, a), tag, [P, PACK, PASS], F32)
+        def load_wf(b, a, raw):
             nc.sync.dma_start(
-                raw[:],
+                raw,
                 wf[a * PASS : (a + 1) * PASS, b * PASS : (b + 1) * PASS].rearrange("(p j) c -> p j c", j=PACK),
             )
-            wf_raw[(b, a)] = raw[:]
+            wf_raw[(b, a)] = raw
+
+        def wf_room(b, a, tag):
+            return shared("wf_raw%d%d" % (b, a), tag, [P, PACK, PASS], F32)[:]
 
         nc.scalar.copy(
-            vec_rows[0:H_PASSES, 0:PACK, :].rearrange("b (e f) (u i) -> b e f u i", f=2, i=4),
+            vec_rows[0:H_PASSES, :, :].rearrange("b (e f) (u i) -> b e f u i", f=2, i=4),
             gain_rows[:].rearrange("b (u e i f) -> b e f u i", e=2, i=4, f=2),
         )
-        nc.scalar.copy(vec_rows[0:N_TILES, PACK, :], bias_rows[:])
         gain_columns = psum.tile([P, PACK, P], F32, name="gain_columns", tag="bank7")
         for t in range(PACK):
             nc.tensor.transpose(gain_columns[:, t, :], vec_rows[:, t, :], identity[:])
-        bias_columns = psum.tile([P, P], F32, name="bias_columns", tag="bank6")
-        nc.tensor.transpose(bias_columns[:], vec_rows[:, PACK, :], identity[:])
         magnitude = held("magnitude", [P, PACK, H_PASSES], F32)
         root = held("root", [P, PACK, H_PASSES], F32)
         sign = held("sign", [P, H_PASSES, PACK], BF16)
-        bias = held("bias", [P, N_TILES], F32)
         nc.scalar.activation(magnitude[:], gain_columns[:, :, 0:H_PASSES], ACT.Abs)
         nc.scalar.activation(root[:], magnitude[:], ACT.Sqrt)
         nc.scalar.activation(sign[:].rearrange("p b t -> p t b"), gain_columns[:, :, 0:H_PASSES], ACT.Sign)
-        nc.scalar.activation(bias[:], bias_columns[:, 0:N_TILES], ACT.Copy)
 
         wm_raw = {}
 
@@ -138,12 +133,17 @@ def tile_list_factored_quadratic_scores_kernel(
         v_sc = held("v_sc", [P, S], U8)
         nc.vector.tensor_copy(v_sc[:], tab_sc[:].bitcast(U8).indirect(offsets[:]))
         for q in range(4):
-            nc.sync.dma_start(v_sc_low[32 * q : 32 * q + 4, :], v_sc[32 * q + 4 : 32 * q + 8, :].bitcast(I32))
-        load_wf(0, 0, "room2")
+            nc.sync.dma_start(v_sc_low[32 * q : 32 * q + 4, :], v_sc[32 * q + 16 : 32 * q + 20, :].bitcast(I32))
+        first_wf = shared("first_wf", "room2", [P, K_PASSES, PACK, PASS], F32)
+        load_wf(0, 0, first_wf[:, 0])
+        load_wf(0, 1, first_wf[:, 1])
         gather_words(0)
-        load_wf(0, 1, "room0")
+        load_wm(0, "room0")
         gather_words(1)
-        load_wm(0, "room1")
+        load_wf(1, 0, wf_room(1, 0, "room1"))
+
+        def v_plane(a, cols):
+            return v_sc[:, cols] if a == 0 else v_sc_low[:].bitcast(U8)[:, cols]
 
         lin_sq = {}
 
@@ -153,13 +153,12 @@ def tile_list_factored_quadratic_scores_kernel(
                 acc = next_bank()
                 order = (0, 1) if jh == 0 else (1, 0)
                 for a in order:
-                    plane = v_sc[:, cols] if a == 0 else v_sc_low[:].bitcast(U8)[:, cols]
                     nc.tensor.matmul_mx(
                         out=acc[:],
                         lhsT=wl_w[:, a, :].bitcast(U8)[:, 2 * u * P : 2 * (u + 1) * P].bitcast(FP4X4),
                         lhsT_scale=wl_sc[:, a, :].bitcast(U8)[:, u * P : (u + 1) * P],
                         rhs=v_w[(a, jh)][:].bitcast(FP8X4),
-                        rhs_scale=plane,
+                        rhs_scale=v_plane(a, cols),
                         start=(a == order[0]),
                         stop=(a == order[1]),
                     )
@@ -226,7 +225,7 @@ def tile_list_factored_quadratic_scores_kernel(
                         lhsT=codes[:, t * P : (t + 1) * P].bitcast(FP8X4),
                         lhsT_scale=scales[:, t * P : (t + 1) * P],
                         rhs=v_w[(a, jh)][:].bitcast(FP8X4),
-                        rhs_scale=v_sc[4 * a : P, cols],
+                        rhs_scale=v_plane(a, cols),
                         start=(a == 0),
                         stop=(a == K_PASSES - 1),
                     )
@@ -278,29 +277,31 @@ def tile_list_factored_quadratic_scores_kernel(
         square_lin(0, range(N_TILES))
         square_lin(1, [0, 1])
         cast_wf(0, 0, "work", on_vector)
-        load_wf(1, 0, "room2")
         quantise("wf00", parts=2)
         cast_wf(0, 1, "work", on_vector)
-        load_wf(1, 1, "room0")
+        load_wf(1, 1, wf_room(1, 1, "room2"))
         quantise("wf01", parts=2)
         square_h(0, 0)
         square_h(0, 1)
         cast_wm(0, "work", parts=2)
-        load_wm(1, "room1")
+        load_wm(1, "room0")
         sign_wm(0, parts=2)
         quantise("wm0", parts=2)
         cast_wf(1, 0, "other_work", on_vector)
+        bias = shared("bias", "room1", [P, N_TILES], F32)
+        with nc.allow_non_contiguous_dma(reason="one bias value a partition"):
+            nc.sync.dma_start(bias[:], b0.rearrange("(u p) -> p u", p=P))
         quantise("wf10", parts=2)
         cast_wf(1, 1, "work", on_vector)
         quantise("wf11", parts=2)
         interleave_z(0, 1, "z_grouped01", on_scalar)
         square_h(1, 0)
         square_h(1, 1)
-        interleave_z(0, 0, "room0", on_vector)
+        interleave_z(0, 0, "room2", on_vector)
         cast_wm(1, "other_work")
         quantise("z00")
         sign_wm(1)
-        interleave_z(1, 0, "room1", on_vector)
+        interleave_z(1, 0, "room0", on_vector)
         quantise("wm1")
         interleave_z(1, 1, "z_grouped11", on_scalar)
         quantise("z10")

@@ -81,9 +81,9 @@ def tile_list_factored_quadratic_scores_kernel(
                 wl_sc[32 * q : 32 * q + 4, :, :],
                 wl_scales_i[:, 4 * q : 4 * q + 4, :].rearrange("a r c -> r a c"),
             )
-        load_table_words(1)
         wl_w = held("wl_w", [P, K_PASSES, N // 2], I32)
         nc.sync.dma_start(wl_w[:], wl_words.bitcast(I32).rearrange("a p c -> p a c"))
+        load_table_words(1)
 
         wf_raw = {}
 
@@ -172,26 +172,30 @@ def tile_list_factored_quadratic_scores_kernel(
         quantised = {}
         grouped_tiles = {}
 
-        def quantise(key, tag=None, parts=1):
-            codes = shared("codes_" + key, tag or "codes_" + key, [P, COLS], U32)
-            scales = held("scales_" + key, [P, COLS], U8)
+        def quantise(key, tag=None, parts=1, only=None):
+            if key not in quantised:
+                codes = shared("codes_" + key, tag or "codes_" + key, [P, COLS], U32)
+                scales = held("scales_" + key, [P, COLS], U8)
+                quantised[key] = (codes, scales)
+            codes, scales = quantised[key]
             width = COLS // parts
-            for part in range(parts):
+            for part in range(parts) if only is None else [only]:
                 words = slice(part * width, (part + 1) * width)
                 nc.vector.quantize_mx(
                     out=codes[:, words].bitcast(FP8X4),
                     scales=scales[:, words],
                     in_=grouped_tiles[key][:, PACK * part * width : PACK * (part + 1) * width],
                 )
-            quantised[key] = (codes, scales)
 
-        def cast_wf(b, a, tag, copy):
-            grouped = shared("wf_grouped%d%d" % (b, a), tag, [P, PASS * PACK], BF16)
+        def cast_wf(b, a, tag, copy, halves=(0, 1)):
+            key = "wf%d%d" % (b, a)
+            if key not in grouped_tiles:
+                grouped_tiles[key] = shared("grouped_" + key, tag, [P, PASS * PACK], BF16)
+            grouped = grouped_tiles[key]
             dst = grouped[:].rearrange("p (e f u i j) -> p e u j i f", e=2, f=2, i=4, j=PACK)
             src = wf_raw[(b, a)].rearrange("p j (u e i f) -> p e u j i f", e=2, i=4, f=2)
-            for e in range(2):
+            for e in halves:
                 copy(dst[:, e], src[:, e])
-            grouped_tiles["wf%d%d" % (b, a)] = grouped
 
         def cast_wm(b, tag, parts=1):
             grouped = shared("wm_grouped%d" % b, tag, [P, N * PACK], BF16)
@@ -218,7 +222,8 @@ def tile_list_factored_quadratic_scores_kernel(
             planes = shared(name, "z_planes01" if (b, jh) == (1, 0) else name, [P, PACK, COLS], BF16)
             for t in range(PACK):
                 acc = next_bank()
-                for a in range(K_PASSES):
+                order = (0, 1) if jh == 0 else (1, 0)
+                for a in order:
                     codes, scales = quantised["wf%d%d" % (b, a)]
                     nc.tensor.matmul_mx(
                         out=acc[:],
@@ -226,21 +231,20 @@ def tile_list_factored_quadratic_scores_kernel(
                         lhsT_scale=scales[:, t * P : (t + 1) * P],
                         rhs=v_w[(a, jh)][:].bitcast(FP8X4),
                         rhs_scale=v_plane(a, cols),
-                        start=(a == 0),
-                        stop=(a == K_PASSES - 1),
+                        start=(a == order[0]),
+                        stop=(a == order[1]),
                     )
                 nc.scalar.activation(planes[:, t, :], acc[:], ACT.Square, scale=root[:, t, b : b + 1])
             z_planes[(b, jh)] = planes
 
-        def interleave_z(b, jh, tag, copy):
-            grouped = shared("z_grouped%d%d" % (b, jh), tag, [P, COLS * PACK], BF16)
-            dst = grouped[:].rearrange("p (c i t) -> p c t i", i=4, t=PACK)
-            copy(dst, z_planes[(b, jh)][:].rearrange("p t (c i) -> p c t i", i=4))
-            grouped_tiles["z%d%d" % (b, jh)] = grouped
+        def interleave_z(b, jh, tag, copy, first=0, last=COLS):
+            key = "z%d%d" % (b, jh)
+            if key not in grouped_tiles:
+                grouped_tiles[key] = shared("grouped_" + key, tag, [P, COLS * PACK], BF16)
+            dst = grouped_tiles[key][:, PACK * first : PACK * last].rearrange("p (c i t) -> p c t i", i=4, t=PACK)
+            copy(dst, z_planes[(b, jh)][:, :, first:last].rearrange("p t (c i) -> p c t i", i=4))
 
         y_bank = {(0, 0): 2, (0, 1): 3, (0, 2): 4, (0, 3): 5, (1, 0): 0, (1, 1): 1, (1, 2): 2, (1, 3): 3}
-
-        late_stores = []
 
         def finish(jh, tiles):
             cols = slice(jh * COLS, (jh + 1) * COLS)
@@ -259,18 +263,10 @@ def tile_list_factored_quadratic_scores_kernel(
                         stop=(b == H_PASSES - 1),
                     )
                 result = held("result%d%d" % (jh, u), [P, COLS], F32)
-                if jh == 0 and u >= 2:
-                    rest = late[:, u, :]
-                    nc.scalar.activation(rest, acc[:], ACT.Identity, bias=bias[:, u : u + 1], scale=-1.0)
-                    nc.gpsimd.tensor_tensor(result[:], lin_sq[(jh, u)], rest, ALU.add)
-                else:
-                    nc.vector.scalar_tensor_tensor(
-                        result[:], lin_sq[(jh, u)], bias[:, u : u + 1], acc[:], ALU.add, ALU.subtract
-                    )
-                if jh == 0 and u >= 2:
-                    late_stores.append((out[u * P : (u + 1) * P, cols], result[:]))
-                else:
-                    nc.sync.dma_start(out[u * P : (u + 1) * P, cols], result[:])
+                nc.vector.scalar_tensor_tensor(
+                    result[:], lin_sq[(jh, u)], bias[:, u : u + 1], acc[:], ALU.add, ALU.subtract
+                )
+                nc.sync.dma_start(out[u * P : (u + 1) * P, cols], result[:])
 
         on_vector, on_scalar = nc.vector.tensor_copy, nc.scalar.copy
 
@@ -278,9 +274,11 @@ def tile_list_factored_quadratic_scores_kernel(
         square_lin(1, [0, 1])
         cast_wf(0, 0, "work", on_vector)
         quantise("wf00", parts=2)
-        cast_wf(0, 1, "work", on_vector)
+        cast_wf(0, 1, "work", on_vector, [0])
+        quantise("wf01", parts=2, only=0)
+        cast_wf(0, 1, "work", on_vector, [1])
         load_wf(1, 1, wf_room(1, 1, "room2"))
-        quantise("wf01", parts=2)
+        quantise("wf01", parts=2, only=1)
         square_h(0, 0)
         square_h(0, 1)
         cast_wm(0, "work", parts=2)
@@ -295,21 +293,21 @@ def tile_list_factored_quadratic_scores_kernel(
         cast_wf(1, 1, "work", on_vector)
         quantise("wf11", parts=2)
         interleave_z(0, 1, "z_grouped01", on_scalar)
-        square_h(1, 0)
-        square_h(1, 1)
         interleave_z(0, 0, "room2", on_vector)
         cast_wm(1, "other_work")
         quantise("z00")
         sign_wm(1)
-        interleave_z(1, 0, "room0", on_vector)
+        square_h(1, 0)
+        interleave_z(1, 0, "room0", on_scalar, 0, COLS // 2)
+        square_h(1, 1)
+        interleave_z(1, 0, "room0", on_vector, COLS // 2, COLS)
         quantise("wm1")
         interleave_z(1, 1, "z_grouped11", on_scalar)
         quantise("z10")
         quantise("z01", "z_planes01")
-        late = shared("late", "z_planes11", [P, 4, COLS], F32)
-        finish(0, range(N_TILES))
+        late = shared("late", "z_planes11", [P, 2, COLS], F32)
+        finish(0, [0, 1])
         quantise("z11", "lin_sq01")
+        finish(0, [2, 3])
         square_lin(1, [2, 3], late)
-        for rows, result in late_stores:
-            nc.scalar.dma_start(rows, result)
         finish(1, range(N_TILES))

@@ -298,9 +298,9 @@ def tile_list_factored_quadratic_scores_kernel(
         quantise("z00")
         sign_wm(1)
         square_h(1, 0)
-        interleave_z(1, 0, "room0", on_scalar, 0, COLS // 2)
+        interleave_z(1, 0, "room0", on_scalar, 0, COLS // 4)
         square_h(1, 1)
-        interleave_z(1, 0, "room0", on_vector, COLS // 2, COLS)
+        interleave_z(1, 0, "room0", on_vector, COLS // 4, COLS)
         quantise("wm1")
         interleave_z(1, 1, "z_grouped11", on_scalar)
         quantise("z10")

@@ -98,8 +98,8 @@ def tile_list_factored_quadratic_scores_kernel(
             return shared("wf_raw%d%d" % (b, a), tag, [P, PACK, PASS], F32)[:]
 
         nc.scalar.copy(
-            vec_rows[0:H_PASSES, :, :].rearrange("b (e f) (u i) -> b e f u i", f=2, i=4),
-            gain_rows[:].rearrange("b (u e i f) -> b e f u i", e=2, i=4, f=2),
+            vec_rows[0:H_PASSES, :, :].rearrange("b (e f) (u i) -> b e f u i", f=2, i=2),
+            gain_rows[:].rearrange("b (u e i f) -> b e f u i", e=2, i=2, f=2),
         )
         gain_columns = psum.tile([P, PACK, P], F32, name="gain_columns", tag="bank7")
         for t in range(PACK):
@@ -115,7 +115,7 @@ def tile_list_factored_quadratic_scores_kernel(
 
         def load_wm(b, tag):
             raw = shared("wm_raw%d" % b, tag, [P, PACK, N], F32)
-            rows = wm[b * PASS : (b + 1) * PASS, :].rearrange("(u e i f) c -> e u i (f c)", e=2, i=4, f=2)
+            rows = wm[b * PASS : (b + 1) * PASS, :].rearrange("(u e i f) c -> e u i (f c)", e=2, i=2, f=2)
             for e in range(2):
                 nc.sync.dma_start(raw[:, 2 * e : 2 * e + 2, :].rearrange("p f c -> p (f c)"), rows[e])
             wm_raw[b] = raw[:]
@@ -192,8 +192,8 @@ def tile_list_factored_quadratic_scores_kernel(
             if key not in grouped_tiles:
                 grouped_tiles[key] = shared("grouped_" + key, tag, [P, PASS * PACK], BF16)
             grouped = grouped_tiles[key]
-            dst = grouped[:].rearrange("p (e f u i j) -> p e u j i f", e=2, f=2, i=4, j=PACK)
-            src = wf_raw[(b, a)].rearrange("p j (u e i f) -> p e u j i f", e=2, i=4, f=2)
+            dst = grouped[:].rearrange("p (e f u i j) -> p e u j i f", e=2, f=2, i=2, j=PACK)
+            src = wf_raw[(b, a)].rearrange("p j (u e i f) -> p e u j i f", e=2, i=2, f=2)
             for e in halves:
                 copy(dst[:, e], src[:, e])
 

@@ -21,11 +21,16 @@ P = 128
 PACK = 4
 PASS = P * PACK
 COLS = 512
+BANKS = 8
+QUADRANTS = 4
 HALVES = S // COLS
 K_PASSES = K // PASS
 H_PASSES = H // PASS
 N_TILES = N // P
 LIST_COLS = COLS // 16
+EARLY_LIN = 2
+SCALAR_COLUMNS = 96
+LINE = 8
 
 
 def tile_list_factored_quadratic_scores_kernel(
@@ -39,15 +44,20 @@ def tile_list_factored_quadratic_scores_kernel(
         def held(name, shape, dtype):
             return keep.tile(shape, dtype, name=name, align_bytes=64)
 
+        def shared(name, tag, shape, dtype):
+            return keep.tile(shape, dtype, name=name, tag=tag, align_bytes=64)
+
+        def bank(number):
+            return psum.tile([P, COLS], F32, name="acc", tag="bank%d" % number)
+
         banks_opened = []
 
         def next_bank():
-            bank = len(banks_opened) % 8
-            banks_opened.append(bank)
-            return psum.tile([P, COLS], F32, name="acc", tag="bank%d" % bank)
+            banks_opened.append(len(banks_opened) % BANKS)
+            return bank(banks_opened[-1])
 
-        def shared(name, tag, shape, dtype):
-            return keep.tile(shape, dtype, name=name, tag=tag, align_bytes=64)
+        def pass_order(half):
+            return (0, 1) if half == 0 else (1, 0)
 
         offsets = keep.tile([P, S // 16], U16, name="offsets")
         nc.sync.dma_start(offsets[:], offs)
@@ -56,9 +66,9 @@ def tile_list_factored_quadratic_scores_kernel(
         nc.gpsimd.memset(tab_sc[:], 0)
         gain_rows = held("gain_rows", [H_PASSES, PASS], F32)
         nc.sync.dma_start(gain_rows[:], gain.rearrange("(b r) -> b r", b=H_PASSES))
-        scale_rows = tab_scales.bitcast(I32).rearrange("a (q r) c -> r q a c", r=4)
-        for r in range(4):
-            nc.sync.dma_start(tab_sc[r:P:16, :], scale_rows[r])
+        scale_rows = tab_scales.bitcast(I32).rearrange("a (q m) c -> m q a c", q=QUADRANTS)
+        for m in range(4):
+            nc.sync.dma_start(tab_sc[m:P:16, :], scale_rows[m])
         tab_w = [shared("tab_w%d" % a, "room%d" % a, [P, T], I32) for a in range(K_PASSES)]
 
         def load_table_words(a):
@@ -68,18 +78,18 @@ def tile_list_factored_quadratic_scores_kernel(
 
         wl_sc = held("wl_sc", [P, K_PASSES, N // 4], I32)
         nc.gpsimd.memset(wl_sc[:], 0)
-        vec_rows = held("vec_rows", [P, PACK, P], F32)
-        nc.gpsimd.memset(vec_rows[:], 0.0)
-        v_sc_low = held("v_sc_low", [P, S // 4], I32)
-        nc.gpsimd.memset(v_sc_low[:], 0)
+        gain_slots = held("gain_slots", [P, PACK, P], F32)
+        nc.gpsimd.memset(gain_slots[:], 0.0)
+        v_sc_second = held("v_sc_second", [P, S // 4], I32)
+        nc.gpsimd.memset(v_sc_second[:], 0)
         identity = held("identity", [P, P], F32)
         make_identity(nc, identity[:])
 
         wl_scales_i = wl_scales.bitcast(I32)
-        for q in range(4):
+        for q in range(QUADRANTS):
             nc.sync.dma_start(
                 wl_sc[32 * q : 32 * q + 4, :, :],
-                wl_scales_i[:, 4 * q : 4 * q + 4, :].rearrange("a r c -> r a c"),
+                wl_scales_i[:, 4 * q : 4 * q + 4, :].rearrange("a m c -> m a c"),
             )
         wl_w = held("wl_w", [P, K_PASSES, N // 2], I32)
         nc.sync.dma_start(wl_w[:], wl_words.bitcast(I32).rearrange("a p c -> p a c"))
@@ -98,12 +108,12 @@ def tile_list_factored_quadratic_scores_kernel(
             return shared("wf_raw%d%d" % (b, a), tag, [P, PACK, PASS], F32)[:]
 
         nc.scalar.copy(
-            vec_rows[0:H_PASSES, :, :].rearrange("b (e f) (u i) -> b e f u i", f=2, i=2),
+            gain_slots[0:H_PASSES, :, :].rearrange("b (e f) (u i) -> b e f u i", f=2, i=2),
             gain_rows[:].rearrange("b (u e i f) -> b e f u i", e=2, i=2, f=2),
         )
-        gain_columns = psum.tile([P, PACK, P], F32, name="gain_columns", tag="bank7")
-        for t in range(PACK):
-            nc.tensor.transpose(gain_columns[:, t, :], vec_rows[:, t, :], identity[:])
+        gain_columns = psum.tile([P, PACK, P], F32, name="gain_columns", tag="bank%d" % (BANKS - 1))
+        for slot in range(PACK):
+            nc.tensor.transpose(gain_columns[:, slot, :], gain_slots[:, slot, :], identity[:])
         magnitude = held("magnitude", [P, PACK, H_PASSES], F32)
         root = held("root", [P, PACK, H_PASSES], F32)
         sign = held("sign", [P, H_PASSES, PACK], BF16)
@@ -123,17 +133,16 @@ def tile_list_factored_quadratic_scores_kernel(
         v_w = {}
 
         def gather_words(a):
-            for jh in range(HALVES):
-                picked = held("v_w%d%d" % (a, jh), [P, COLS], U32)
-                nc.vector.tensor_copy(
-                    picked[:], tab_w[a][:].bitcast(U32).indirect(offsets[:, jh * LIST_COLS : (jh + 1) * LIST_COLS])
-                )
-                v_w[(a, jh)] = picked
+            for half in range(HALVES):
+                picked = held("v_w%d%d" % (a, half), [P, COLS], U32)
+                entries = offsets[:, half * LIST_COLS : (half + 1) * LIST_COLS]
+                nc.vector.tensor_copy(picked[:], tab_w[a][:].bitcast(U32).indirect(entries))
+                v_w[(a, half)] = picked
 
         v_sc = held("v_sc", [P, S], U8)
         nc.vector.tensor_copy(v_sc[:], tab_sc[:].bitcast(U8).indirect(offsets[:]))
-        for q in range(4):
-            nc.sync.dma_start(v_sc_low[32 * q : 32 * q + 4, :], v_sc[32 * q + 16 : 32 * q + 20, :].bitcast(I32))
+        for q in range(QUADRANTS):
+            nc.sync.dma_start(v_sc_second[32 * q : 32 * q + 4, :], v_sc[32 * q + 16 : 32 * q + 20, :].bitcast(I32))
         first_wf = shared("first_wf", "room2", [P, K_PASSES, PACK, PASS], F32)
         load_wf(0, 0, first_wf[:, 0])
         load_wf(0, 1, first_wf[:, 1])
@@ -142,35 +151,30 @@ def tile_list_factored_quadratic_scores_kernel(
         gather_words(1)
         load_wf(1, 0, wf_room(1, 0, "room1"))
 
-        def v_plane(a, cols):
-            return v_sc[:, cols] if a == 0 else v_sc_low[:].bitcast(U8)[:, cols]
+        def v_plane(a, half):
+            plane = v_sc[:] if a == 0 else v_sc_second[:].bitcast(U8)
+            return plane[:, half * COLS : (half + 1) * COLS]
 
         lin_sq = {}
 
-        def square_lin(jh, tiles, room=None):
-            cols = slice(jh * COLS, (jh + 1) * COLS)
-            for u in tiles:
-                acc = next_bank()
-                order = (0, 1) if jh == 0 else (1, 0)
-                for a in order:
-                    nc.tensor.matmul_mx(
-                        out=acc[:],
-                        lhsT=wl_w[:, a, :].bitcast(U8)[:, 2 * u * P : 2 * (u + 1) * P].bitcast(FP4X4),
-                        lhsT_scale=wl_sc[:, a, :].bitcast(U8)[:, u * P : (u + 1) * P],
-                        rhs=v_w[(a, jh)][:].bitcast(FP8X4),
-                        rhs_scale=v_plane(a, cols),
-                        start=(a == order[0]),
-                        stop=(a == order[1]),
-                    )
-                if room is None:
-                    squared = shared("lin_sq%d%d" % (jh, u), "lin_sq%d%d" % (jh, u), [P, COLS], F32)[:]
-                else:
-                    squared = room[:, u - 2, :]
-                nc.scalar.activation(squared, acc[:], ACT.Square)
-                lin_sq[(jh, u)] = squared
+        def square_lin(half, u, squared):
+            acc = next_bank()
+            order = pass_order(half)
+            for a in order:
+                nc.tensor.matmul_mx(
+                    out=acc[:],
+                    lhsT=wl_w[:, a, :].bitcast(U8)[:, 2 * u * P : 2 * (u + 1) * P].bitcast(FP4X4),
+                    lhsT_scale=wl_sc[:, a, :].bitcast(U8)[:, u * P : (u + 1) * P],
+                    rhs=v_w[(a, half)][:].bitcast(FP8X4),
+                    rhs_scale=v_plane(a, half),
+                    start=(a == order[0]),
+                    stop=(a == order[1]),
+                )
+            nc.scalar.activation(squared, acc[:], ACT.Square)
+            lin_sq[(half, u)] = squared
 
+        grouped = {}
         quantised = {}
-        grouped_tiles = {}
 
         def quantise(key, tag=None, parts=1, only=None):
             if key not in quantised:
@@ -184,130 +188,130 @@ def tile_list_factored_quadratic_scores_kernel(
                 nc.vector.quantize_mx(
                     out=codes[:, words].bitcast(FP8X4),
                     scales=scales[:, words],
-                    in_=grouped_tiles[key][:, PACK * part * width : PACK * (part + 1) * width],
+                    in_=grouped[key][:, PACK * part * width : PACK * (part + 1) * width],
                 )
 
-        def cast_wf(b, a, tag, copy, halves=(0, 1)):
+        def cast_wf(b, a, tag, slot_pairs=(0, 1)):
             key = "wf%d%d" % (b, a)
-            if key not in grouped_tiles:
-                grouped_tiles[key] = shared("grouped_" + key, tag, [P, PASS * PACK], BF16)
-            grouped = grouped_tiles[key]
-            dst = grouped[:].rearrange("p (e f u i j) -> p e u j i f", e=2, f=2, i=2, j=PACK)
+            if key not in grouped:
+                grouped[key] = shared("grouped_" + key, tag, [P, PASS * PACK], BF16)
+            dst = grouped[key][:].rearrange("p (e f u i j) -> p e u j i f", e=2, f=2, i=2, j=PACK)
             src = wf_raw[(b, a)].rearrange("p j (u e i f) -> p e u j i f", e=2, i=2, f=2)
-            for e in halves:
-                copy(dst[:, e], src[:, e])
+            for e in slot_pairs:
+                nc.vector.tensor_copy(dst[:, e], src[:, e])
 
         def cast_wm(b, tag, parts=1):
-            grouped = shared("wm_grouped%d" % b, tag, [P, N * PACK], BF16)
-            dst = grouped[:].rearrange("p (c i j) -> p c j i", i=4, j=PACK)
+            key = "wm%d" % b
+            grouped[key] = shared("grouped_" + key, tag, [P, N * PACK], BF16)
+            dst = grouped[key][:].rearrange("p (c i j) -> p c j i", i=4, j=PACK)
             src = wm_raw[b].rearrange("p j (c i) -> p c j i", i=4)
             width = N // 4 // parts
             for part in range(parts):
-                nc.vector.tensor_copy(dst[:, part * width : (part + 1) * width], src[:, part * width : (part + 1) * width])
-            grouped_tiles["wm%d" % b] = grouped
+                columns = slice(part * width, (part + 1) * width)
+                nc.vector.tensor_copy(dst[:, columns], src[:, columns])
 
         def sign_wm(b, parts=1):
-            grouped = grouped_tiles["wm%d" % b][:].rearrange("p (c j) -> p c j", j=PACK)
+            rounded = grouped["wm%d" % b][:].rearrange("p (c j) -> p c j", j=PACK)
             width = N // parts
             signs = sign[:, b, :].unsqueeze(1).broadcast_to([P, width, PACK])
             for part in range(parts):
-                columns = grouped[:, part * width : (part + 1) * width, :]
-                nc.vector.tensor_tensor(columns, columns, signs, ALU.mult)
+                piece = rounded[:, part * width : (part + 1) * width, :]
+                nc.vector.tensor_tensor(piece, piece, signs, ALU.mult)
 
-        z_planes = {}
+        z_slots = {}
 
-        def square_h(b, jh):
-            cols = slice(jh * COLS, (jh + 1) * COLS)
-            name = "z_planes%d%d" % (b, jh)
-            planes = shared(name, "z_planes01" if (b, jh) == (1, 0) else name, [P, PACK, COLS], BF16)
-            for t in range(PACK):
+        def square_h(b, half, tag):
+            squares = shared("z_slots%d%d" % (b, half), tag, [P, PACK, COLS], BF16)
+            for slot in range(PACK):
                 acc = next_bank()
-                order = (0, 1) if jh == 0 else (1, 0)
+                order = pass_order(half)
                 for a in order:
                     codes, scales = quantised["wf%d%d" % (b, a)]
                     nc.tensor.matmul_mx(
                         out=acc[:],
-                        lhsT=codes[:, t * P : (t + 1) * P].bitcast(FP8X4),
-                        lhsT_scale=scales[:, t * P : (t + 1) * P],
-                        rhs=v_w[(a, jh)][:].bitcast(FP8X4),
-                        rhs_scale=v_plane(a, cols),
+                        lhsT=codes[:, slot * P : (slot + 1) * P].bitcast(FP8X4),
+                        lhsT_scale=scales[:, slot * P : (slot + 1) * P],
+                        rhs=v_w[(a, half)][:].bitcast(FP8X4),
+                        rhs_scale=v_plane(a, half),
                         start=(a == order[0]),
                         stop=(a == order[1]),
                     )
-                nc.scalar.activation(planes[:, t, :], acc[:], ACT.Square, scale=root[:, t, b : b + 1])
-            z_planes[(b, jh)] = planes
+                nc.scalar.activation(squares[:, slot, :], acc[:], ACT.Square, scale=root[:, slot, b : b + 1])
+            z_slots[(b, half)] = squares
 
-        def interleave_z(b, jh, tag, copy, first=0, last=COLS):
-            key = "z%d%d" % (b, jh)
-            if key not in grouped_tiles:
-                grouped_tiles[key] = shared("grouped_" + key, tag, [P, COLS * PACK], BF16)
-            dst = grouped_tiles[key][:, PACK * first : PACK * last].rearrange("p (c i t) -> p c t i", i=4, t=PACK)
-            copy(dst, z_planes[(b, jh)][:, :, first:last].rearrange("p t (c i) -> p c t i", i=4))
+        def interleave_z(b, half, tag, copy, first=0, last=COLS):
+            key = "z%d%d" % (b, half)
+            if key not in grouped:
+                grouped[key] = shared("grouped_" + key, tag, [P, COLS * PACK], BF16)
+            dst = grouped[key][:, PACK * first : PACK * last].rearrange("p (c i t) -> p c t i", i=LINE, t=PACK)
+            copy(dst, z_slots[(b, half)][:, :, first:last].rearrange("p t (c i) -> p c t i", i=LINE))
 
-        y_bank = {(0, 0): 2, (0, 1): 3, (0, 2): 4, (0, 3): 5, (1, 0): 0, (1, 1): 1, (1, 2): 2, (1, 3): 3}
-
-        def finish(jh, tiles):
-            cols = slice(jh * COLS, (jh + 1) * COLS)
-            for u in tiles:
-                acc = psum.tile([P, COLS], F32, name="acc", tag="bank%d" % y_bank[(jh, u)])
-                for b in range(H_PASSES):
-                    w_codes, w_scales = quantised["wm%d" % b]
-                    z_codes, z_scales = quantised["z%d%d" % (b, jh)]
-                    nc.tensor.matmul_mx(
-                        out=acc[:],
-                        lhsT=w_codes[:, u * P : (u + 1) * P].bitcast(FP8X4),
-                        lhsT_scale=w_scales[:, u * P : (u + 1) * P],
-                        rhs=z_codes[:].bitcast(FP8X4),
-                        rhs_scale=z_scales[:],
-                        start=(b == 0),
-                        stop=(b == H_PASSES - 1),
-                    )
-                result = held("result%d%d" % (jh, u), [P, COLS], F32)
-                nc.vector.scalar_tensor_tensor(
-                    result[:], lin_sq[(jh, u)], bias[:, u : u + 1], acc[:], ALU.add, ALU.subtract
+        def finish(half, u, result):
+            acc = bank((N_TILES * half + u) % (BANKS - (N_TILES - EARLY_LIN)))
+            for b in range(H_PASSES):
+                w_codes, w_scales = quantised["wm%d" % b]
+                z_codes, z_scales = quantised["z%d%d" % (b, half)]
+                nc.tensor.matmul_mx(
+                    out=acc[:],
+                    lhsT=w_codes[:, u * P : (u + 1) * P].bitcast(FP8X4),
+                    lhsT_scale=w_scales[:, u * P : (u + 1) * P],
+                    rhs=z_codes[:].bitcast(FP8X4),
+                    rhs_scale=z_scales[:],
+                    start=(b == 0),
+                    stop=(b == H_PASSES - 1),
                 )
-                nc.sync.dma_start(out[u * P : (u + 1) * P, cols], result[:])
+            nc.vector.scalar_tensor_tensor(result, lin_sq[(half, u)], bias[:, u : u + 1], acc[:], ALU.add, ALU.subtract)
+            nc.sync.dma_start(out[u * P : (u + 1) * P, half * COLS : (half + 1) * COLS], result)
+
+        def float_tile(name, half, u):
+            return held("%s%d%d" % (name, half, u), [P, COLS], F32)[:]
 
         on_vector, on_scalar = nc.vector.tensor_copy, nc.scalar.copy
 
-        square_lin(0, range(N_TILES))
-        square_lin(1, [0, 1])
-        cast_wf(0, 0, "work", on_vector)
+        for u in range(N_TILES):
+            square_lin(0, u, float_tile("lin_sq", 0, u))
+        for u in range(EARLY_LIN):
+            square_lin(1, u, float_tile("lin_sq", 1, u))
+        cast_wf(0, 0, "work")
         quantise("wf00", parts=2)
-        cast_wf(0, 1, "work", on_vector, [0])
+        cast_wf(0, 1, "work", [0])
         quantise("wf01", parts=2, only=0)
-        cast_wf(0, 1, "work", on_vector, [1])
+        cast_wf(0, 1, "work", [1])
         load_wf(1, 1, wf_room(1, 1, "room2"))
         quantise("wf01", parts=2, only=1)
-        square_h(0, 0)
-        square_h(0, 1)
+        square_h(0, 0, "z_slots00")
+        square_h(0, 1, "z_slots01")
         cast_wm(0, "work", parts=2)
         load_wm(1, "room0")
         sign_wm(0, parts=2)
         quantise("wm0", parts=2)
-        cast_wf(1, 0, "other_work", on_vector)
+        cast_wf(1, 0, "other_work")
         bias = shared("bias", "room1", [P, N_TILES], F32)
         with nc.allow_non_contiguous_dma(reason="one bias value a partition"):
             nc.sync.dma_start(bias[:], b0.rearrange("(u p) -> p u", p=P))
         quantise("wf10", parts=2)
-        cast_wf(1, 1, "work", on_vector)
+        cast_wf(1, 1, "work")
         quantise("wf11", parts=2)
-        interleave_z(0, 1, "z_grouped01", on_scalar)
+        interleave_z(0, 1, "grouped_z01", on_scalar)
         interleave_z(0, 0, "room2", on_vector)
         cast_wm(1, "other_work")
         quantise("z00")
         sign_wm(1)
-        square_h(1, 0)
-        interleave_z(1, 0, "room0", on_scalar, 0, COLS // 4)
-        square_h(1, 1)
-        interleave_z(1, 0, "room0", on_vector, COLS // 4, COLS)
+        square_h(1, 0, "z_slots01")
+        interleave_z(1, 0, "room0", on_scalar, 0, SCALAR_COLUMNS)
+        square_h(1, 1, "z_slots11")
+        interleave_z(1, 0, "room0", on_vector, SCALAR_COLUMNS, COLS)
         quantise("wm1")
-        interleave_z(1, 1, "z_grouped11", on_scalar)
+        interleave_z(1, 1, "grouped_z11", on_scalar)
         quantise("z10")
-        quantise("z01", "z_planes01")
-        late = shared("late", "z_planes11", [P, 2, COLS], F32)
-        finish(0, [0, 1])
+        quantise("z01", "z_slots01")
+        late_lin = range(EARLY_LIN, N_TILES)
+        late = shared("late", "z_slots11", [P, len(late_lin) + 1, COLS], F32)
+        for u in range(N_TILES - 1):
+            finish(0, u, float_tile("result", 0, u))
         quantise("z11", "lin_sq01")
-        finish(0, [2, 3])
-        square_lin(1, [2, 3], late)
-        finish(1, range(N_TILES))
+        finish(0, N_TILES - 1, late[:, len(late_lin), :])
+        for u in late_lin:
+            square_lin(1, u, late[:, u - EARLY_LIN, :])
+        for u in range(N_TILES):
+            finish(1, u, float_tile("result", 1, u))

@@ -30,6 +30,7 @@ N_TILES = N // P
 LIST_COLS = COLS // 16
 EARLY_LIN = 2
 SCALAR_COLUMNS = 96
+PIECE = PASS // 2
 LINE = 8
 
 
@@ -66,6 +67,8 @@ def tile_list_factored_quadratic_scores_kernel(
         nc.gpsimd.memset(tab_sc[:], 0)
         gain_rows = held("gain_rows", [H_PASSES, PASS], F32)
         nc.sync.dma_start(gain_rows[:], gain.rearrange("(b r) -> b r", b=H_PASSES))
+        wl_w = held("wl_w", [P, K_PASSES, N // 2], I32)
+        nc.sync.dma_start(wl_w[:], wl_words.bitcast(I32).rearrange("a p c -> p a c"))
         scale_rows = tab_scales.bitcast(I32).rearrange("a (q m) c -> m q a c", q=QUADRANTS)
         for m in range(4):
             nc.sync.dma_start(tab_sc[m:P:16, :], scale_rows[m])
@@ -91,25 +94,27 @@ def tile_list_factored_quadratic_scores_kernel(
                 wl_sc[32 * q : 32 * q + 4, :, :],
                 wl_scales_i[:, 4 * q : 4 * q + 4, :].rearrange("a m c -> m a c"),
             )
-        wl_w = held("wl_w", [P, K_PASSES, N // 2], I32)
-        nc.sync.dma_start(wl_w[:], wl_words.bitcast(I32).rearrange("a p c -> p a c"))
         load_table_words(1)
 
         wf_raw = {}
 
-        def load_wf(b, a, raw):
-            nc.sync.dma_start(
-                raw,
-                wf[a * PASS : (a + 1) * PASS, b * PASS : (b + 1) * PASS].rearrange("(p j) c -> p j c", j=PACK),
-            )
-            wf_raw[(b, a)] = raw
+        def load_rows(source, room):
+            raw = room.rearrange("p (j c) -> p j c", j=PACK)
+            nc.sync.dma_start(raw, source.rearrange("(p j) c -> p j c", j=PACK))
+            return raw
 
-        def wf_room(b, a, tag):
-            return shared("wf_raw%d%d" % (b, a), tag, [P, PACK, PASS], F32)[:]
+        def load_wf(b, a, side, room):
+            columns = slice(b * PASS + side * PIECE, b * PASS + (side + 1) * PIECE)
+            wf_raw[(b, a, side)] = load_rows(wf[a * PASS : (a + 1) * PASS, columns], room)
+
+        def pieces(name, tag, count):
+            return shared(name, tag, [P, count, PACK * PIECE], F32)
+
+        load_wf(0, 0, 0, pieces("wf_first", "early", 1)[:, 0, :])
 
         nc.scalar.copy(
-            gain_slots[0:H_PASSES, :, :].rearrange("b (e f) (u i) -> b e f u i", f=2, i=2),
-            gain_rows[:].rearrange("b (u e i f) -> b e f u i", e=2, i=2, f=2),
+            gain_slots[0:H_PASSES, :, :],
+            gain_rows[:].rearrange("b (m t) -> b t m", t=PACK),
         )
         gain_columns = psum.tile([P, PACK, P], F32, name="gain_columns", tag="bank%d" % (BANKS - 1))
         for slot in range(PACK):
@@ -122,13 +127,6 @@ def tile_list_factored_quadratic_scores_kernel(
         nc.scalar.activation(sign[:].rearrange("p b t -> p t b"), gain_columns[:, :, 0:H_PASSES], ACT.Sign)
 
         wm_raw = {}
-
-        def load_wm(b, tag):
-            raw = shared("wm_raw%d" % b, tag, [P, PACK, N], F32)
-            rows = wm[b * PASS : (b + 1) * PASS, :].rearrange("(u e i f) c -> e u i (f c)", e=2, i=2, f=2)
-            for e in range(2):
-                nc.sync.dma_start(raw[:, 2 * e : 2 * e + 2, :].rearrange("p f c -> p (f c)"), rows[e])
-            wm_raw[b] = raw[:]
 
         v_w = {}
 
@@ -143,13 +141,18 @@ def tile_list_factored_quadratic_scores_kernel(
         nc.vector.tensor_copy(v_sc[:], tab_sc[:].bitcast(U8).indirect(offsets[:]))
         for q in range(QUADRANTS):
             nc.sync.dma_start(v_sc_second[32 * q : 32 * q + 4, :], v_sc[32 * q + 16 : 32 * q + 20, :].bitcast(I32))
-        first_wf = shared("first_wf", "room2", [P, K_PASSES, PACK, PASS], F32)
-        load_wf(0, 0, first_wf[:, 0])
-        load_wf(0, 1, first_wf[:, 1])
+        room = pieces("wf_second", "room2", 3)
+        load_wf(0, 0, 1, room[:, 0, :])
+        load_wf(0, 1, 0, room[:, 1, :])
+        load_wf(0, 1, 1, room[:, 2, :])
         gather_words(0)
-        load_wm(0, "room0")
+        room = pieces("wm_first", "room0", 2)
+        for side in range(2):
+            wm_raw[(0, side)] = load_rows(wm[0:PASS, side * PIECE : (side + 1) * PIECE], room[:, side, :])
         gather_words(1)
-        load_wf(1, 0, wf_room(1, 0, "room1"))
+        room = pieces("wf_third", "room1", 2)
+        for side in range(2):
+            load_wf(1, 0, side, room[:, side, :])
 
         def v_plane(a, half):
             plane = v_sc[:] if a == 0 else v_sc_second[:].bitcast(U8)
@@ -157,8 +160,8 @@ def tile_list_factored_quadratic_scores_kernel(
 
         lin_sq = {}
 
-        def square_lin(half, u, squared):
-            acc = next_bank()
+        def square_lin(half, u, squared, number):
+            acc = bank(number)
             order = pass_order(half)
             for a in order:
                 nc.tensor.matmul_mx(
@@ -191,24 +194,24 @@ def tile_list_factored_quadratic_scores_kernel(
                     in_=grouped[key][:, PACK * part * width : PACK * (part + 1) * width],
                 )
 
-        def cast_wf(b, a, tag, slot_pairs=(0, 1)):
+        def cast_wf(b, a, side, copy=nc.vector.tensor_copy, parts=1):
             key = "wf%d%d" % (b, a)
             if key not in grouped:
-                grouped[key] = shared("grouped_" + key, tag, [P, PASS * PACK], BF16)
-            dst = grouped[key][:].rearrange("p (e f u i j) -> p e u j i f", e=2, f=2, i=2, j=PACK)
-            src = wf_raw[(b, a)].rearrange("p j (u e i f) -> p e u j i f", e=2, i=2, f=2)
-            for e in slot_pairs:
-                nc.vector.tensor_copy(dst[:, e], src[:, e])
-
-        def cast_wm(b, tag, parts=1):
-            key = "wm%d" % b
-            grouped[key] = shared("grouped_" + key, tag, [P, N * PACK], BF16)
-            dst = grouped[key][:].rearrange("p (c i j) -> p c j i", i=4, j=PACK)
-            src = wm_raw[b].rearrange("p j (c i) -> p c j i", i=4)
-            width = N // 4 // parts
+                grouped[key] = held("grouped_" + key, [P, PASS * PACK], BF16)
+            dst = grouped[key][:].rearrange("p (t s u i j) -> p s u j i t", t=PACK, s=2, i=2, j=PACK)
+            src = wf_raw[(b, a, side)].rearrange("p j (u i t) -> p u j i t", i=2, t=PACK)
+            width = PACK // parts
             for part in range(parts):
-                columns = slice(part * width, (part + 1) * width)
-                nc.vector.tensor_copy(dst[:, columns], src[:, columns])
+                slots = slice(part * width, (part + 1) * width)
+                copy(dst[:, side, :, :, :, slots], src[:, :, :, :, slots])
+
+        def cast_wm(b, raw, first):
+            key = "wm%d" % b
+            if key not in grouped:
+                grouped[key] = held("grouped_" + key, [P, N * PACK], BF16)
+            src = raw.rearrange("p j (c i) -> p c j i", i=4)
+            dst = grouped[key][:].rearrange("p (c i j) -> p c j i", i=4, j=PACK)
+            nc.vector.tensor_copy(dst[:, first // 4 : first // 4 + src.shape[1]], src)
 
         def sign_wm(b, parts=1):
             rounded = grouped["wm%d" % b][:].rearrange("p (c j) -> p c j", j=PACK)
@@ -220,10 +223,10 @@ def tile_list_factored_quadratic_scores_kernel(
 
         z_slots = {}
 
-        def square_h(b, half, tag):
+        def square_h(b, half, tag, banks):
             squares = shared("z_slots%d%d" % (b, half), tag, [P, PACK, COLS], BF16)
             for slot in range(PACK):
-                acc = next_bank()
+                acc = bank(banks[slot])
                 order = pass_order(half)
                 for a in order:
                     codes, scales = quantised["wf%d%d" % (b, a)]
@@ -247,7 +250,7 @@ def tile_list_factored_quadratic_scores_kernel(
             copy(dst, z_slots[(b, half)][:, :, first:last].rearrange("p t (c i) -> p c t i", i=LINE))
 
         def finish(half, u, result):
-            acc = bank((N_TILES * half + u) % (BANKS - (N_TILES - EARLY_LIN)))
+            acc = bank(((4, 5, 1, 7), (0, 6, 4, 5))[half][u])
             for b in range(H_PASSES):
                 w_codes, w_scales = quantised["wm%d" % b]
                 z_codes, z_scales = quantised["z%d%d" % (b, half)]
@@ -268,38 +271,46 @@ def tile_list_factored_quadratic_scores_kernel(
 
         on_vector, on_scalar = nc.vector.tensor_copy, nc.scalar.copy
 
+        cast_wf(0, 0, 0, on_scalar)
+        early = shared("early_lin", "early", [P, N_TILES + EARLY_LIN, COLS], F32)
         for u in range(N_TILES):
-            square_lin(0, u, float_tile("lin_sq", 0, u))
+            square_lin(0, u, early[:, u, :], u)
         for u in range(EARLY_LIN):
-            square_lin(1, u, float_tile("lin_sq", 1, u))
-        cast_wf(0, 0, "work")
+            square_lin(1, u, early[:, N_TILES + u, :], N_TILES + u)
+        cast_wf(0, 0, 1)
         quantise("wf00", parts=2)
-        cast_wf(0, 1, "work", [0])
-        quantise("wf01", parts=2, only=0)
-        cast_wf(0, 1, "work", [1])
-        load_wf(1, 1, wf_room(1, 1, "room2"))
-        quantise("wf01", parts=2, only=1)
-        square_h(0, 0, "z_slots00")
-        square_h(0, 1, "z_slots01")
-        cast_wm(0, "work", parts=2)
-        load_wm(1, "room0")
+        cast_wf(0, 1, 0)
+        cast_wf(0, 1, 1, parts=2)
+        room = pieces("wf_last", "room2", 2)
+        for side in range(2):
+            load_wf(1, 1, side, room[:, side, :])
+        quantise("wf01", parts=2)
+        square_h(0, 0, "z_slots00", (6, 7, 0, 1))
+        square_h(0, 1, "z_slots01", (6, 7, 0, 6))
+        for side in range(2):
+            cast_wm(0, wm_raw[(0, side)], side * PIECE)
+        last_wm = load_rows(wm[PASS:, :], shared("wm_last", "room0", [P, PACK * N], F32)[:])
         sign_wm(0, parts=2)
         quantise("wm0", parts=2)
-        cast_wf(1, 0, "other_work")
+        cast_wf(1, 0, 0)
+        cast_wf(1, 0, 1)
         bias = shared("bias", "room1", [P, N_TILES], F32)
         with nc.allow_non_contiguous_dma(reason="one bias value a partition"):
             nc.sync.dma_start(bias[:], b0.rearrange("(u p) -> p u", p=P))
+        cast_wf(1, 1, 0)
         quantise("wf10", parts=2)
-        cast_wf(1, 1, "work")
+        cast_wf(1, 1, 1, parts=2)
         quantise("wf11", parts=2)
         interleave_z(0, 1, "grouped_z01", on_scalar)
-        interleave_z(0, 0, "room2", on_vector)
-        cast_wm(1, "other_work")
-        quantise("z00")
-        sign_wm(1)
-        square_h(1, 0, "z_slots01")
+        interleave_z(0, 0, "room2", on_vector, 0, COLS // 2)
+        interleave_z(0, 0, "room2", on_vector, COLS // 2, COLS)
+        quantise("z00", parts=2)
+        for side in range(2):
+            cast_wm(1, last_wm[:, :, side * PIECE : (side + 1) * PIECE], side * PIECE)
+        sign_wm(1, parts=2)
+        square_h(1, 0, "z_slots01", (2, 3, 4, 5))
         interleave_z(1, 0, "room0", on_scalar, 0, SCALAR_COLUMNS)
-        square_h(1, 1, "z_slots11")
+        square_h(1, 1, "z_slots11", (1, 7, 0, 6))
         interleave_z(1, 0, "room0", on_vector, SCALAR_COLUMNS, COLS)
         quantise("wm1")
         interleave_z(1, 1, "grouped_z11", on_scalar)
@@ -309,9 +320,9 @@ def tile_list_factored_quadratic_scores_kernel(
         late = shared("late", "z_slots11", [P, len(late_lin) + 1, COLS], F32)
         for u in range(N_TILES - 1):
             finish(0, u, float_tile("result", 0, u))
-        quantise("z11", "lin_sq01")
+        quantise("z11")
         finish(0, N_TILES - 1, late[:, len(late_lin), :])
         for u in late_lin:
-            square_lin(1, u, late[:, u - EARLY_LIN, :])
+            square_lin(1, u, late[:, u - EARLY_LIN, :], u)
         for u in range(N_TILES):
             finish(1, u, float_tile("result", 1, u))

@@ -28,8 +28,7 @@ K_PASSES = K // PASS
 H_PASSES = H // PASS
 N_TILES = N // P
 LIST_COLS = COLS // 16
-EARLY_LIN = 2
-SCALAR_COLUMNS = 96
+SCALAR_COLUMNS = 288
 PIECE = PASS // 2
 LINE = 8
 
@@ -50,12 +49,6 @@ def tile_list_factored_quadratic_scores_kernel(
 
         def bank(number):
             return psum.tile([P, COLS], F32, name="acc", tag="bank%d" % number)
-
-        banks_opened = []
-
-        def next_bank():
-            banks_opened.append(len(banks_opened) % BANKS)
-            return bank(banks_opened[-1])
 
         def pass_order(half):
             return (0, 1) if half == 0 else (1, 0)
@@ -160,21 +153,33 @@ def tile_list_factored_quadratic_scores_kernel(
 
         lin_sq = {}
 
-        def square_lin(half, u, squared, number):
-            acc = bank(number)
+        def lin_passes(acc, half, u, columns):
             order = pass_order(half)
             for a in order:
                 nc.tensor.matmul_mx(
-                    out=acc[:],
+                    out=acc,
                     lhsT=wl_w[:, a, :].bitcast(U8)[:, 2 * u * P : 2 * (u + 1) * P].bitcast(FP4X4),
                     lhsT_scale=wl_sc[:, a, :].bitcast(U8)[:, u * P : (u + 1) * P],
-                    rhs=v_w[(a, half)][:].bitcast(FP8X4),
-                    rhs_scale=v_plane(a, half),
+                    rhs=v_w[(a, half)][:, columns].bitcast(FP8X4),
+                    rhs_scale=v_plane(a, half)[:, columns],
                     start=(a == order[0]),
                     stop=(a == order[1]),
                 )
+
+        def square_lin(u, squared):
+            acc = bank(u)
+            lin_passes(acc[:], 0, u, slice(0, COLS))
             nc.scalar.activation(squared, acc[:], ACT.Square)
-            lin_sq[(half, u)] = squared
+            lin_sq[(0, u)] = squared
+
+        def square_lin_quarter(side, pair, squared, number):
+            acc = bank(number)
+            for place in range(2):
+                lin_passes(acc[:, sides[place]], 1, 2 * pair + place, sides[side])
+                lin_sq[(1, side, 2 * pair + place)] = squared[:, sides[place]]
+            nc.scalar.activation(squared, acc[:], ACT.Square)
+
+        sides = (slice(0, PIECE), slice(PIECE, COLS))
 
         grouped = {}
         quantised = {}
@@ -249,22 +254,39 @@ def tile_list_factored_quadratic_scores_kernel(
             dst = grouped[key][:, PACK * first : PACK * last].rearrange("p (c i t) -> p c t i", i=LINE, t=PACK)
             copy(dst, z_slots[(b, half)][:, :, first:last].rearrange("p t (c i) -> p c t i", i=LINE))
 
-        def finish(half, u, result):
-            acc = bank(((4, 5, 1, 7), (0, 6, 4, 5))[half][u])
+        def y_pass(acc, half, u, b, columns, start, stop):
+            w_codes, w_scales = quantised["wm%d" % b]
+            z_codes, z_scales = quantised["z%d%d" % (b, half)]
+            nc.tensor.matmul_mx(
+                out=acc,
+                lhsT=w_codes[:, u * P : (u + 1) * P].bitcast(FP8X4),
+                lhsT_scale=w_scales[:, u * P : (u + 1) * P],
+                rhs=z_codes[:, columns].bitcast(FP8X4),
+                rhs_scale=z_scales[:, columns],
+                start=start,
+                stop=stop,
+            )
+
+        def combine(result, squared, u, acc, first):
+            nc.vector.scalar_tensor_tensor(result, squared, bias[:, u : u + 1], acc, ALU.add, ALU.subtract)
+            nc.sync.dma_start(out[u * P : (u + 1) * P, first : first + result.shape[1]], result)
+
+        def finish(u, result):
+            acc = bank((4, 5, 1, 7)[u])
             for b in range(H_PASSES):
-                w_codes, w_scales = quantised["wm%d" % b]
-                z_codes, z_scales = quantised["z%d%d" % (b, half)]
-                nc.tensor.matmul_mx(
-                    out=acc[:],
-                    lhsT=w_codes[:, u * P : (u + 1) * P].bitcast(FP8X4),
-                    lhsT_scale=w_scales[:, u * P : (u + 1) * P],
-                    rhs=z_codes[:].bitcast(FP8X4),
-                    rhs_scale=z_scales[:],
-                    start=(b == 0),
-                    stop=(b == H_PASSES - 1),
-                )
-            nc.vector.scalar_tensor_tensor(result, lin_sq[(half, u)], bias[:, u : u + 1], acc[:], ALU.add, ALU.subtract)
-            nc.sync.dma_start(out[u * P : (u + 1) * P, half * COLS : (half + 1) * COLS], result)
+                y_pass(acc[:], 0, u, b, slice(0, COLS), b == 0, b == H_PASSES - 1)
+            combine(result, lin_sq[(0, u)], u, acc[:], 0)
+
+        def finish_quarter(side, pair, number):
+            acc = bank(number)
+            for b in range(H_PASSES):
+                for place in range(2):
+                    first, last = (b, place) == (0, 0), (b, place) == (H_PASSES - 1, 1)
+                    y_pass(acc[:, sides[place]], 1, 2 * pair + place, b, sides[side], first, last)
+            for place in range(2):
+                u = 2 * pair + place
+                result = held("result1%d%d" % (side, u), [P, PIECE], F32)
+                combine(result[:], lin_sq[(1, side, u)], u, acc[:, sides[place]], COLS + side * PIECE)
 
         def float_tile(name, half, u):
             return held("%s%d%d" % (name, half, u), [P, COLS], F32)[:]
@@ -272,11 +294,11 @@ def tile_list_factored_quadratic_scores_kernel(
         on_vector, on_scalar = nc.vector.tensor_copy, nc.scalar.copy
 
         cast_wf(0, 0, 0, on_scalar)
-        early = shared("early_lin", "early", [P, N_TILES + EARLY_LIN, COLS], F32)
+        early = shared("early_lin", "early", [P, N_TILES + 2, COLS], F32)
         for u in range(N_TILES):
-            square_lin(0, u, early[:, u, :], u)
-        for u in range(EARLY_LIN):
-            square_lin(1, u, early[:, N_TILES + u, :], N_TILES + u)
+            square_lin(u, early[:, u, :])
+        for pair in range(2):
+            square_lin_quarter(0, pair, early[:, N_TILES + pair, :], N_TILES + pair)
         cast_wf(0, 0, 1)
         quantise("wf00", parts=2)
         cast_wf(0, 1, 0)
@@ -313,16 +335,19 @@ def tile_list_factored_quadratic_scores_kernel(
         square_h(1, 1, "z_slots11", (1, 7, 0, 6))
         interleave_z(1, 0, "room0", on_vector, SCALAR_COLUMNS, COLS)
         quantise("wm1")
-        interleave_z(1, 1, "grouped_z11", on_scalar)
+        interleave_z(1, 1, "grouped_z11", on_scalar, 0, PIECE)
+        interleave_z(1, 1, "grouped_z11", on_scalar, PIECE, COLS)
         quantise("z10")
         quantise("z01", "z_slots01")
-        late_lin = range(EARLY_LIN, N_TILES)
-        late = shared("late", "z_slots11", [P, len(late_lin) + 1, COLS], F32)
+        late = shared("late", "z_slots11", [P, 2, COLS], F32)
         for u in range(N_TILES - 1):
-            finish(0, u, float_tile("result", 0, u))
-        quantise("z11")
-        finish(0, N_TILES - 1, late[:, len(late_lin), :])
-        for u in late_lin:
-            square_lin(1, u, late[:, u - EARLY_LIN, :], u)
-        for u in range(N_TILES):
-            finish(1, u, float_tile("result", 1, u))
+            finish(u, float_tile("result", 0, u))
+        quantise("z11", parts=2, only=0)
+        finish(N_TILES - 1, float_tile("result", 0, N_TILES - 1))
+        finish_quarter(0, 0, 0)
+        quantise("z11", parts=2, only=1)
+        finish_quarter(0, 1, 6)
+        for pair in range(2):
+            square_lin_quarter(1, pair, late[:, pair, :], 2 + pair)
+        for pair in range(2):
+            finish_quarter(1, pair, 4 + pair)

@@ -28,7 +28,7 @@ K_PASSES = K // PASS
 H_PASSES = H // PASS
 N_TILES = N // P
 LIST_COLS = COLS // 16
-SCALAR_COLUMNS = 288
+SCALAR_COLUMNS = 256
 PIECE = PASS // 2
 LINE = 8
 
@@ -151,9 +151,17 @@ def tile_list_factored_quadratic_scores_kernel(
             plane = v_sc[:] if a == 0 else v_sc_second[:].bitcast(U8)
             return plane[:, half * COLS : (half + 1) * COLS]
 
+        spans = (slice(0, COLS), slice(COLS, COLS + PIECE), slice(COLS + PIECE, S))
+        sides = (slice(0, PIECE), slice(PIECE, COLS))
+
+        def within_half(span):
+            half = spans[span].start // COLS
+            return half, slice(spans[span].start - half * COLS, spans[span].stop - half * COLS)
+
         lin_sq = {}
 
-        def lin_passes(acc, half, u, columns):
+        def lin_passes(acc, span, u):
+            half, columns = within_half(span)
             order = pass_order(half)
             for a in order:
                 nc.tensor.matmul_mx(
@@ -168,29 +176,28 @@ def tile_list_factored_quadratic_scores_kernel(
 
         def square_lin(u, squared):
             acc = bank(u)
-            lin_passes(acc[:], 0, u, slice(0, COLS))
+            lin_passes(acc[:], 0, u)
             nc.scalar.activation(squared, acc[:], ACT.Square)
             lin_sq[(0, u)] = squared
 
-        def square_lin_quarter(side, pair, squared, number):
+        def square_lin_pair(span, pair, squared, number):
             acc = bank(number)
             for place in range(2):
-                lin_passes(acc[:, sides[place]], 1, 2 * pair + place, sides[side])
-                lin_sq[(1, side, 2 * pair + place)] = squared[:, sides[place]]
+                lin_passes(acc[:, sides[place]], span, 2 * pair + place)
+                lin_sq[(span, 2 * pair + place)] = squared[:, sides[place]]
             nc.scalar.activation(squared, acc[:], ACT.Square)
-
-        sides = (slice(0, PIECE), slice(PIECE, COLS))
 
         grouped = {}
         quantised = {}
 
-        def quantise(key, tag=None, parts=1, only=None):
+        def quantise(key, parts=1, only=None, codes=None):
+            columns = grouped[key].shape[1] // PACK
             if key not in quantised:
-                codes = shared("codes_" + key, tag or "codes_" + key, [P, COLS], U32)
-                scales = held("scales_" + key, [P, COLS], U8)
-                quantised[key] = (codes, scales)
+                if codes is None:
+                    codes = held("codes_" + key, [P, columns], U32)
+                quantised[key] = (codes, held("scales_" + key, [P, columns], U8))
             codes, scales = quantised[key]
-            width = COLS // parts
+            width = columns // parts
             for part in range(parts) if only is None else [only]:
                 words = slice(part * width, (part + 1) * width)
                 nc.vector.quantize_mx(
@@ -202,34 +209,37 @@ def tile_list_factored_quadratic_scores_kernel(
         def cast_wf(b, a, side, copy=nc.vector.tensor_copy, parts=1):
             key = "wf%d%d" % (b, a)
             if key not in grouped:
-                grouped[key] = held("grouped_" + key, [P, PASS * PACK], BF16)
-            dst = grouped[key][:].rearrange("p (t s u i j) -> p s u j i t", t=PACK, s=2, i=2, j=PACK)
+                grouped[key] = shared("grouped_" + key, "grouped_" + key, [P, PASS * PACK], BF16)[:]
+            dst = grouped[key].rearrange("p (t s u i j) -> p s u j i t", t=PACK, s=2, i=2, j=PACK)
             src = wf_raw[(b, a, side)].rearrange("p j (u i t) -> p u j i t", i=2, t=PACK)
             width = PACK // parts
             for part in range(parts):
                 slots = slice(part * width, (part + 1) * width)
                 copy(dst[:, side, :, :, :, slots], src[:, :, :, :, slots])
 
-        def cast_wm(b, raw, first):
+        def cast_wm(b, side):
             key = "wm%d" % b
             if key not in grouped:
-                grouped[key] = held("grouped_" + key, [P, N * PACK], BF16)
-            src = raw.rearrange("p j (c i) -> p c j i", i=4)
-            dst = grouped[key][:].rearrange("p (c i j) -> p c j i", i=4, j=PACK)
-            nc.vector.tensor_copy(dst[:, first // 4 : first // 4 + src.shape[1]], src)
+                grouped[key] = shared("grouped_" + key, "grouped_" + key, [P, N * PACK], BF16)[:]
+            dst = grouped[key].rearrange("p (s c i j) -> p s c j i", s=2, i=4, j=PACK)
+            nc.vector.tensor_copy(dst[:, side], wm_raw[(b, side)].rearrange("p j (c i) -> p c j i", i=4))
 
-        def sign_wm(b, parts=1):
-            rounded = grouped["wm%d" % b][:].rearrange("p (c j) -> p c j", j=PACK)
-            width = N // parts
-            signs = sign[:, b, :].unsqueeze(1).broadcast_to([P, width, PACK])
-            for part in range(parts):
-                piece = rounded[:, part * width : (part + 1) * width, :]
-                nc.vector.tensor_tensor(piece, piece, signs, ALU.mult)
+        def sign_wm(b, side):
+            rounded = grouped["wm%d" % b].rearrange("p (s c j) -> p s c j", s=2, j=PACK)[:, side]
+            signs = sign[:, b, :].unsqueeze(1).broadcast_to([P, PIECE, PACK])
+            nc.vector.tensor_tensor(rounded, rounded, signs, ALU.mult)
 
         z_slots = {}
 
-        def square_h(b, half, tag, banks):
+        def square_h(b, half, tag, banks, cut=COLS):
             squares = shared("z_slots%d%d" % (b, half), tag, [P, PACK, COLS], BF16)
+            sums = []
+
+            def square(slot, columns):
+                nc.scalar.activation(
+                    squares[:, slot, columns], sums[slot][:, columns], ACT.Square, scale=root[:, slot, b : b + 1]
+                )
+
             for slot in range(PACK):
                 acc = bank(banks[slot])
                 order = pass_order(half)
@@ -244,52 +254,61 @@ def tile_list_factored_quadratic_scores_kernel(
                         start=(a == order[0]),
                         stop=(a == order[1]),
                     )
-                nc.scalar.activation(squares[:, slot, :], acc[:], ACT.Square, scale=root[:, slot, b : b + 1])
+                sums.append(acc)
+                square(slot, slice(0, COLS if slot < 2 else cut))
+            if cut < COLS:
+                for slot in (2, 3):
+                    square(slot, slice(cut, COLS))
             z_slots[(b, half)] = squares
 
-        def interleave_z(b, half, tag, copy, first=0, last=COLS):
-            key = "z%d%d" % (b, half)
-            if key not in grouped:
-                grouped[key] = shared("grouped_" + key, tag, [P, COLS * PACK], BF16)
-            dst = grouped[key][:, PACK * first : PACK * last].rearrange("p (c i t) -> p c t i", i=LINE, t=PACK)
-            copy(dst, z_slots[(b, half)][:, :, first:last].rearrange("p t (c i) -> p c t i", i=LINE))
+        def z_room(b, span, tag):
+            width = spans[span].stop - spans[span].start
+            grouped["z%d%d" % (b, span)] = shared("grouped_z%d%d" % (b, span), tag, [P, width * PACK], BF16)[:]
 
-        def y_pass(acc, half, u, b, columns, start, stop):
+        def interleave_z(b, span, copy, first, last):
+            half, columns = within_half(span)
+            dst = grouped["z%d%d" % (b, span)][:, PACK * first : PACK * last]
+            src = z_slots[(b, half)][:, :, columns.start + first : columns.start + last]
+            copy(
+                dst.rearrange("p (c i t) -> p c t i", i=LINE, t=PACK),
+                src.rearrange("p t (c i) -> p c t i", i=LINE),
+            )
+
+        def y_pass(acc, span, u, b, start, stop):
             w_codes, w_scales = quantised["wm%d" % b]
-            z_codes, z_scales = quantised["z%d%d" % (b, half)]
+            z_codes, z_scales = quantised["z%d%d" % (b, span)]
             nc.tensor.matmul_mx(
                 out=acc,
                 lhsT=w_codes[:, u * P : (u + 1) * P].bitcast(FP8X4),
                 lhsT_scale=w_scales[:, u * P : (u + 1) * P],
-                rhs=z_codes[:, columns].bitcast(FP8X4),
-                rhs_scale=z_scales[:, columns],
+                rhs=z_codes[:].bitcast(FP8X4),
+                rhs_scale=z_scales[:],
                 start=start,
                 stop=stop,
             )
 
-        def combine(result, squared, u, acc, first):
-            nc.vector.scalar_tensor_tensor(result, squared, bias[:, u : u + 1], acc, ALU.add, ALU.subtract)
-            nc.sync.dma_start(out[u * P : (u + 1) * P, first : first + result.shape[1]], result)
+        def combine(span, u, acc):
+            result = held("result%d%d" % (span, u), [P, acc.shape[1]], F32)
+            nc.vector.scalar_tensor_tensor(
+                result[:], lin_sq[(span, u)], bias[:, u : u + 1], acc, ALU.add, ALU.subtract
+            )
+            nc.sync.dma_start(out[u * P : (u + 1) * P, spans[span]], result[:])
 
-        def finish(u, result):
-            acc = bank((4, 5, 1, 7)[u])
-            for b in range(H_PASSES):
-                y_pass(acc[:], 0, u, b, slice(0, COLS), b == 0, b == H_PASSES - 1)
-            combine(result, lin_sq[(0, u)], u, acc[:], 0)
+        def finish(u, number):
+            acc = bank(number)
+            order = (0, 1) if u < 2 else (1, 0)
+            for b in order:
+                y_pass(acc[:], 0, u, b, b == order[0], b == order[1])
+            combine(0, u, acc[:])
 
-        def finish_quarter(side, pair, number):
+        def finish_pair(span, pair, number):
             acc = bank(number)
             for b in range(H_PASSES):
                 for place in range(2):
                     first, last = (b, place) == (0, 0), (b, place) == (H_PASSES - 1, 1)
-                    y_pass(acc[:, sides[place]], 1, 2 * pair + place, b, sides[side], first, last)
+                    y_pass(acc[:, sides[place]], span, 2 * pair + place, b, first, last)
             for place in range(2):
-                u = 2 * pair + place
-                result = held("result1%d%d" % (side, u), [P, PIECE], F32)
-                combine(result[:], lin_sq[(1, side, u)], u, acc[:, sides[place]], COLS + side * PIECE)
-
-        def float_tile(name, half, u):
-            return held("%s%d%d" % (name, half, u), [P, COLS], F32)[:]
+                combine(span, 2 * pair + place, acc[:, sides[place]])
 
         on_vector, on_scalar = nc.vector.tensor_copy, nc.scalar.copy
 
@@ -298,7 +317,7 @@ def tile_list_factored_quadratic_scores_kernel(
         for u in range(N_TILES):
             square_lin(u, early[:, u, :])
         for pair in range(2):
-            square_lin_quarter(0, pair, early[:, N_TILES + pair, :], N_TILES + pair)
+            square_lin_pair(1, pair, early[:, N_TILES + pair, :], N_TILES + pair)
         cast_wf(0, 0, 1)
         quantise("wf00", parts=2)
         cast_wf(0, 1, 0)
@@ -310,9 +329,11 @@ def tile_list_factored_quadratic_scores_kernel(
         square_h(0, 0, "z_slots00", (6, 7, 0, 1))
         square_h(0, 1, "z_slots01", (6, 7, 0, 6))
         for side in range(2):
-            cast_wm(0, wm_raw[(0, side)], side * PIECE)
+            cast_wm(0, side)
         last_wm = load_rows(wm[PASS:, :], shared("wm_last", "room0", [P, PACK * N], F32)[:])
-        sign_wm(0, parts=2)
+        for side in range(2):
+            wm_raw[(1, side)] = last_wm[:, :, sides[side]]
+            sign_wm(0, side)
         quantise("wm0", parts=2)
         cast_wf(1, 0, 0)
         cast_wf(1, 0, 1)
@@ -323,31 +344,46 @@ def tile_list_factored_quadratic_scores_kernel(
         quantise("wf10", parts=2)
         cast_wf(1, 1, 1, parts=2)
         quantise("wf11", parts=2)
-        interleave_z(0, 1, "grouped_z01", on_scalar)
-        interleave_z(0, 0, "room2", on_vector, 0, COLS // 2)
-        interleave_z(0, 0, "room2", on_vector, COLS // 2, COLS)
-        quantise("z00", parts=2)
+        z_room(0, 0, "grouped_z00")
+        interleave_z(0, 0, on_scalar, 0, COLS)
+        quantise("z00", codes=shared("codes_z00", "room2", [P, COLS], U32))
+        z_room(0, 1, "grouped_wf11")
+        interleave_z(0, 1, on_vector, 0, PIECE)
         for side in range(2):
-            cast_wm(1, last_wm[:, :, side * PIECE : (side + 1) * PIECE], side * PIECE)
-        sign_wm(1, parts=2)
-        square_h(1, 0, "z_slots01", (2, 3, 4, 5))
-        interleave_z(1, 0, "room0", on_scalar, 0, SCALAR_COLUMNS)
+            cast_wm(1, side)
+        for side in range(2):
+            sign_wm(1, side)
+        square_h(1, 0, "z_slots00", (2, 3, 4, 5), SCALAR_COLUMNS)
+        z_room(1, 0, "grouped_z10")
+        interleave_z(1, 0, on_scalar, 0, SCALAR_COLUMNS)
         square_h(1, 1, "z_slots11", (1, 7, 0, 6))
-        interleave_z(1, 0, "room0", on_vector, SCALAR_COLUMNS, COLS)
-        quantise("wm1")
-        interleave_z(1, 1, "grouped_z11", on_scalar, 0, PIECE)
-        interleave_z(1, 1, "grouped_z11", on_scalar, PIECE, COLS)
+        interleave_z(1, 0, on_vector, SCALAR_COLUMNS, COLS)
+        quantise("wm1", parts=2, only=0)
+        for span in (1, 2):
+            z_room(1, span, "grouped_z1%d" % span)
+            interleave_z(1, span, on_scalar, 0, PIECE)
         quantise("z10")
-        quantise("z01", "z_slots01")
-        late = shared("late", "z_slots11", [P, 2, COLS], F32)
+        quantise("z01", codes=shared("codes_z01", "z_slots00", [P, PIECE], U32))
+        quantise("wm1", parts=2, only=1)
+        z_room(0, 2, "grouped_wm1")
+        nc.gpsimd.tensor_scalar(
+            grouped["z02"].rearrange("p (c t) -> p c t", t=PACK),
+            z_slots[(0, 1)][:, :, PIECE:].rearrange("p t c -> p c t"),
+            1.0,
+            0.0,
+            ALU.mult,
+            ALU.add,
+        )
         for u in range(N_TILES - 1):
-            finish(u, float_tile("result", 0, u))
-        quantise("z11", parts=2, only=0)
-        finish(N_TILES - 1, float_tile("result", 0, N_TILES - 1))
-        finish_quarter(0, 0, 0)
-        quantise("z11", parts=2, only=1)
-        finish_quarter(0, 1, 6)
+            finish(u, (4, 5, 1, 7)[u])
+        quantise("z11")
+        finish(N_TILES - 1, 7)
+        finish_pair(1, 0, 0)
+        quantise("z02")
+        quantise("z12")
+        finish_pair(1, 1, 6)
+        late = shared("late", "z_slots11", [P, 2, COLS], F32)
         for pair in range(2):
-            square_lin_quarter(1, pair, late[:, pair, :], 2 + pair)
+            square_lin_pair(2, pair, late[:, pair, :], 2 + pair)
         for pair in range(2):
-            finish_quarter(1, pair, 4 + pair)
+            finish_pair(2, pair, 4 + pair)

@@ -28,7 +28,8 @@ K_PASSES = K // PASS
 H_PASSES = H // PASS
 N_TILES = N // P
 LIST_COLS = COLS // 16
-SCALAR_COLUMNS = 256
+SCALAR_COLUMNS = 224
+GPSIMD_COLUMNS = 144
 PIECE = PASS // 2
 LINE = 8
 
@@ -76,6 +77,8 @@ def tile_list_factored_quadratic_scores_kernel(
         nc.gpsimd.memset(wl_sc[:], 0)
         gain_slots = held("gain_slots", [P, PACK, P], F32)
         nc.gpsimd.memset(gain_slots[:], 0.0)
+        sign_rows = held("sign_rows", [P, PASS], BF16)
+        nc.gpsimd.memset(sign_rows[:], 0.0)
         v_sc_second = held("v_sc_second", [P, S // 4], I32)
         nc.gpsimd.memset(v_sc_second[:], 0)
         identity = held("identity", [P, P], F32)
@@ -114,10 +117,13 @@ def tile_list_factored_quadratic_scores_kernel(
             nc.tensor.transpose(gain_columns[:, slot, :], gain_slots[:, slot, :], identity[:])
         magnitude = held("magnitude", [P, PACK, H_PASSES], F32)
         root = held("root", [P, PACK, H_PASSES], F32)
-        sign = held("sign", [P, H_PASSES, PACK], BF16)
         nc.scalar.activation(magnitude[:], gain_columns[:, :, 0:H_PASSES], ACT.Abs)
         nc.scalar.activation(root[:], magnitude[:], ACT.Sqrt)
-        nc.scalar.activation(sign[:].rearrange("p b t -> p t b"), gain_columns[:, :, 0:H_PASSES], ACT.Sign)
+        nc.scalar.activation(sign_rows[0:H_PASSES, :], gain_rows[:], ACT.Sign)
+        sign_words = psum.tile([P, P, 2], F32, name="sign_words", tag="bank6")
+        for e in range(2):
+            nc.tensor.transpose(sign_words[:, :, e], sign_rows[:].bitcast(F32)[:, e::2], identity[:])
+        sign = sign_words[:].rearrange("p b e -> p (b e)").bitcast(BF16).rearrange("p (b t) -> p b t", t=PACK)
 
         wm_raw = {}
 
@@ -274,6 +280,17 @@ def tile_list_factored_quadratic_scores_kernel(
                 src.rearrange("p t (c i) -> p c t i", i=LINE),
             )
 
+        def interleave_on_gpsimd(span, last):
+            half, columns = within_half(span)
+            nc.gpsimd.tensor_scalar(
+                grouped["z0%d" % span][:, 0 : PACK * last].rearrange("p (c t) -> p c t", t=PACK),
+                z_slots[(0, half)][:, :, columns.start : columns.start + last].rearrange("p t c -> p c t"),
+                1.0,
+                0.0,
+                ALU.mult,
+                ALU.add,
+            )
+
         def y_pass(acc, span, u, b, start, stop):
             w_codes, w_scales = quantised["wm%d" % b]
             z_codes, z_scales = quantised["z%d%d" % (b, span)]
@@ -326,13 +343,13 @@ def tile_list_factored_quadratic_scores_kernel(
         for side in range(2):
             load_wf(1, 1, side, room[:, side, :])
         quantise("wf01", parts=2)
-        square_h(0, 0, "z_slots00", (6, 7, 0, 1))
-        square_h(0, 1, "z_slots01", (6, 7, 0, 6))
+        square_h(0, 0, "z_slots00", (7, 0, 1, 2))
+        square_h(0, 1, "z_slots01", (7, 0, 1, 7))
         for side in range(2):
             cast_wm(0, side)
-        last_wm = load_rows(wm[PASS:, :], shared("wm_last", "room0", [P, PACK * N], F32)[:])
+        room = pieces("wm_last", "room0", 2)
         for side in range(2):
-            wm_raw[(1, side)] = last_wm[:, :, sides[side]]
+            wm_raw[(1, side)] = load_rows(wm[PASS:, sides[side]], room[:, side, :])
             sign_wm(0, side)
         quantise("wm0", parts=2)
         cast_wf(1, 0, 0)
@@ -346,17 +363,18 @@ def tile_list_factored_quadratic_scores_kernel(
         quantise("wf11", parts=2)
         z_room(0, 0, "grouped_z00")
         interleave_z(0, 0, on_scalar, 0, COLS)
+        cast_wm(1, 0)
         quantise("z00", codes=shared("codes_z00", "room2", [P, COLS], U32))
-        z_room(0, 1, "grouped_wf11")
-        interleave_z(0, 1, on_vector, 0, PIECE)
-        for side in range(2):
-            cast_wm(1, side)
+        cast_wm(1, 1)
+        z_room(0, 1, "room0")
+        interleave_on_gpsimd(1, GPSIMD_COLUMNS)
         for side in range(2):
             sign_wm(1, side)
         square_h(1, 0, "z_slots00", (2, 3, 4, 5), SCALAR_COLUMNS)
         z_room(1, 0, "grouped_z10")
         interleave_z(1, 0, on_scalar, 0, SCALAR_COLUMNS)
         square_h(1, 1, "z_slots11", (1, 7, 0, 6))
+        interleave_z(0, 1, on_vector, GPSIMD_COLUMNS, PIECE)
         interleave_z(1, 0, on_vector, SCALAR_COLUMNS, COLS)
         quantise("wm1", parts=2, only=0)
         for span in (1, 2):
@@ -366,14 +384,7 @@ def tile_list_factored_quadratic_scores_kernel(
         quantise("z01", codes=shared("codes_z01", "z_slots00", [P, PIECE], U32))
         quantise("wm1", parts=2, only=1)
         z_room(0, 2, "grouped_wm1")
-        nc.gpsimd.tensor_scalar(
-            grouped["z02"].rearrange("p (c t) -> p c t", t=PACK),
-            z_slots[(0, 1)][:, :, PIECE:].rearrange("p t c -> p c t"),
-            1.0,
-            0.0,
-            ALU.mult,
-            ALU.add,
-        )
+        interleave_on_gpsimd(2, PIECE)
         for u in range(N_TILES - 1):
             finish(u, (4, 5, 1, 7)[u])
         quantise("z11")

@@ -28,8 +28,9 @@ K_PASSES = K // PASS
 H_PASSES = H // PASS
 N_TILES = N // P
 LIST_COLS = COLS // 16
-SCALAR_COLUMNS = 224
-GPSIMD_COLUMNS = 144
+SCALAR_COLUMNS = 160
+GPSIMD_COLUMNS = 384
+THIRD_COLUMNS = 160
 PIECE = PASS // 2
 LINE = 8
 
@@ -40,6 +41,7 @@ def tile_list_factored_quadratic_scores_kernel(
     nc = tc.nc
     with ExitStack() as ctx:
         keep = ctx.enter_context(tc.tile_pool(name="keep", bufs=1))
+        reused = ctx.enter_context(tc.tile_pool(name="reused", bufs=1))
         psum = ctx.enter_context(tc.psum_pool(name="psum", bufs=1))
 
         def held(name, shape, dtype):
@@ -196,21 +198,17 @@ def tile_list_factored_quadratic_scores_kernel(
         grouped = {}
         quantised = {}
 
-        def quantise(key, parts=1, only=None, codes=None):
-            columns = grouped[key].shape[1] // PACK
+        def quantise_columns(key, source, first, tag=None):
             if key not in quantised:
-                if codes is None:
-                    codes = held("codes_" + key, [P, columns], U32)
-                quantised[key] = (codes, held("scales_" + key, [P, columns], U8))
+                codes = shared("codes_" + key, tag or "codes_" + key, [P, COLS], U32)
+                quantised[key] = (codes, held("scales_" + key, [P, COLS], U8))
             codes, scales = quantised[key]
-            width = columns // parts
-            for part in range(parts) if only is None else [only]:
-                words = slice(part * width, (part + 1) * width)
-                nc.vector.quantize_mx(
-                    out=codes[:, words].bitcast(FP8X4),
-                    scales=scales[:, words],
-                    in_=grouped[key][:, PACK * part * width : PACK * (part + 1) * width],
-                )
+            words = slice(first, first + source.shape[1] // PACK)
+            nc.vector.quantize_mx(out=codes[:, words].bitcast(FP8X4), scales=scales[:, words], in_=source)
+
+        def quantise(key, *parts):
+            for side in parts:
+                quantise_columns(key, grouped[key][:, PACK * PIECE * side : PACK * PIECE * (side + 1)], PIECE * side)
 
         def cast_wf(b, a, side, copy=nc.vector.tensor_copy, parts=1):
             key = "wf%d%d" % (b, a)
@@ -229,6 +227,15 @@ def tile_list_factored_quadratic_scores_kernel(
                 grouped[key] = shared("grouped_" + key, "grouped_" + key, [P, N * PACK], BF16)[:]
             dst = grouped[key].rearrange("p (s c i j) -> p s c j i", s=2, i=4, j=PACK)
             nc.vector.tensor_copy(dst[:, side], wm_raw[(b, side)].rearrange("p j (c i) -> p c j i", i=4))
+
+        def cast_and_sign_wm(b, side):
+            key = "wm%d" % b
+            if key not in grouped:
+                grouped[key] = held("grouped_" + key, [P, N * PACK], BF16)[:]
+            dst = grouped[key].rearrange("p (s c i j) -> p s c j i", s=2, i=4, j=PACK)
+            signs = sign[:, b, :].unsqueeze(1).unsqueeze(3).broadcast_to([P, PIECE // 4, PACK, 4])
+            src = wm_raw[(b, side)].rearrange("p j (c i) -> p c j i", i=4)
+            nc.vector.tensor_tensor(dst[:, side], src, signs, ALU.mult)
 
         def sign_wm(b, side):
             rounded = grouped["wm%d" % b].rearrange("p (s c j) -> p s c j", s=2, j=PACK)[:, side]
@@ -267,24 +274,22 @@ def tile_list_factored_quadratic_scores_kernel(
                     square(slot, slice(cut, COLS))
             z_slots[(b, half)] = squares
 
-        def z_room(b, span, tag):
-            width = spans[span].stop - spans[span].start
-            grouped["z%d%d" % (b, span)] = shared("grouped_z%d%d" % (b, span), tag, [P, width * PACK], BF16)[:]
+        def z_room(name, tag, columns):
+            return shared(name, tag, [P, columns * PACK], BF16)
 
-        def interleave_z(b, span, copy, first, last):
-            half, columns = within_half(span)
-            dst = grouped["z%d%d" % (b, span)][:, PACK * first : PACK * last]
-            src = z_slots[(b, half)][:, :, columns.start + first : columns.start + last]
+        def placed(name, columns, start):
+            return reused.tile([P, columns * PACK], BF16, name=name, offset=start * PACK * 2, align_bytes=64)
+
+        def interleave_z(copy, room, b, half, first, last, start=0):
             copy(
-                dst.rearrange("p (c i t) -> p c t i", i=LINE, t=PACK),
-                src.rearrange("p t (c i) -> p c t i", i=LINE),
+                room[:, PACK * (first - start) : PACK * (last - start)].rearrange("p (c i t) -> p c t i", i=LINE, t=PACK),
+                z_slots[(b, half)][:, :, first:last].rearrange("p t (c i) -> p c t i", i=LINE),
             )
 
-        def interleave_on_gpsimd(span, last):
-            half, columns = within_half(span)
+        def interleave_on_gpsimd(room, b, first, last, start=0):
             nc.gpsimd.tensor_scalar(
-                grouped["z0%d" % span][:, 0 : PACK * last].rearrange("p (c t) -> p c t", t=PACK),
-                z_slots[(0, half)][:, :, columns.start : columns.start + last].rearrange("p t c -> p c t"),
+                room[:, PACK * (first - start) : PACK * (last - start)].rearrange("p (c t) -> p c t", t=PACK),
+                z_slots[(b, 1)][:, :, first:last].rearrange("p t c -> p c t"),
                 1.0,
                 0.0,
                 ALU.mult,
@@ -292,40 +297,39 @@ def tile_list_factored_quadratic_scores_kernel(
             )
 
         def y_pass(acc, span, u, b, start, stop):
+            half, columns = within_half(span)
             w_codes, w_scales = quantised["wm%d" % b]
-            z_codes, z_scales = quantised["z%d%d" % (b, span)]
+            z_codes, z_scales = quantised["z%d%d" % (b, half)]
             nc.tensor.matmul_mx(
                 out=acc,
                 lhsT=w_codes[:, u * P : (u + 1) * P].bitcast(FP8X4),
                 lhsT_scale=w_scales[:, u * P : (u + 1) * P],
-                rhs=z_codes[:].bitcast(FP8X4),
-                rhs_scale=z_scales[:],
+                rhs=z_codes[:, columns].bitcast(FP8X4),
+                rhs_scale=z_scales[:, columns],
                 start=start,
                 stop=stop,
             )
 
-        def combine(span, u, acc):
-            result = held("result%d%d" % (span, u), [P, acc.shape[1]], F32)
-            nc.vector.scalar_tensor_tensor(
-                result[:], lin_sq[(span, u)], bias[:, u : u + 1], acc, ALU.add, ALU.subtract
-            )
-            nc.sync.dma_start(out[u * P : (u + 1) * P, spans[span]], result[:])
+        def combine(span, u, acc, result):
+            nc.vector.scalar_tensor_tensor(result, lin_sq[(span, u)], bias[:, u : u + 1], acc, ALU.add, ALU.subtract)
+            nc.sync.dma_start(out[u * P : (u + 1) * P, spans[span]], result)
 
         def finish(u, number):
             acc = bank(number)
             order = (0, 1) if u < 2 else (1, 0)
             for b in order:
                 y_pass(acc[:], 0, u, b, b == order[0], b == order[1])
-            combine(0, u, acc[:])
+            combine(0, u, acc[:], held("result%d" % u, [P, COLS], F32)[:])
 
-        def finish_pair(span, pair, number):
+        def finish_pair(span, pair, number, results):
             acc = bank(number)
-            for b in range(H_PASSES):
+            order = (0, 1) if span == 1 else (1, 0)
+            for b in order:
                 for place in range(2):
-                    first, last = (b, place) == (0, 0), (b, place) == (H_PASSES - 1, 1)
+                    first, last = (b, place) == (order[0], 0), (b, place) == (order[1], 1)
                     y_pass(acc[:, sides[place]], span, 2 * pair + place, b, first, last)
             for place in range(2):
-                combine(span, 2 * pair + place, acc[:, sides[place]])
+                combine(span, 2 * pair + place, acc[:, sides[place]], results[:, sides[place]])
 
         on_vector, on_scalar = nc.vector.tensor_copy, nc.scalar.copy
 
@@ -336,13 +340,13 @@ def tile_list_factored_quadratic_scores_kernel(
         for pair in range(2):
             square_lin_pair(1, pair, early[:, N_TILES + pair, :], N_TILES + pair)
         cast_wf(0, 0, 1)
-        quantise("wf00", parts=2)
+        quantise("wf00", 0, 1)
         cast_wf(0, 1, 0)
         cast_wf(0, 1, 1, parts=2)
         room = pieces("wf_last", "room2", 2)
         for side in range(2):
             load_wf(1, 1, side, room[:, side, :])
-        quantise("wf01", parts=2)
+        quantise("wf01", 0, 1)
         square_h(0, 0, "z_slots00", (7, 0, 1, 2))
         square_h(0, 1, "z_slots01", (7, 0, 1, 7))
         for side in range(2):
@@ -351,50 +355,52 @@ def tile_list_factored_quadratic_scores_kernel(
         for side in range(2):
             wm_raw[(1, side)] = load_rows(wm[PASS:, sides[side]], room[:, side, :])
             sign_wm(0, side)
-        quantise("wm0", parts=2)
+        quantise("wm0", 0, 1)
         cast_wf(1, 0, 0)
         cast_wf(1, 0, 1)
         bias = shared("bias", "room1", [P, N_TILES], F32)
         with nc.allow_non_contiguous_dma(reason="one bias value a partition"):
             nc.sync.dma_start(bias[:], b0.rearrange("(u p) -> p u", p=P))
+        grouped["wf11"] = placed("grouped_wf11", COLS, 0)[:]
         cast_wf(1, 1, 0)
-        quantise("wf10", parts=2)
+        quantise("wf10", 0, 1)
         cast_wf(1, 1, 1, parts=2)
-        quantise("wf11", parts=2)
-        z_room(0, 0, "grouped_z00")
-        interleave_z(0, 0, on_scalar, 0, COLS)
-        cast_wm(1, 0)
-        quantise("z00", codes=shared("codes_z00", "room2", [P, COLS], U32))
-        cast_wm(1, 1)
-        z_room(0, 1, "room0")
-        interleave_on_gpsimd(1, GPSIMD_COLUMNS)
+        quantise("wf11", 0, 1)
+        z00 = z_room("z00", "z00", COLS)
+        interleave_z(on_scalar, z00, 0, 0, 0, COLS)
+        z01 = placed("z01", GPSIMD_COLUMNS, 0)
+        interleave_on_gpsimd(z01, 0, 0, GPSIMD_COLUMNS)
         for side in range(2):
-            sign_wm(1, side)
+            cast_and_sign_wm(1, side)
+        quantise("wm1", 0)
+        quantise_columns("z00", z00[:], 0, "room0")
         square_h(1, 0, "z_slots00", (2, 3, 4, 5), SCALAR_COLUMNS)
-        z_room(1, 0, "grouped_z10")
-        interleave_z(1, 0, on_scalar, 0, SCALAR_COLUMNS)
+        z10 = z_room("z10", "z10", COLS)
+        interleave_z(on_scalar, z10, 1, 0, 0, SCALAR_COLUMNS)
         square_h(1, 1, "z_slots11", (1, 7, 0, 6))
-        interleave_z(0, 1, on_vector, GPSIMD_COLUMNS, PIECE)
-        interleave_z(1, 0, on_vector, SCALAR_COLUMNS, COLS)
-        quantise("wm1", parts=2, only=0)
-        for span in (1, 2):
-            z_room(1, span, "grouped_z1%d" % span)
-            interleave_z(1, span, on_scalar, 0, PIECE)
-        quantise("z10")
-        quantise("z01", codes=shared("codes_z01", "z_slots00", [P, PIECE], U32))
-        quantise("wm1", parts=2, only=1)
-        z_room(0, 2, "grouped_wm1")
-        interleave_on_gpsimd(2, PIECE)
+        interleave_z(on_vector, z10, 1, 0, SCALAR_COLUMNS, PIECE)
+        interleave_z(on_vector, z10, 1, 0, PIECE, COLS)
+        for side in range(2):
+            quantise_columns("z10", z10[:, PACK * PIECE * side : PACK * PIECE * (side + 1)], PIECE * side)
+        quantise("wm1", 1)
+        quantise_columns("z01", z01[:], 0, "z_slots00")
+        third = placed("third", PIECE, 0)
+        interleave_z(on_scalar, third, 1, 1, 0, THIRD_COLUMNS)
+        interleave_on_gpsimd(third, 1, THIRD_COLUMNS, PIECE)
+        fourth = placed("fourth", PIECE, PIECE)
+        interleave_z(on_scalar, fourth, 1, 1, PIECE, COLS, PIECE)
         for u in range(N_TILES - 1):
             finish(u, (4, 5, 1, 7)[u])
-        quantise("z11")
+        quantise_columns("z11", third[:], 0)
+        rest = placed("rest", COLS - GPSIMD_COLUMNS, 0)
+        interleave_on_gpsimd(rest, 0, GPSIMD_COLUMNS, COLS, GPSIMD_COLUMNS)
         finish(N_TILES - 1, 7)
-        finish_pair(1, 0, 0)
-        quantise("z02")
-        quantise("z12")
-        finish_pair(1, 1, 6)
+        finish_pair(1, 0, 0, held("results10", [P, COLS], F32))
+        quantise_columns("z11", fourth[:], PIECE)
+        quantise_columns("z01", rest[:], GPSIMD_COLUMNS)
+        finish_pair(1, 1, 6, reused.tile([P, COLS], F32, name="results11", offset=0, align_bytes=64))
         late = shared("late", "z_slots11", [P, 2, COLS], F32)
         for pair in range(2):
             square_lin_pair(2, pair, late[:, pair, :], 2 + pair)
         for pair in range(2):
-            finish_pair(2, pair, 4 + pair)
+            finish_pair(2, pair, 4 + pair, held("results2%d" % pair, [P, COLS], F32))

@@ -147,13 +147,13 @@ def tile_list_factored_quadratic_scores_kernel(
         load_wf(0, 1, 0, room[:, 1, :])
         load_wf(0, 1, 1, room[:, 2, :])
         gather_words(0)
-        room = pieces("wm_first", "room0", 2)
-        for side in range(2):
-            wm_raw[(0, side)] = load_rows(wm[0:PASS, side * PIECE : (side + 1) * PIECE], room[:, side, :])
-        gather_words(1)
-        room = pieces("wf_third", "room1", 2)
+        room = pieces("wf_third", "room0", 2)
         for side in range(2):
             load_wf(1, 0, side, room[:, side, :])
+        gather_words(1)
+        room = pieces("wm_first", "room1", 2)
+        for side in range(2):
+            wm_raw[(0, side)] = load_rows(wm[0:PASS, side * PIECE : (side + 1) * PIECE], room[:, side, :])
 
         def v_plane(a, half):
             plane = v_sc[:] if a == 0 else v_sc_second[:].bitcast(U8)
@@ -221,26 +221,14 @@ def tile_list_factored_quadratic_scores_kernel(
                 slots = slice(part * width, (part + 1) * width)
                 copy(dst[:, side, :, :, :, slots], src[:, :, :, :, slots])
 
-        def cast_wm(b, side):
+        def cast_and_sign_wm(b, side):
             key = "wm%d" % b
             if key not in grouped:
                 grouped[key] = shared("grouped_" + key, "grouped_" + key, [P, N * PACK], BF16)[:]
             dst = grouped[key].rearrange("p (s c i j) -> p s c j i", s=2, i=4, j=PACK)
-            nc.vector.tensor_copy(dst[:, side], wm_raw[(b, side)].rearrange("p j (c i) -> p c j i", i=4))
-
-        def cast_and_sign_wm(b, side):
-            key = "wm%d" % b
-            if key not in grouped:
-                grouped[key] = held("grouped_" + key, [P, N * PACK], BF16)[:]
-            dst = grouped[key].rearrange("p (s c i j) -> p s c j i", s=2, i=4, j=PACK)
             signs = sign[:, b, :].unsqueeze(1).unsqueeze(3).broadcast_to([P, PIECE // 4, PACK, 4])
             src = wm_raw[(b, side)].rearrange("p j (c i) -> p c j i", i=4)
             nc.vector.tensor_tensor(dst[:, side], src, signs, ALU.mult)
-
-        def sign_wm(b, side):
-            rounded = grouped["wm%d" % b].rearrange("p (s c j) -> p s c j", s=2, j=PACK)[:, side]
-            signs = sign[:, b, :].unsqueeze(1).broadcast_to([P, PIECE, PACK])
-            nc.vector.tensor_tensor(rounded, rounded, signs, ALU.mult)
 
         z_slots = {}
 
@@ -286,10 +274,10 @@ def tile_list_factored_quadratic_scores_kernel(
                 z_slots[(b, half)][:, :, first:last].rearrange("p t (c i) -> p c t i", i=LINE),
             )
 
-        def interleave_on_gpsimd(room, b, first, last, start=0):
+        def interleave_on_gpsimd(room, b, half, first, last, start=0):
             nc.gpsimd.tensor_scalar(
                 room[:, PACK * (first - start) : PACK * (last - start)].rearrange("p (c t) -> p c t", t=PACK),
-                z_slots[(b, 1)][:, :, first:last].rearrange("p t c -> p c t"),
+                z_slots[(b, half)][:, :, first:last].rearrange("p t c -> p c t"),
                 1.0,
                 0.0,
                 ALU.mult,
@@ -321,13 +309,13 @@ def tile_list_factored_quadratic_scores_kernel(
                 y_pass(acc[:], 0, u, b, b == order[0], b == order[1])
             combine(0, u, acc[:], held("result%d" % u, [P, COLS], F32)[:])
 
-        def finish_pair(span, pair, number, results):
+        def finish_pair(span, pair, number):
             acc = bank(number)
-            order = (0, 1) if span == 1 else (1, 0)
-            for b in order:
+            for b in range(H_PASSES):
                 for place in range(2):
-                    first, last = (b, place) == (order[0], 0), (b, place) == (order[1], 1)
+                    first, last = (b, place) == (0, 0), (b, place) == (H_PASSES - 1, 1)
                     y_pass(acc[:, sides[place]], span, 2 * pair + place, b, first, last)
+            results = held("results%d%d" % (span, pair), [P, COLS], F32)
             for place in range(2):
                 combine(span, 2 * pair + place, acc[:, sides[place]], results[:, sides[place]])
 
@@ -348,59 +336,60 @@ def tile_list_factored_quadratic_scores_kernel(
             load_wf(1, 1, side, room[:, side, :])
         quantise("wf01", 0, 1)
         square_h(0, 0, "z_slots00", (7, 0, 1, 2))
-        square_h(0, 1, "z_slots01", (7, 0, 1, 7))
         for side in range(2):
-            cast_wm(0, side)
+            cast_wf(1, 0, side)
+        quantise("wf10", 0, 1)
+        z00 = z_room("z00", "grouped_wf10", COLS)
+        interleave_on_gpsimd(z00, 0, 0, 0, GPSIMD_COLUMNS)
+        interleave_z(on_scalar, z00, 0, 0, GPSIMD_COLUMNS, COLS)
+        square_h(0, 1, "z_slots01", (3, 4, 5, 2))
+        z0_fourth = z_room("z0_fourth", "z0_fourth", PIECE)
+        interleave_z(on_scalar, z0_fourth, 0, 1, PIECE, COLS, PIECE)
+        for side in range(2):
+            cast_and_sign_wm(0, side)
         room = pieces("wm_last", "room0", 2)
         for side in range(2):
             wm_raw[(1, side)] = load_rows(wm[PASS:, sides[side]], room[:, side, :])
-            sign_wm(0, side)
-        quantise("wm0", 0, 1)
-        cast_wf(1, 0, 0)
-        cast_wf(1, 0, 1)
-        bias = shared("bias", "room1", [P, N_TILES], F32)
-        with nc.allow_non_contiguous_dma(reason="one bias value a partition"):
-            nc.sync.dma_start(bias[:], b0.rearrange("(u p) -> p u", p=P))
+        quantise("wm0", 0)
         grouped["wf11"] = placed("grouped_wf11", COLS, 0)[:]
         cast_wf(1, 1, 0)
-        quantise("wf10", 0, 1)
+        quantise("wm0", 1)
+        bias = shared("bias", "grouped_wm0", [P, N_TILES], F32)
+        with nc.allow_non_contiguous_dma(reason="one bias value a partition"):
+            nc.sync.dma_start(bias[:], b0.rearrange("(u p) -> p u", p=P))
         cast_wf(1, 1, 1, parts=2)
         quantise("wf11", 0, 1)
-        z00 = z_room("z00", "z00", COLS)
-        interleave_z(on_scalar, z00, 0, 0, 0, COLS)
-        z01 = placed("z01", GPSIMD_COLUMNS, 0)
-        interleave_on_gpsimd(z01, 0, 0, GPSIMD_COLUMNS)
+        z0_third = placed("z0_third", PIECE, P)
+        interleave_on_gpsimd(z0_third, 0, 1, 0, PIECE)
         for side in range(2):
             cast_and_sign_wm(1, side)
         quantise("wm1", 0)
         quantise_columns("z00", z00[:], 0, "room0")
-        square_h(1, 0, "z_slots00", (2, 3, 4, 5), SCALAR_COLUMNS)
+        square_h(1, 0, "z_slots10", (3, 4, 5, 2), SCALAR_COLUMNS)
         z10 = z_room("z10", "z10", COLS)
         interleave_z(on_scalar, z10, 1, 0, 0, SCALAR_COLUMNS)
-        square_h(1, 1, "z_slots11", (1, 7, 0, 6))
+        square_h(1, 1, "z_slots11", (7, 0, 1, 6))
         interleave_z(on_vector, z10, 1, 0, SCALAR_COLUMNS, PIECE)
         interleave_z(on_vector, z10, 1, 0, PIECE, COLS)
         for side in range(2):
             quantise_columns("z10", z10[:, PACK * PIECE * side : PACK * PIECE * (side + 1)], PIECE * side)
         quantise("wm1", 1)
-        quantise_columns("z01", z01[:], 0, "z_slots00")
-        third = placed("third", PIECE, 0)
-        interleave_z(on_scalar, third, 1, 1, 0, THIRD_COLUMNS)
-        interleave_on_gpsimd(third, 1, THIRD_COLUMNS, PIECE)
-        fourth = placed("fourth", PIECE, PIECE)
-        interleave_z(on_scalar, fourth, 1, 1, PIECE, COLS, PIECE)
+        quantise_columns("z01", z0_fourth[:], PIECE, "z_slots10")
+        quantise_columns("z01", z0_third[:], 0)
+        z1_third = placed("z1_third", PIECE, 0)
+        interleave_z(on_scalar, z1_third, 1, 1, 0, THIRD_COLUMNS)
+        interleave_on_gpsimd(z1_third, 1, 1, THIRD_COLUMNS, PIECE)
+        z1_fourth = placed("z1_fourth", PIECE, PIECE)
+        interleave_z(on_scalar, z1_fourth, 1, 1, PIECE, COLS, PIECE)
         for u in range(N_TILES - 1):
-            finish(u, (4, 5, 1, 7)[u])
-        quantise_columns("z11", third[:], 0)
-        rest = placed("rest", COLS - GPSIMD_COLUMNS, 0)
-        interleave_on_gpsimd(rest, 0, GPSIMD_COLUMNS, COLS, GPSIMD_COLUMNS)
-        finish(N_TILES - 1, 7)
-        finish_pair(1, 0, 0, held("results10", [P, COLS], F32))
-        quantise_columns("z11", fourth[:], PIECE)
-        quantise_columns("z01", rest[:], GPSIMD_COLUMNS)
-        finish_pair(1, 1, 6, reused.tile([P, COLS], F32, name="results11", offset=0, align_bytes=64))
+            finish(u, (5, 2, 7)[u])
+        quantise_columns("z11", z1_third[:], 0)
+        finish(N_TILES - 1, 0)
+        finish_pair(1, 0, 1)
+        quantise_columns("z11", z1_fourth[:], PIECE)
+        finish_pair(1, 1, 6)
         late = shared("late", "z_slots11", [P, 2, COLS], F32)
         for pair in range(2):
-            square_lin_pair(2, pair, late[:, pair, :], 2 + pair)
+            square_lin_pair(2, pair, late[:, pair, :], 3 + pair)
         for pair in range(2):
-            finish_pair(2, pair, 4 + pair, held("results2%d" % pair, [P, COLS], F32))
+            finish_pair(2, pair, (5, 2)[pair])

@@ -28,11 +28,15 @@ K_PASSES = K // PASS
 H_PASSES = H // PASS
 N_TILES = N // P
 LIST_COLS = COLS // 16
-SCALAR_COLUMNS = 160
 GPSIMD_COLUMNS = 384
-THIRD_COLUMNS = 160
 PIECE = PASS // 2
 LINE = 8
+SCALAR_COLUMNS = COLS - (GPSIMD_COLUMNS - PIECE)
+AT_QUARTERS = 64
+AT_BESIDE = PIECE
+AT_SLOTS10 = AT_QUARTERS + 3 * PIECE
+AT_SLOTS00 = AT_SLOTS10 + COLS
+AT_LAST_CODES = AT_SLOTS00 + COLS
 
 
 def tile_list_factored_quadratic_scores_kernel(
@@ -108,6 +112,14 @@ def tile_list_factored_quadratic_scores_kernel(
         def pieces(name, tag, count):
             return shared(name, tag, [P, count, PACK * PIECE], F32)
 
+        wm_raw = {}
+
+        def load_wm(b, tag):
+            room = pieces("wm_raw%d" % b, tag, 2)
+            for side in range(2):
+                source = wm[b * PASS : (b + 1) * PASS, side * PIECE : (side + 1) * PIECE]
+                wm_raw[(b, side)] = load_rows(source, room[:, side, :])
+
         load_wf(0, 0, 0, pieces("wf_first", "early", 1)[:, 0, :])
 
         nc.scalar.copy(
@@ -126,8 +138,6 @@ def tile_list_factored_quadratic_scores_kernel(
         for e in range(2):
             nc.tensor.transpose(sign_words[:, :, e], sign_rows[:].bitcast(F32)[:, e::2], identity[:])
         sign = sign_words[:].rearrange("p b e -> p (b e)").bitcast(BF16).rearrange("p (b t) -> p b t", t=PACK)
-
-        wm_raw = {}
 
         v_w = {}
 
@@ -151,9 +161,9 @@ def tile_list_factored_quadratic_scores_kernel(
         for side in range(2):
             load_wf(1, 0, side, room[:, side, :])
         gather_words(1)
-        room = pieces("wm_first", "room1", 2)
+        room = pieces("wf_last", "room1", 2)
         for side in range(2):
-            wm_raw[(0, side)] = load_rows(wm[0:PASS, side * PIECE : (side + 1) * PIECE], room[:, side, :])
+            load_wf(1, 1, side, room[:, side, :])
 
         def v_plane(a, half):
             plane = v_sc[:] if a == 0 else v_sc_second[:].bitcast(U8)
@@ -198,10 +208,14 @@ def tile_list_factored_quadratic_scores_kernel(
         grouped = {}
         quantised = {}
 
-        def quantise_columns(key, source, first, tag=None):
+        def placed(name, shape, dtype, start):
+            return reused.tile(shape, dtype, name=name, offset=start * 8, align_bytes=64)
+
+        def quantise_columns(key, source, first, start=None, width=COLS):
             if key not in quantised:
-                codes = shared("codes_" + key, tag or "codes_" + key, [P, COLS], U32)
-                quantised[key] = (codes, held("scales_" + key, [P, COLS], U8))
+                name = "codes_" + key
+                codes = held(name, [P, width], U32) if start is None else placed(name, [P, width], U32, start)
+                quantised[key] = (codes, held("scales_" + key, [P, width], U8))
             codes, scales = quantised[key]
             words = slice(first, first + source.shape[1] // PACK)
             nc.vector.quantize_mx(out=codes[:, words].bitcast(FP8X4), scales=scales[:, words], in_=source)
@@ -209,6 +223,10 @@ def tile_list_factored_quadratic_scores_kernel(
         def quantise(key, *parts):
             for side in parts:
                 quantise_columns(key, grouped[key][:, PACK * PIECE * side : PACK * PIECE * (side + 1)], PIECE * side)
+
+        def quantise_wm(b, side, start=None):
+            source = grouped["wm%d" % b][:, PACK * PIECE * side : PACK * PIECE * (side + 1)]
+            quantise_columns("wm%d%d" % (b, side), source, 0, start, PIECE)
 
         def cast_wf(b, a, side, copy=nc.vector.tensor_copy, parts=1):
             key = "wf%d%d" % (b, a)
@@ -222,18 +240,14 @@ def tile_list_factored_quadratic_scores_kernel(
                 copy(dst[:, side, :, :, :, slots], src[:, :, :, :, slots])
 
         def cast_and_sign_wm(b, side):
-            key = "wm%d" % b
-            if key not in grouped:
-                grouped[key] = shared("grouped_" + key, "grouped_" + key, [P, N * PACK], BF16)[:]
-            dst = grouped[key].rearrange("p (s c i j) -> p s c j i", s=2, i=4, j=PACK)
+            dst = grouped["wm%d" % b].rearrange("p (s c i j) -> p s c j i", s=2, i=4, j=PACK)
             signs = sign[:, b, :].unsqueeze(1).unsqueeze(3).broadcast_to([P, PIECE // 4, PACK, 4])
             src = wm_raw[(b, side)].rearrange("p j (c i) -> p c j i", i=4)
             nc.vector.tensor_tensor(dst[:, side], src, signs, ALU.mult)
 
         z_slots = {}
 
-        def square_h(b, half, tag, banks, cut=COLS):
-            squares = shared("z_slots%d%d" % (b, half), tag, [P, PACK, COLS], BF16)
+        def square_h(b, half, squares, banks, cut=COLS, after_first=None):
             sums = []
 
             def square(slot, columns):
@@ -257,6 +271,8 @@ def tile_list_factored_quadratic_scores_kernel(
                     )
                 sums.append(acc)
                 square(slot, slice(0, COLS if slot < 2 else cut))
+                if slot == 0 and after_first is not None:
+                    after_first()
             if cut < COLS:
                 for slot in (2, 3):
                     square(slot, slice(cut, COLS))
@@ -264,9 +280,6 @@ def tile_list_factored_quadratic_scores_kernel(
 
         def z_room(name, tag, columns):
             return shared(name, tag, [P, columns * PACK], BF16)
-
-        def placed(name, columns, start):
-            return reused.tile([P, columns * PACK], BF16, name=name, offset=start * PACK * 2, align_bytes=64)
 
         def interleave_z(copy, room, b, half, first, last, start=0):
             copy(
@@ -285,15 +298,15 @@ def tile_list_factored_quadratic_scores_kernel(
             )
 
         def y_pass(acc, span, u, b, start, stop):
-            half, columns = within_half(span)
-            w_codes, w_scales = quantised["wm%d" % b]
-            z_codes, z_scales = quantised["z%d%d" % (b, half)]
+            w_codes, w_scales = quantised["wm%d%d" % (b, u // 2)]
+            rows = slice(u % 2 * P, (u % 2 + 1) * P)
+            z_codes, z_scales = quantised["z%d%d" % (b, span)]
             nc.tensor.matmul_mx(
                 out=acc,
-                lhsT=w_codes[:, u * P : (u + 1) * P].bitcast(FP8X4),
-                lhsT_scale=w_scales[:, u * P : (u + 1) * P],
-                rhs=z_codes[:, columns].bitcast(FP8X4),
-                rhs_scale=z_scales[:, columns],
+                lhsT=w_codes[:, rows].bitcast(FP8X4),
+                lhsT_scale=w_scales[:, rows],
+                rhs=z_codes[:].bitcast(FP8X4),
+                rhs_scale=z_scales[:],
                 start=start,
                 stop=stop,
             )
@@ -304,22 +317,24 @@ def tile_list_factored_quadratic_scores_kernel(
 
         def finish(u, number):
             acc = bank(number)
-            order = (0, 1) if u < 2 else (1, 0)
-            for b in order:
-                y_pass(acc[:], 0, u, b, b == order[0], b == order[1])
+            for b in range(H_PASSES):
+                y_pass(acc[:], 0, u, b, b == 0, b == H_PASSES - 1)
             combine(0, u, acc[:], held("result%d" % u, [P, COLS], F32)[:])
 
-        def finish_pair(span, pair, number):
+        def sum_pair(span, pair, number):
             acc = bank(number)
             for b in range(H_PASSES):
                 for place in range(2):
                     first, last = (b, place) == (0, 0), (b, place) == (H_PASSES - 1, 1)
                     y_pass(acc[:, sides[place]], span, 2 * pair + place, b, first, last)
+            return acc
+
+        def combine_pair(span, pair, acc):
             results = held("results%d%d" % (span, pair), [P, COLS], F32)
             for place in range(2):
                 combine(span, 2 * pair + place, acc[:, sides[place]], results[:, sides[place]])
 
-        on_vector, on_scalar = nc.vector.tensor_copy, nc.scalar.copy
+        on_scalar = nc.scalar.copy
 
         cast_wf(0, 0, 0, on_scalar)
         early = shared("early_lin", "early", [P, N_TILES + 2, COLS], F32)
@@ -331,65 +346,68 @@ def tile_list_factored_quadratic_scores_kernel(
         quantise("wf00", 0, 1)
         cast_wf(0, 1, 0)
         cast_wf(0, 1, 1, parts=2)
-        room = pieces("wf_last", "room2", 2)
-        for side in range(2):
-            load_wf(1, 1, side, room[:, side, :])
+        load_wm(0, "room2")
         quantise("wf01", 0, 1)
-        square_h(0, 0, "z_slots00", (7, 0, 1, 2))
+        square_h(0, 0, placed("z_slots00", [P, PACK, COLS], BF16, AT_SLOTS00), (7, 0, 1, 2))
         for side in range(2):
             cast_wf(1, 0, side)
+        load_wm(1, "room0")
         quantise("wf10", 0, 1)
-        z00 = z_room("z00", "grouped_wf10", COLS)
-        interleave_on_gpsimd(z00, 0, 0, 0, GPSIMD_COLUMNS)
-        interleave_z(on_scalar, z00, 0, 0, GPSIMD_COLUMNS, COLS)
-        square_h(0, 1, "z_slots01", (3, 4, 5, 2))
-        z0_fourth = z_room("z0_fourth", "z0_fourth", PIECE)
-        interleave_z(on_scalar, z0_fourth, 0, 1, PIECE, COLS, PIECE)
-        for side in range(2):
-            cast_and_sign_wm(0, side)
-        room = pieces("wm_last", "room0", 2)
-        for side in range(2):
-            wm_raw[(1, side)] = load_rows(wm[PASS:, sides[side]], room[:, side, :])
-        quantise("wm0", 0)
-        grouped["wf11"] = placed("grouped_wf11", COLS, 0)[:]
+        square_h(0, 1, held("z_slots01", [P, PACK, COLS], BF16), (3, 4, 5, 7))
         cast_wf(1, 1, 0)
-        quantise("wm0", 1)
-        bias = shared("bias", "grouped_wm0", [P, N_TILES], F32)
-        with nc.allow_non_contiguous_dma(reason="one bias value a partition"):
-            nc.sync.dma_start(bias[:], b0.rearrange("(u p) -> p u", p=P))
         cast_wf(1, 1, 1, parts=2)
         quantise("wf11", 0, 1)
-        z0_third = placed("z0_third", PIECE, P)
-        interleave_on_gpsimd(z0_third, 0, 1, 0, PIECE)
+
+        z00 = z_room("z00", "grouped_wf11", COLS)
+        interleave_on_gpsimd(z00, 0, 0, 0, GPSIMD_COLUMNS)
+        interleave_z(on_scalar, z00, 0, 0, GPSIMD_COLUMNS, COLS)
+        grouped["wm0"] = placed("grouped_wm0", [P, N * PACK], BF16, AT_BESIDE)[:]
+        for side in range(2):
+            cast_and_sign_wm(0, side)
+        bias = shared("bias", "room2", [P, N_TILES], F32)
+        with nc.allow_non_contiguous_dma(reason="one bias value a partition"):
+            nc.sync.dma_start(bias[:], b0.rearrange("(u p) -> p u", p=P))
+        quantise_wm(0, 0, AT_SLOTS00)
+        quantise_columns("z00", z00[:], 0)
+        quantise_wm(0, 1, AT_SLOTS00 + PIECE // 2)
+
+        square_h(1, 0, placed("z_slots10", [P, PACK, COLS], BF16, AT_SLOTS10), (0, 1, 2, 3), SCALAR_COLUMNS)
+        beside = placed("beside", [P, GPSIMD_COLUMNS * PACK], BF16, AT_BESIDE)
+        interleave_on_gpsimd(beside, 0, 1, 0, PIECE)
+        interleave_on_gpsimd(beside, 1, 0, SCALAR_COLUMNS, COLS, SCALAR_COLUMNS - PIECE)
+        z10 = z_room("z10", "z10", SCALAR_COLUMNS)
+        interleave_z(on_scalar, z10, 1, 0, 0, SCALAR_COLUMNS // 2)
+        grouped["wm1"] = z_room("grouped_wm1", "grouped_wf11", COLS)[:]
         for side in range(2):
             cast_and_sign_wm(1, side)
-        quantise("wm1", 0)
-        quantise_columns("z00", z00[:], 0, "room0")
-        square_h(1, 0, "z_slots10", (3, 4, 5, 2), SCALAR_COLUMNS)
-        z10 = z_room("z10", "z10", COLS)
-        interleave_z(on_scalar, z10, 1, 0, 0, SCALAR_COLUMNS)
-        square_h(1, 1, "z_slots11", (7, 0, 1, 6))
-        interleave_z(on_vector, z10, 1, 0, SCALAR_COLUMNS, PIECE)
-        interleave_z(on_vector, z10, 1, 0, PIECE, COLS)
-        for side in range(2):
-            quantise_columns("z10", z10[:, PACK * PIECE * side : PACK * PIECE * (side + 1)], PIECE * side)
-        quantise("wm1", 1)
-        quantise_columns("z01", z0_fourth[:], PIECE, "z_slots10")
-        quantise_columns("z01", z0_third[:], 0)
-        z1_third = placed("z1_third", PIECE, 0)
-        interleave_z(on_scalar, z1_third, 1, 1, 0, THIRD_COLUMNS)
-        interleave_on_gpsimd(z1_third, 1, 1, THIRD_COLUMNS, PIECE)
-        z1_fourth = placed("z1_fourth", PIECE, PIECE)
+
+        def rest_of_z10():
+            interleave_z(on_scalar, z10, 1, 0, SCALAR_COLUMNS // 2, SCALAR_COLUMNS)
+
+        square_h(1, 1, shared("z_slots11", "z_slots11", [P, PACK, COLS], BF16), (4, 5, 0, 1), COLS, rest_of_z10)
+        quantise_wm(1, 0)
+        quantise_columns("z10", beside[:, PACK * PIECE :], SCALAR_COLUMNS)
+        quantise_columns("z10", z10[:], 0)
+        quantise_wm(1, 1, AT_SLOTS10)
+        quantise_columns("z01", beside[:, 0 : PACK * PIECE], 0, AT_SLOTS10 + PIECE // 2, PIECE)
+
+        z0_fourth = placed("z0_fourth", [P, PIECE * PACK], BF16, AT_QUARTERS)
+        interleave_on_gpsimd(z0_fourth, 0, 1, PIECE, COLS, PIECE)
+        z1_third = placed("z1_third", [P, PIECE * PACK], BF16, AT_QUARTERS + PIECE)
+        interleave_z(on_scalar, z1_third, 1, 1, 0, PIECE)
+        z1_fourth = placed("z1_fourth", [P, PIECE * PACK], BF16, AT_QUARTERS + 2 * PIECE)
         interleave_z(on_scalar, z1_fourth, 1, 1, PIECE, COLS, PIECE)
         for u in range(N_TILES - 1):
-            finish(u, (5, 2, 7)[u])
-        quantise_columns("z11", z1_third[:], 0)
-        finish(N_TILES - 1, 0)
-        finish_pair(1, 0, 1)
-        quantise_columns("z11", z1_fourth[:], PIECE)
-        finish_pair(1, 1, 6)
+            finish(u, (7, 2, 3)[u])
+        quantise_columns("z11", z1_third[:], 0, AT_LAST_CODES, PIECE)
+        finish(N_TILES - 1, 6)
+        quantise_columns("z02", z0_fourth[:], 0, None, PIECE)
+        third = [sum_pair(1, pair, (5, 0)[pair]) for pair in range(2)]
+        combine_pair(1, 0, third[0])
+        quantise_columns("z12", z1_fourth[:], 0, AT_LAST_CODES, PIECE)
+        combine_pair(1, 1, third[1])
         late = shared("late", "z_slots11", [P, 2, COLS], F32)
         for pair in range(2):
-            square_lin_pair(2, pair, late[:, pair, :], 3 + pair)
+            square_lin_pair(2, pair, late[:, pair, :], (4, 7)[pair])
         for pair in range(2):
-            finish_pair(2, pair, (5, 2)[pair])
+            combine_pair(2, pair, sum_pair(2, pair, (2, 3)[pair]))

@@ -32,9 +32,12 @@ GPSIMD_COLUMNS = 384
 PIECE = PASS // 2
 LINE = 8
 SCALAR_COLUMNS = COLS - (GPSIMD_COLUMNS - PIECE)
-AT_QUARTERS = 64
+OVERLAP = 64
+AT_QUARTERS = OVERLAP
 AT_BESIDE = PIECE
-AT_SLOTS10 = AT_QUARTERS + 3 * PIECE
+AT_Z00 = AT_BESIDE + GPSIMD_COLUMNS - OVERLAP
+AT_WM1 = AT_Z00 + GPSIMD_COLUMNS - OVERLAP
+AT_SLOTS10 = AT_WM1 + COLS
 AT_SLOTS00 = AT_SLOTS10 + COLS
 AT_LAST_CODES = AT_SLOTS00 + COLS
 
@@ -220,9 +223,9 @@ def tile_list_factored_quadratic_scores_kernel(
             words = slice(first, first + source.shape[1] // PACK)
             nc.vector.quantize_mx(out=codes[:, words].bitcast(FP8X4), scales=scales[:, words], in_=source)
 
-        def quantise(key, *parts):
-            for side in parts:
-                quantise_columns(key, grouped[key][:, PACK * PIECE * side : PACK * PIECE * (side + 1)], PIECE * side)
+        def quantise(key):
+            for pair in range(2):
+                quantise_columns(key, grouped[key][pair], PIECE * pair)
 
         def quantise_wm(b, side, start=None):
             source = grouped["wm%d" % b][:, PACK * PIECE * side : PACK * PIECE * (side + 1)]
@@ -231,13 +234,14 @@ def tile_list_factored_quadratic_scores_kernel(
         def cast_wf(b, a, side, copy=nc.vector.tensor_copy, parts=1):
             key = "wf%d%d" % (b, a)
             if key not in grouped:
-                grouped[key] = shared("grouped_" + key, "grouped_" + key, [P, PASS * PACK], BF16)[:]
-            dst = grouped[key].rearrange("p (t s u i j) -> p s u j i t", t=PACK, s=2, i=2, j=PACK)
+                whole = held("grouped_" + key, [P, PASS * PACK], BF16)
+                grouped[key] = (whole[:, 0 : PACK * PIECE], whole[:, PACK * PIECE :], whole[:])
             src = wf_raw[(b, a, side)].rearrange("p j (u i t) -> p u j i t", i=2, t=PACK)
             width = PACK // parts
             for part in range(parts):
-                slots = slice(part * width, (part + 1) * width)
-                copy(dst[:, side, :, :, :, slots], src[:, :, :, :, slots])
+                room = grouped[key][part if parts == 2 else 2]
+                dst = room.rearrange("p (t s u i j) -> p s u j i t", t=width, s=2, i=2, j=PACK)
+                copy(dst[:, side], src[:, :, :, :, part * width : (part + 1) * width])
 
         def cast_and_sign_wm(b, side):
             dst = grouped["wm%d" % b].rearrange("p (s c i j) -> p s c j i", s=2, i=4, j=PACK)
@@ -247,7 +251,7 @@ def tile_list_factored_quadratic_scores_kernel(
 
         z_slots = {}
 
-        def square_h(b, half, squares, banks, cut=COLS, after_first=None):
+        def square_h(b, half, squares, banks, cut=COLS):
             sums = []
 
             def square(slot, columns):
@@ -271,8 +275,6 @@ def tile_list_factored_quadratic_scores_kernel(
                     )
                 sums.append(acc)
                 square(slot, slice(0, COLS if slot < 2 else cut))
-                if slot == 0 and after_first is not None:
-                    after_first()
             if cut < COLS:
                 for slot in (2, 3):
                     square(slot, slice(cut, COLS))
@@ -343,30 +345,36 @@ def tile_list_factored_quadratic_scores_kernel(
         for pair in range(2):
             square_lin_pair(1, pair, early[:, N_TILES + pair, :], N_TILES + pair)
         cast_wf(0, 0, 1)
-        quantise("wf00", 0, 1)
+        quantise("wf00")
         cast_wf(0, 1, 0)
         cast_wf(0, 1, 1, parts=2)
         load_wm(0, "room2")
-        quantise("wf01", 0, 1)
+        quantise("wf01")
         square_h(0, 0, placed("z_slots00", [P, PACK, COLS], BF16, AT_SLOTS00), (7, 0, 1, 2))
         for side in range(2):
             cast_wf(1, 0, side)
         load_wm(1, "room0")
-        quantise("wf10", 0, 1)
+        quantise("wf10")
         square_h(0, 1, held("z_slots01", [P, PACK, COLS], BF16), (3, 4, 5, 7))
-        cast_wf(1, 1, 0)
+        grouped["wf11"] = (
+            placed("wf11_first", [P, PIECE * PACK], BF16, AT_Z00 + OVERLAP)[:],
+            held("wf11_second", [P, PIECE * PACK], BF16)[:],
+        )
+        cast_wf(1, 1, 0, parts=2)
+        z00_rest = z_room("z00_rest", "z00_rest", COLS - GPSIMD_COLUMNS)
+        interleave_z(nc.vector.tensor_copy, z00_rest, 0, 0, GPSIMD_COLUMNS, COLS, GPSIMD_COLUMNS)
         cast_wf(1, 1, 1, parts=2)
-        quantise("wf11", 0, 1)
+        quantise("wf11")
 
-        z00 = z_room("z00", "grouped_wf11", COLS)
+        z00 = placed("z00", [P, GPSIMD_COLUMNS * PACK], BF16, AT_Z00)
         interleave_on_gpsimd(z00, 0, 0, 0, GPSIMD_COLUMNS)
-        interleave_z(on_scalar, z00, 0, 0, GPSIMD_COLUMNS, COLS)
-        grouped["wm0"] = placed("grouped_wm0", [P, N * PACK], BF16, AT_BESIDE)[:]
+        grouped["wm0"] = held("grouped_wm0", [P, N * PACK], BF16)[:]
         for side in range(2):
             cast_and_sign_wm(0, side)
         bias = shared("bias", "room2", [P, N_TILES], F32)
         with nc.allow_non_contiguous_dma(reason="one bias value a partition"):
             nc.sync.dma_start(bias[:], b0.rearrange("(u p) -> p u", p=P))
+        quantise_columns("z00", z00_rest[:], GPSIMD_COLUMNS, AT_SLOTS00 + PIECE)
         quantise_wm(0, 0, AT_SLOTS00)
         quantise_columns("z00", z00[:], 0)
         quantise_wm(0, 1, AT_SLOTS00 + PIECE // 2)
@@ -376,20 +384,16 @@ def tile_list_factored_quadratic_scores_kernel(
         interleave_on_gpsimd(beside, 0, 1, 0, PIECE)
         interleave_on_gpsimd(beside, 1, 0, SCALAR_COLUMNS, COLS, SCALAR_COLUMNS - PIECE)
         z10 = z_room("z10", "z10", SCALAR_COLUMNS)
-        interleave_z(on_scalar, z10, 1, 0, 0, SCALAR_COLUMNS // 2)
-        grouped["wm1"] = z_room("grouped_wm1", "grouped_wf11", COLS)[:]
+        interleave_z(on_scalar, z10, 1, 0, 0, SCALAR_COLUMNS)
+        grouped["wm1"] = placed("grouped_wm1", [P, N * PACK], BF16, AT_WM1)[:]
         for side in range(2):
             cast_and_sign_wm(1, side)
-
-        def rest_of_z10():
-            interleave_z(on_scalar, z10, 1, 0, SCALAR_COLUMNS // 2, SCALAR_COLUMNS)
-
-        square_h(1, 1, shared("z_slots11", "z_slots11", [P, PACK, COLS], BF16), (4, 5, 0, 1), COLS, rest_of_z10)
+        square_h(1, 1, shared("z_slots11", "z_slots11", [P, PACK, COLS], BF16), (0, 1, 2, 3))
         quantise_wm(1, 0)
         quantise_columns("z10", beside[:, PACK * PIECE :], SCALAR_COLUMNS)
         quantise_columns("z10", z10[:], 0)
-        quantise_wm(1, 1, AT_SLOTS10)
         quantise_columns("z01", beside[:, 0 : PACK * PIECE], 0, AT_SLOTS10 + PIECE // 2, PIECE)
+        quantise_wm(1, 1, AT_SLOTS10)
 
         z0_fourth = placed("z0_fourth", [P, PIECE * PACK], BF16, AT_QUARTERS)
         interleave_on_gpsimd(z0_fourth, 0, 1, PIECE, COLS, PIECE)
@@ -398,16 +402,16 @@ def tile_list_factored_quadratic_scores_kernel(
         z1_fourth = placed("z1_fourth", [P, PIECE * PACK], BF16, AT_QUARTERS + 2 * PIECE)
         interleave_z(on_scalar, z1_fourth, 1, 1, PIECE, COLS, PIECE)
         for u in range(N_TILES - 1):
-            finish(u, (7, 2, 3)[u])
+            finish(u, (4, 5, 7)[u])
         quantise_columns("z11", z1_third[:], 0, AT_LAST_CODES, PIECE)
         finish(N_TILES - 1, 6)
         quantise_columns("z02", z0_fourth[:], 0, None, PIECE)
-        third = [sum_pair(1, pair, (5, 0)[pair]) for pair in range(2)]
+        third = [sum_pair(1, pair, (2, 3)[pair]) for pair in range(2)]
         combine_pair(1, 0, third[0])
         quantise_columns("z12", z1_fourth[:], 0, AT_LAST_CODES, PIECE)
         combine_pair(1, 1, third[1])
         late = shared("late", "z_slots11", [P, 2, COLS], F32)
         for pair in range(2):
-            square_lin_pair(2, pair, late[:, pair, :], (4, 7)[pair])
+            square_lin_pair(2, pair, late[:, pair, :], pair)
         for pair in range(2):
-            combine_pair(2, pair, sum_pair(2, pair, (2, 3)[pair]))
+            combine_pair(2, pair, sum_pair(2, pair, (4, 5)[pair]))

from contextlib import ExitStack

import concourse.mybir as mybir
from concourse.masks import make_identity

K, H, N, T, S = 1024, 1024, 512, 2048, 1024
FLOPS = 2 * S * (K * H + K * N + H * N)

F32 = mybir.dt.float32
BF16 = mybir.dt.bfloat16
I32 = mybir.dt.int32
U32 = mybir.dt.uint32
U16 = mybir.dt.uint16
U8 = mybir.dt.uint8
FP8X4 = mybir.dt.float8_e4m3fn_x4
FP4X4 = mybir.dt.float4_e2m1fn_x4
ALU = mybir.AluOpType
ACT = mybir.ActivationFunctionType

P = 128
PACK = 4
PASS = P * PACK
COLS = 512
BANKS = 8
QUADRANTS = 4
HALVES = S // COLS
K_PASSES = K // PASS
H_PASSES = H // PASS
N_TILES = N // P
LIST_COLS = COLS // 16
GPSIMD_COLUMNS = 384
PIECE = PASS // 2
LINE = 8
SCALAR_COLUMNS = COLS - (GPSIMD_COLUMNS - PIECE)
OVERLAP = 64
AT_QUARTERS = OVERLAP
AT_BESIDE = PIECE
AT_Z00 = AT_BESIDE + GPSIMD_COLUMNS - OVERLAP
AT_WM1 = AT_Z00 + GPSIMD_COLUMNS - OVERLAP
AT_SLOTS10 = AT_WM1 + COLS
AT_SLOTS00 = AT_SLOTS10 + COLS
AT_LAST_CODES = AT_SLOTS00 + COLS


def tile_list_factored_quadratic_scores_kernel(
    tc, tab_words, tab_scales, offs, wf, wl_words, wl_scales, gain, wm, b0, out
):
    nc = tc.nc
    with ExitStack() as ctx:
        keep = ctx.enter_context(tc.tile_pool(name="keep", bufs=1))
        reused = ctx.enter_context(tc.tile_pool(name="reused", bufs=1))
        psum = ctx.enter_context(tc.psum_pool(name="psum", bufs=1))

        def held(name, shape, dtype):
            return keep.tile(shape, dtype, name=name, align_bytes=64)

        def shared(name, tag, shape, dtype):
            return keep.tile(shape, dtype, name=name, tag=tag, align_bytes=64)

        def bank(number):
            return psum.tile([P, COLS], F32, name="acc", tag="bank%d" % number)

        def pass_order(half):
            return (0, 1) if half == 0 else (1, 0)

        offsets = keep.tile([P, S // 16], U16, name="offsets")
        nc.sync.dma_start(offsets[:], offs)

        tab_sc = shared("tab_sc", "room2", [P, T // 4], I32)
        nc.gpsimd.memset(tab_sc[:], 0)
        gain_rows = held("gain_rows", [H_PASSES, PASS], F32)
        nc.sync.dma_start(gain_rows[:], gain.rearrange("(b r) -> b r", b=H_PASSES))
        wl_w = held("wl_w", [P, K_PASSES, N // 2], I32)
        nc.sync.dma_start(wl_w[:], wl_words.bitcast(I32).rearrange("a p c -> p a c"))
        scale_rows = tab_scales.bitcast(I32).rearrange("a (q m) c -> m q a c", q=QUADRANTS)
        for m in range(4):
            nc.sync.dma_start(tab_sc[m:P:16, :], scale_rows[m])
        tab_w = [shared("tab_w%d" % a, "room%d" % a, [P, T], I32) for a in range(K_PASSES)]

        def load_table_words(a):
            nc.sync.dma_start(tab_w[a][:], tab_words[a].rearrange("p t i -> p (t i)").bitcast(I32))

        load_table_words(0)

        wl_sc = held("wl_sc", [P, K_PASSES, N // 4], I32)
        nc.gpsimd.memset(wl_sc[:], 0)
        gain_slots = held("gain_slots", [P, PACK, P], F32)
        nc.gpsimd.memset(gain_slots[:], 0.0)
        sign_rows = held("sign_rows", [P, PASS], BF16)
        nc.gpsimd.memset(sign_rows[:], 0.0)
        v_sc_second = held("v_sc_second", [P, S // 4], I32)
        nc.gpsimd.memset(v_sc_second[:], 0)
        identity = held("identity", [P, P], F32)
        make_identity(nc, identity[:])

        wl_scales_i = wl_scales.bitcast(I32)
        for q in range(QUADRANTS):
            nc.sync.dma_start(
                wl_sc[32 * q : 32 * q + 4, :, :],
                wl_scales_i[:, 4 * q : 4 * q + 4, :].rearrange("a m c -> m a c"),
            )
        load_table_words(1)

        wf_raw = {}

        def load_rows(source, room):
            raw = room.rearrange("p (j c) -> p j c", j=PACK)
            nc.sync.dma_start(raw, source.rearrange("(p j) c -> p j c", j=PACK))
            return raw

        def load_wf(b, a, side, room):
            columns = slice(b * PASS + side * PIECE, b * PASS + (side + 1) * PIECE)
            wf_raw[(b, a, side)] = load_rows(wf[a * PASS : (a + 1) * PASS, columns], room)

        def pieces(name, tag, count):
            return shared(name, tag, [P, count, PACK * PIECE], F32)

        wm_raw = {}

        def load_wm(b, tag):
            room = pieces("wm_raw%d" % b, tag, 2)
            for side in range(2):
                source = wm[b * PASS : (b + 1) * PASS, side * PIECE : (side + 1) * PIECE]
                wm_raw[(b, side)] = load_rows(source, room[:, side, :])

        load_wf(0, 0, 0, pieces("wf_first", "early", 1)[:, 0, :])

        nc.scalar.copy(
            gain_slots[0:H_PASSES, :, :],
            gain_rows[:].rearrange("b (m t) -> b t m", t=PACK),
        )
        gain_columns = psum.tile([P, PACK, P], F32, name="gain_columns", tag="bank%d" % (BANKS - 1))
        for slot in range(PACK):
            nc.tensor.transpose(gain_columns[:, slot, :], gain_slots[:, slot, :], identity[:])
        magnitude = held("magnitude", [P, PACK, H_PASSES], F32)
        root = held("root", [P, PACK, H_PASSES], F32)
        nc.scalar.activation(magnitude[:], gain_columns[:, :, 0:H_PASSES], ACT.Abs)
        nc.scalar.activation(root[:], magnitude[:], ACT.Sqrt)
        nc.scalar.activation(sign_rows[0:H_PASSES, :], gain_rows[:], ACT.Sign)
        sign_words = psum.tile([P, P, 2], F32, name="sign_words", tag="bank6")
        for e in range(2):
            nc.tensor.transpose(sign_words[:, :, e], sign_rows[:].bitcast(F32)[:, e::2], identity[:])
        sign = sign_words[:].rearrange("p b e -> p (b e)").bitcast(BF16).rearrange("p (b t) -> p b t", t=PACK)

        v_w = {}

        def gather_words(a):
            for half in range(HALVES):
                picked = held("v_w%d%d" % (a, half), [P, COLS], U32)
                entries = offsets[:, half * LIST_COLS : (half + 1) * LIST_COLS]
                nc.vector.tensor_copy(picked[:], tab_w[a][:].bitcast(U32).indirect(entries))
                v_w[(a, half)] = picked

        v_sc = held("v_sc", [P, S], U8)
        nc.vector.tensor_copy(v_sc[:], tab_sc[:].bitcast(U8).indirect(offsets[:]))
        for q in range(QUADRANTS):
            nc.sync.dma_start(v_sc_second[32 * q : 32 * q + 4, :], v_sc[32 * q + 16 : 32 * q + 20, :].bitcast(I32))
        room = pieces("wf_second", "room2", 3)
        load_wf(0, 0, 1, room[:, 0, :])
        load_wf(0, 1, 0, room[:, 1, :])
        load_wf(0, 1, 1, room[:, 2, :])
        gather_words(0)
        room = pieces("wf_third", "room0", 2)
        for side in range(2):
            load_wf(1, 0, side, room[:, side, :])
        gather_words(1)
        room = pieces("wf_last", "room1", 2)
        for side in range(2):
            load_wf(1, 1, side, room[:, side, :])

        def v_plane(a, half):
            plane = v_sc[:] if a == 0 else v_sc_second[:].bitcast(U8)
            return plane[:, half * COLS : (half + 1) * COLS]

        spans = (slice(0, COLS), slice(COLS, COLS + PIECE), slice(COLS + PIECE, S))
        sides = (slice(0, PIECE), slice(PIECE, COLS))

        def within_half(span):
            half = spans[span].start // COLS
            return half, slice(spans[span].start - half * COLS, spans[span].stop - half * COLS)

        lin_sq = {}

        def lin_passes(acc, span, u):
            half, columns = within_half(span)
            order = pass_order(half)
            for a in order:
                nc.tensor.matmul_mx(
                    out=acc,
                    lhsT=wl_w[:, a, :].bitcast(U8)[:, 2 * u * P : 2 * (u + 1) * P].bitcast(FP4X4),
                    lhsT_scale=wl_sc[:, a, :].bitcast(U8)[:, u * P : (u + 1) * P],
                    rhs=v_w[(a, half)][:, columns].bitcast(FP8X4),
                    rhs_scale=v_plane(a, half)[:, columns],
                    start=(a == order[0]),
                    stop=(a == order[1]),
                )

        def square_lin(u, squared):
            acc = bank(u)
            lin_passes(acc[:], 0, u)
            nc.scalar.activation(squared, acc[:], ACT.Square)
            lin_sq[(0, u)] = squared

        def square_lin_pair(span, pair, squared, number):
            acc = bank(number)
            for place in range(2):
                lin_passes(acc[:, sides[place]], span, 2 * pair + place)
                lin_sq[(span, 2 * pair + place)] = squared[:, sides[place]]
            nc.scalar.activation(squared, acc[:], ACT.Square)

        grouped = {}
        quantised = {}

        def placed(name, shape, dtype, start):
            return reused.tile(shape, dtype, name=name, offset=start * 8, align_bytes=64)

        def quantise_columns(key, source, first, start=None, width=COLS):
            if key not in quantised:
                name = "codes_" + key
                codes = held(name, [P, width], U32) if start is None else placed(name, [P, width], U32, start)
                quantised[key] = (codes, held("scales_" + key, [P, width], U8))
            codes, scales = quantised[key]
            words = slice(first, first + source.shape[1] // PACK)
            nc.vector.quantize_mx(out=codes[:, words].bitcast(FP8X4), scales=scales[:, words], in_=source)

        def quantise(key):
            for pair in range(2):
                quantise_columns(key, grouped[key][pair], PIECE * pair)

        def quantise_wm(b, side, start=None):
            source = grouped["wm%d" % b][:, PACK * PIECE * side : PACK * PIECE * (side + 1)]
            quantise_columns("wm%d%d" % (b, side), source, 0, start, PIECE)

        def cast_wf(b, a, side, copy=nc.vector.tensor_copy, parts=1):
            key = "wf%d%d" % (b, a)
            if key not in grouped:
                whole = held("grouped_" + key, [P, PASS * PACK], BF16)
                grouped[key] = (whole[:, 0 : PACK * PIECE], whole[:, PACK * PIECE :], whole[:])
            src = wf_raw[(b, a, side)].rearrange("p j (u i t) -> p u j i t", i=2, t=PACK)
            width = PACK // parts
            for part in range(parts):
                room = grouped[key][part if parts == 2 else 2]
                dst = room.rearrange("p (t s u i j) -> p s u j i t", t=width, s=2, i=2, j=PACK)
                copy(dst[:, side], src[:, :, :, :, part * width : (part + 1) * width])

        def cast_and_sign_wm(b, side):
            dst = grouped["wm%d" % b].rearrange("p (s c i j) -> p s c j i", s=2, i=4, j=PACK)
            signs = sign[:, b, :].unsqueeze(1).unsqueeze(3).broadcast_to([P, PIECE // 4, PACK, 4])
            src = wm_raw[(b, side)].rearrange("p j (c i) -> p c j i", i=4)
            nc.vector.tensor_tensor(dst[:, side], src, signs, ALU.mult)

        z_slots = {}

        def square_h(b, half, squares, banks, cut=COLS):
            sums = []

            def square(slot, columns):
                nc.scalar.activation(
                    squares[:, slot, columns], sums[slot][:, columns], ACT.Square, scale=root[:, slot, b : b + 1]
                )

            for slot in range(PACK):
                acc = bank(banks[slot])
                order = pass_order(half)
                for a in order:
                    codes, scales = quantised["wf%d%d" % (b, a)]
                    nc.tensor.matmul_mx(
                        out=acc[:],
                        lhsT=codes[:, slot * P : (slot + 1) * P].bitcast(FP8X4),
                        lhsT_scale=scales[:, slot * P : (slot + 1) * P],
                        rhs=v_w[(a, half)][:].bitcast(FP8X4),
                        rhs_scale=v_plane(a, half),
                        start=(a == order[0]),
                        stop=(a == order[1]),
                    )
                sums.append(acc)
                square(slot, slice(0, COLS if slot < 2 else cut))
            if cut < COLS:
                for slot in (2, 3):
                    square(slot, slice(cut, COLS))
            z_slots[(b, half)] = squares

        def z_room(name, tag, columns):
            return shared(name, tag, [P, columns * PACK], BF16)

        def interleave_z(copy, room, b, half, first, last, start=0):
            copy(
                room[:, PACK * (first - start) : PACK * (last - start)].rearrange("p (c i t) -> p c t i", i=LINE, t=PACK),
                z_slots[(b, half)][:, :, first:last].rearrange("p t (c i) -> p c t i", i=LINE),
            )

        def interleave_on_gpsimd(room, b, half, first, last, start=0):
            nc.gpsimd.tensor_scalar(
                room[:, PACK * (first - start) : PACK * (last - start)].rearrange("p (c t) -> p c t", t=PACK),
                z_slots[(b, half)][:, :, first:last].rearrange("p t c -> p c t"),
                1.0,
                0.0,
                ALU.mult,
                ALU.add,
            )

        def y_pass(acc, span, u, b, start, stop):
            w_codes, w_scales = quantised["wm%d%d" % (b, u // 2)]
            rows = slice(u % 2 * P, (u % 2 + 1) * P)
            z_codes, z_scales = quantised["z%d%d" % (b, span)]
            nc.tensor.matmul_mx(
                out=acc,
                lhsT=w_codes[:, rows].bitcast(FP8X4),
                lhsT_scale=w_scales[:, rows],
                rhs=z_codes[:].bitcast(FP8X4),
                rhs_scale=z_scales[:],
                start=start,
                stop=stop,
            )

        def combine(span, u, acc, result):
            nc.vector.scalar_tensor_tensor(result, lin_sq[(span, u)], bias[:, u : u + 1], acc, ALU.add, ALU.subtract)
            nc.sync.dma_start(out[u * P : (u + 1) * P, spans[span]], result)

        def finish(u, number):
            acc = bank(number)
            for b in range(H_PASSES):
                y_pass(acc[:], 0, u, b, b == 0, b == H_PASSES - 1)
            combine(0, u, acc[:], held("result%d" % u, [P, COLS], F32)[:])

        def sum_pair(span, pair, number):
            acc = bank(number)
            for b in range(H_PASSES):
                for place in range(2):
                    first, last = (b, place) == (0, 0), (b, place) == (H_PASSES - 1, 1)
                    y_pass(acc[:, sides[place]], span, 2 * pair + place, b, first, last)
            return acc

        def combine_pair(span, pair, acc):
            results = held("results%d%d" % (span, pair), [P, COLS], F32)
            for place in range(2):
                combine(span, 2 * pair + place, acc[:, sides[place]], results[:, sides[place]])

        on_scalar = nc.scalar.copy

        cast_wf(0, 0, 0, on_scalar)
        early = shared("early_lin", "early", [P, N_TILES + 2, COLS], F32)
        for u in range(N_TILES):
            square_lin(u, early[:, u, :])
        for pair in range(2):
            square_lin_pair(1, pair, early[:, N_TILES + pair, :], N_TILES + pair)
        cast_wf(0, 0, 1)
        quantise("wf00")
        cast_wf(0, 1, 0)
        cast_wf(0, 1, 1, parts=2)
        load_wm(0, "room2")
        quantise("wf01")
        square_h(0, 0, placed("z_slots00", [P, PACK, COLS], BF16, AT_SLOTS00), (7, 0, 1, 2))
        for side in range(2):
            cast_wf(1, 0, side)
        load_wm(1, "room0")
        quantise("wf10")
        square_h(0, 1, held("z_slots01", [P, PACK, COLS], BF16), (3, 4, 5, 7))
        grouped["wf11"] = (
            placed("wf11_first", [P, PIECE * PACK], BF16, AT_Z00 + OVERLAP)[:],
            held("wf11_second", [P, PIECE * PACK], BF16)[:],
        )
        cast_wf(1, 1, 0, parts=2)
        z00_rest = z_room("z00_rest", "z00_rest", COLS - GPSIMD_COLUMNS)
        interleave_z(nc.vector.tensor_copy, z00_rest, 0, 0, GPSIMD_COLUMNS, COLS, GPSIMD_COLUMNS)
        cast_wf(1, 1, 1, parts=2)
        quantise("wf11")

        z00 = placed("z00", [P, GPSIMD_COLUMNS * PACK], BF16, AT_Z00)
        interleave_on_gpsimd(z00, 0, 0, 0, GPSIMD_COLUMNS)
        grouped["wm0"] = held("grouped_wm0", [P, N * PACK], BF16)[:]
        for side in range(2):
            cast_and_sign_wm(0, side)
        bias = shared("bias", "room2", [P, N_TILES], F32)
        with nc.allow_non_contiguous_dma(reason="one bias value a partition"):
            nc.sync.dma_start(bias[:], b0.rearrange("(u p) -> p u", p=P))
        quantise_columns("z00", z00_rest[:], GPSIMD_COLUMNS, AT_SLOTS00 + PIECE)
        quantise_wm(0, 0, AT_SLOTS00)
        quantise_columns("z00", z00[:], 0)
        quantise_wm(0, 1, AT_SLOTS00 + PIECE // 2)

        square_h(1, 0, placed("z_slots10", [P, PACK, COLS], BF16, AT_SLOTS10), (0, 1, 2, 3), SCALAR_COLUMNS)
        beside = placed("beside", [P, GPSIMD_COLUMNS * PACK], BF16, AT_BESIDE)
        interleave_on_gpsimd(beside, 0, 1, 0, PIECE)
        interleave_on_gpsimd(beside, 1, 0, SCALAR_COLUMNS, COLS, SCALAR_COLUMNS - PIECE)
        z10 = z_room("z10", "z10", SCALAR_COLUMNS)
        interleave_z(on_scalar, z10, 1, 0, 0, SCALAR_COLUMNS)
        grouped["wm1"] = placed("grouped_wm1", [P, N * PACK], BF16, AT_WM1)[:]
        for side in range(2):
            cast_and_sign_wm(1, side)
        square_h(1, 1, shared("z_slots11", "z_slots11", [P, PACK, COLS], BF16), (0, 1, 2, 3))
        quantise_wm(1, 0)
        quantise_columns("z10", beside[:, PACK * PIECE :], SCALAR_COLUMNS)
        quantise_columns("z10", z10[:], 0)
        quantise_columns("z01", beside[:, 0 : PACK * PIECE], 0, AT_SLOTS10 + PIECE // 2, PIECE)
        quantise_wm(1, 1, AT_SLOTS10)

        z0_fourth = placed("z0_fourth", [P, PIECE * PACK], BF16, AT_QUARTERS)
        interleave_on_gpsimd(z0_fourth, 0, 1, PIECE, COLS, PIECE)
        z1_third = placed("z1_third", [P, PIECE * PACK], BF16, AT_QUARTERS + PIECE)
        interleave_z(on_scalar, z1_third, 1, 1, 0, PIECE)
        z1_fourth = placed("z1_fourth", [P, PIECE * PACK], BF16, AT_QUARTERS + 2 * PIECE)
        interleave_z(on_scalar, z1_fourth, 1, 1, PIECE, COLS, PIECE)
        for u in range(N_TILES - 1):
            finish(u, (4, 5, 7)[u])
        quantise_columns("z11", z1_third[:], 0, AT_LAST_CODES, PIECE)
        finish(N_TILES - 1, 6)
        quantise_columns("z02", z0_fourth[:], 0, None, PIECE)
        third = [sum_pair(1, pair, (2, 3)[pair]) for pair in range(2)]
        combine_pair(1, 0, third[0])
        quantise_columns("z12", z1_fourth[:], 0, AT_LAST_CODES, PIECE)
        combine_pair(1, 1, third[1])
        late = shared("late", "z_slots11", [P, 2, COLS], F32)
        for pair in range(2):
            square_lin_pair(2, pair, late[:, pair, :], pair)
        for pair in range(2):
            combine_pair(2, pair, sum_pair(2, pair, (4, 5)[pair]))
